import numpy as np, ml_dtypes
CORES = [2,3,42,43,82,83,122,123]
N = 8
import mx_ref
BF = ml_dtypes.bfloat16
def gcols(t, e):
    v = np.concatenate([t.reshape(8, 16, -1, 4), np.zeros((8, 16, 1, 4), BF)], axis=2)
    return np.ascontiguousarray(np.stack([v[g][:, e[g]] for g in range(8)])).reshape(128, -1)
def tile(rs):
    return np.stack(rs, axis=2).reshape(128, -1).astype(BF)
def cut(t, i, w=512):
    return t[:, w * i:w * i + w]
def pick(q, e):
    c = np.concatenate([q[0].reshape(128, -1, 4), np.zeros((128, 1, 4), np.uint8)], axis=1); s = np.concatenate([q[1], np.ones((16, 1), np.uint8)], axis=1)
    return (np.ascontiguousarray(c[:, e].reshape(128, -1)), np.ascontiguousarray(s[:, e]))
def join(*qs):
    return (np.concatenate([q[0] for q in qs], axis=1), np.concatenate([q[1] for q in qs], axis=1))
def put(q, e, v):
    c, s = q[0].reshape(128, -1, 4).copy(), q[1].copy(); c[:, e] = v[0].reshape(128, -1, 4); s[:, e] = v[1]
    return (c.reshape(128, -1), s)
def pk(c, s):
    return (np.ascontiguousarray(c), mx_ref.live(s))
def emit(q):
    return q[0], q[1]
def packed(v, rng):
    q = [mx_ref.quantize(np.ascontiguousarray(v[r])) for r in range(N)]
    return np.stack([a for a, b in q]), np.stack([mx_ref.plane(b, rng) for a, b in q])
def values_of_codes():
    e, c = np.zeros((128, 128, 4), np.float32), np.zeros((128, 2, 4), np.uint8)
    e[np.arange(128), np.arange(128), 0] = 1
    c[:127, :, 0] = np.arange(256).reshape(2, 128).T[:127]
    return mx_ref.matmul(mx_ref.quantize(e.reshape(128, 512).astype(BF)), (c.reshape(128, 8), np.full((16, 2), 127, np.uint8))).T.reshape(-1).astype(np.float64)
CODE_VALUE, SCALE_VALUE = values_of_codes(), 2.0 ** (np.arange(256) - 127.0)
def decode(q):
    return (CODE_VALUE[q[0]].reshape(16, 8, -1, 4) * SCALE_VALUE[q[1]][:, None, :, None] + 0.0).reshape(128, -1).astype(np.float32)
def f(rng, *shape):
    return mx_ref.flush((rng.standard_normal(shape, dtype=np.float32) * np.exp2(rng.integers(-2, 3, shape[:-1] + (1,)))).astype(BF))
def wide(rng, *shape, cols=0):
    v = rng.standard_normal(shape, dtype=np.float32) * np.exp2(rng.integers(-12, 13, shape)).astype(np.float32)
    if cols: v *= np.repeat(np.exp2(rng.integers(-cols, cols + 1, shape[:-2] + (1, shape[-1] // 4))) * (rng.random(shape[:-2] + (1, shape[-1] // 4)) > 0.0625), 4, axis=-1).astype(np.float32)
    return mx_ref.flush(v.astype(BF))
C, L, CAP, R = 512, 8, 112, 2
def windows(p):
    s = np.concatenate([p + np.float32(0.0), np.full((8, L - 1), np.inf, np.float32)], axis=1)
    return np.arange(C) + np.argmin(np.stack([s[:, i:i + C] for i in range(L)]), axis=0)
def coarse(v):
    v = np.array(v.astype(np.float32))
    v[np.abs(v) < np.float32(2.0 ** -16)] = 0
    return v.astype(BF)
def numbers_of(rng):
    return {"x": coarse(f(rng, N, 128, 4 * C)), "u": np.array(f(rng, N, 128, 512)), "v": np.array(f(rng, N, 128, 512))}
def sealed(rng, w):
    c, p = packed(np.ascontiguousarray(w).reshape(N, 128, 2048), rng)
    return {"wc": c, "ws": p}
def weights(rng, still=None):
    w = coarse(f(rng, N, 128, 2048)).reshape(N, 128, 4, 128, 4)
    if still is not None: w[:, :, :, np.flatnonzero(still)] = 0
    return sealed(rng, w)
def signs(rng):
    return np.stack([rng.permutation(8) % 2 * 2.0 - 1.0 for r in range(N)])
def plant(rng, s, z=np.ones(N)):
    d = numbers_of(rng)
    x = d["x"].astype(np.float32).reshape(N, 8, 16, C, 4)
    u = d["u"].reshape(N, 128, 128, 4)
    z = z.astype(np.float32).astype(BF)
    x[:, :, 0] = 0
    x[:, :, 0, :, 0] = signs(rng)[:, :, None]
    k = 8 + 2 * R
    x[:, :, k:] = rng.integers(4, 8, (N, 8, 16 - k, C, 4)) * rng.choice([-1.0, 1.0], (N, 8, 16 - k, C, 4)) * 2.0 ** -20
    for t in range(R):
        g = ((s[:, :, t, :, None] >> np.arange(8)) & 1) * np.exp2(np.arange(8) - 23.0)
        x[:, :, 8 + 2 * t] = g[..., :4]
        x[:, :, 9 + 2 * t] = g[..., 4:]
        u[:, :, t::16] = 0
        for h in range(0, 128, 16):
            u[:, h, h + t, 0] = z
            u[:, h + 8 + 2 * t:h + 10 + 2 * t, h + t] = z[:, None, None]
    i = np.arange(128) % 16
    return {"x": x.reshape(N, 128, 4 * C).astype(BF), "u": u.reshape(N, 128, 512), "v": d["v"], **weights(rng, (i == 0) | (i >= 8))}
def setup_inputs(rng):
    return {**numbers_of(rng), **weights(rng)}
def setup_inputs_ties(rng):
    d = numbers_of(rng)
    e = rng.permutation(N)
    x = d["x"].reshape(N, 8, 16, C, 4)
    for r in range(N):
        k = np.zeros(C, int) if r == e[0] else np.full(C, 2) if r == e[1] else rng.permutation(C) % 3
        a = x[r][:, :8, :3].copy()
        a[:, :, 2] = 0
        x[r][:, :8] = a[:, :, k]
    u = d["u"].reshape(N, 8, 16, 128, 4)
    for t in range(R): u[:, :, 8:, t::16] = 0
    return {"x": x.reshape(N, 128, 4 * C), "u": u.reshape(N, 128, 512), "v": d["v"], **weights(rng, np.arange(128) % 16 < 8)}
def setup_inputs_near(rng):
    j = np.arange(C)
    saw = 255 - (j + rng.integers(0, 12, (N, 8, R, 1))) % rng.integers(4, 13, (N, 8, R, 1))
    any8 = rng.integers(8, 16, (N, 8, R, C))
    b = np.stack([np.stack([rng.permutation(8) % 2 for t in range(R)], axis=1) for r in range(N)])
    return plant(rng, np.where(b[..., None] == 1, saw, any8), np.where(rng.permutation(N) < N // 2, 2.0 ** -30, 1.0))
def setup_inputs_slots(rng):
    j = np.arange(C)
    q = np.arange(C + 1)
    n = q + (C - 1 - q) // L + 1
    s = np.zeros((N, 8, R, C), int)
    for r in range(N):
        for t in range(R):
            want = rng.permutation(np.concatenate([[CAP - 1, CAP, CAP + 1, n[0], C], rng.integers(n[0], C + 1, 3)]))
            s[r, :, t] = np.where(j < np.searchsorted(n, want)[:, None], 0, 1 + (C - 1 - j) % L)
    return plant(rng, s)
def setup_inputs_huge(rng):
    d = numbers_of(rng)
    i = np.flatnonzero(np.arange(128) % 16 >= 14)
    x = 2.0 ** 30 * (0.7 + 0.3 * rng.random((N, 128, C, 4)))
    x[:, i] *= 0.25
    c = np.stack([rng.permutation(C) % 2 * 2.0 - 1.0 for r in range(N)])
    c[rng.permutation(N) < N // 2] = 1
    x *= c[:, None, :, None]
    u = d["u"].reshape(N, 128, 8, 16, 4)
    g = np.stack([signs(rng) for t in range(R)], axis=-1)
    a = 2.0 ** 30 * (0.7 + 0.3 * rng.random((N, 128, 8, R, 4))) * g[:, None, :, :, None]
    u[:, :, :, :R] = a.astype(np.float32).astype(BF)
    w = np.zeros((N, 128, 4, 128, 4), np.float32)
    for b in range(4): w[:, i, b, i, b] = 32
    return {"x": x.astype(np.float32).reshape(N, 128, 4 * C).astype(BF), "u": u.reshape(N, 128, 512), "v": d["v"], **sealed(rng, w.astype(BF))}
def setup_inputs_spread(rng):
    d = setup_inputs(rng)
    d["x"] = coarse(wide(rng, N, 128, 4 * C, cols=6))
    return d
def check_inputs(d):
    b = []
    for k in ("x", "u", "v"):
        a = np.abs(d[k].astype(np.float32))
        if not (np.isfinite(a).all() and ((a == 0) | (a >= 2.0 ** -30) & (a <= 2.0 ** 30)).all()): b.append("a value of " + k)
    return b
def reference(x, u, v, wc, ws):
    qu = [mx_ref.quantize(u[r]) for r in range(N)]
    lay = [pk(wc[r], ws[r]) for r in range(N)]
    now = [x[r] for r in range(N)]
    ol = np.zeros((N, 8, 2 * C), np.float32)
    for t in range(R):
        q = [mx_ref.quantize(now[r]) for r in range(N)]
        held = decode(join(*q))
        numbers, far = [], []
        for r in range(N):
            m = windows(mx_ref.matmul(qu[r], q[r])[t::16])
            hit = np.zeros((8, C), bool)
            np.put_along_axis(hit, m, True, axis=1)
            upto = np.add.accumulate(hit, axis=1, dtype=np.int64)
            n = np.take_along_axis(upto, m, axis=1) - 1
            first = np.argsort(~hit, axis=1, kind="stable")[:, :CAP]
            e = np.where(np.arange(CAP) < upto[:, -1:], first, -1)
            p = mx_ref.quantize(gcols(cut(held, r, 4 * C).astype(BF), e))
            w = lay[(r + 1 + t) % N]
            far.append(mx_ref.quantize(tile([mx_ref.matmul(pick(w, np.arange(128 * b, 128 * b + 128)), p) * np.float32(0.03125) for b in range(4)])))
            numbers.append(n)
            ol[r] = np.concatenate([m, n], axis=1)
        came = decode(join(*far)).astype(BF)
        for r in range(N):
            add = gcols(cut(came, r, 4 * CAP), np.where(numbers[r] < CAP, numbers[r], -1))
            now[r] = np.ascontiguousarray((cut(held, r, 4 * C) + add.astype(np.float32)).astype(BF))
    y = np.zeros((N, 128, C), np.float32)
    oc, osc = np.zeros((N, 128, 4 * C), np.uint8), np.zeros((N, 16, C), np.uint8)
    for r in range(N):
        last = mx_ref.quantize(now[r])
        y[r] = mx_ref.matmul(mx_ref.quantize(v[r]), last)
        oc[r], osc[r] = emit(last)
    return {"y": y, "ol": ol, "oc": oc, "osc": osc}

@@ -1,0 +1,408 @@
+from concourse.mybir import dt, AluOpType, AxisListType, ActivationFunctionType
+
+C, CAP, ROUNDS, PAD = 512, 112, 2, 12
+FW = 528
+BIG = 4.0e29
+CODE = "float8_e4m3fn_x4"
+
+
+def _sb(dtype, **widths):
+    return {k: ("sbuf", [128, n], dtype) for k, n in widths.items()}
+
+
+SCRATCH = {
+    "psF": ("psum", [128, 2048], "float32"), "psR": ("psum", [128, 2048], "float32"),
+    **_sb("bfloat16", t0=4 * (C + PAD), t1=4 * (C + PAD), t2=4 * C, ut=512, vt=512, et=2048, fs=4 * FW, pt=512, ht=512,
+          dh=512, tmp=4 * C, keep1=192, f1=192, g1=192),
+    **_sb(CODE, q0=C + PAD, q1=C + PAD, q2=C, uq=128, vq=128, eq=512, woc=512, w0c=512, w1c=512, pq=128, hq=128),
+    **_sb("uint8", s0=C + PAD, s1=C + PAD, s2=C, us=128, vs=128, es=512, wos=512, w0s=512, w1s=512, ps=128, hs=128),
+    **_sb("int32", pi=8),
+    **_sb("uint16", ox=8, ob=4, o1=12, op=2, kap=16, e16=8, n16=32),
+    **_sb("float32", ys=C, pf=8, cf=8, jrow=128, jabs=128, wrow=48, a0=48, cap=48, capf=48, keep=40, r1=192, slot1=192,
+          r2=224, slot2=224, k1=12, st=768, xs=48, m1=48, m2=48, c1=48, c2=48, c3=48, a1=48, a2=48, a3=48, u2=48, u3=48,
+          chg=40, lb=48, mf=64, bt=64, wt=64, ub=40, vw=32, dd=224, dt2=224, em=8, va=32, na=32),
+}
+POOL = {"V": 30, "S": 20, "P": 20, "G": 12, "D": 40}
+SEMAPHORES = [k + str(i) for k in POOL for i in range(POOL[k])] + ["w0in", "w1in", "sent"]
+
+CUT = [[0, 384, 512], [0, 256, 384, 512]]
+DIRECT = [[640, 32], [384, 192, 128]]
+
+
+def plan(cuts, direct):
+    sc, ve, held = [], [], []
+    for k in range(len(cuts) - 1):
+        c0, c1, d = cuts[k], cuts[k + 1], direct[k]
+        own, far = [], []
+        for b in (0, 2, 3, 1):
+            j = min(d, c1 - c0)
+            d -= j
+            if j:
+                own.append(("d", b, c0, c0 + j))
+            if c0 + j < c1:
+                far.insert(0, (b, c0 + j, c1))
+        sc += [("g",) + x for x in far]
+        ve += own[:1] + held + own[1:] + [("a",) + x for x in far]
+        held = [("q", k)]
+    return sc, ve + held
+
+
+def emit(ops, queues, T):
+    writer, readers, known, done = {}, {}, {}, []
+    members = {}
+    for i, o in enumerate(ops):
+        if o["grp"]:
+            members.setdefault(o["grp"], []).append(i)
+    signal = set()
+    for i, o in enumerate(ops):
+        q = o["q"]
+        deps = set()
+        for k in o["r"]:
+            deps.add(writer[k])
+            if k.startswith("ps"):
+                deps.update(j for j in readers.get(k, []) if ops[j]["q"] != q)
+        for k in o["w"]:
+            if k in writer:
+                deps.add(writer[k])
+            deps.update(readers.get(k, []))
+        deps.discard(i)
+        have = known.setdefault(q, set())
+        waits = []
+        for j in sorted(deps, reverse=True):
+            if j in have:
+                continue
+            who = members[ops[j]["grp"]] if ops[j]["grp"] else [j]
+            assert max(who) < i
+            waits.append(who[0])
+            for m in who:
+                have |= done[m]
+                signal.add(m)
+        o["waits"] = waits
+        o["have"] = set(have)
+        done.append(set(have) | {i})
+        for k in o["r"]:
+            readers.setdefault(k, []).append(i)
+        for k in o["w"]:
+            writer[k] = i
+            readers[k] = []
+    last, count, ticket = {}, {}, {}
+    for i, o in enumerate(ops):
+        if o["q"] is None:
+            ticket[i] = o["sem"]
+            continue
+        eng = queues[o["q"]]
+        for j in o["waits"]:
+            eng.wait_ge(T.sem[ticket[j][0]], ticket[j][1])
+        if o["fn"] is None:
+            continue
+        ins = o["fn"]()
+        if i not in signal:
+            continue
+        step = 16 if o["dma"] else 1
+        pool = "D" if o["dma"] else o["q"]
+        who = members[o["grp"]] if o["grp"] else [i]
+        if who[0] == i:
+            name = None
+            for n in range(POOL[pool]):
+                s = pool + str(n)
+                if s not in last or (not o["dma"] and all(m in o["have"] for m in last[s])):
+                    name = s
+                    break
+            last[name] = who
+            count[name] = count.get(name, 0) + step * len(who)
+            ticket[i] = (name, count[name])
+        ins.then_inc(T.sem[ticket[who[0]][0]], step)
+
+
+def rank_program(g, core, T, topo):
+    rank = T.rank_of(core)
+    if rank is None:
+        return
+    cores = T.cores
+    n_ranks = len(cores)
+    A, F = AluOpType, ActivationFunctionType
+    v, s, pe = g.vector, g.scalar, g.tensor
+    queues = {"V": v, "S": s, "P": pe, "G": g, "Y": g.sync}
+    ops = []
+
+    def op(q, fn, r=(), w=(), grp=None, dma=False, sem=None):
+        ops.append({"q": q, "fn": fn, "r": list(r), "w": list(w), "grp": grp, "dma": dma, "sem": sem})
+
+    def dma(q, out, in_, r, w, grp=None):
+        op(q, lambda: queues[q].dma_start(out, in_), r, w, grp, True)
+
+    def tt(out, a, b, alu, r, w, grp=None):
+        op("V", lambda: v.tensor_tensor(out, a, b, alu), r, w, grp)
+
+    def ts(out, a, s1, o0, r, w, s2=None, o1=None, grp=None):
+        if o1 is None:
+            op("V", lambda: v.tensor_scalar(out, a, s1, None, o0), r, w, grp)
+        else:
+            op("V", lambda: v.tensor_scalar(out, a, s1, s2, o0, o1), r, w, grp)
+
+    def cp(out, a, r, w, grp=None):
+        op("V", lambda: v.tensor_copy(out, a), r, w, grp)
+
+    def fill(ap, c, w, grp=None, r=()):
+        op("V", lambda: v.memset(ap, c), r, w, grp)
+
+    def scan(out, d0, d1, o0, o1, r, w, grp=None):
+        op("V", lambda: v.tensor_tensor_scan(out, d0, d1, 0.0, o0, o1), r, w, grp)
+
+    def turn(out, a, r, w, grp=None):
+        op("V", lambda: v.transpose(out, a), r, w, grp)
+
+    def act(out, a, r, w, func=None, bias=0.0, scale=1.0, grp=None):
+        op("S", lambda: s.activation(out, a, F.Copy if func is None else func, bias=bias, scale=scale), r, w, grp)
+
+    def quant(qc, qs, tile, r, w):
+        op("V", lambda: v.quantize_mx(qc, qs, tile), r, w)
+
+    def mm(out, wc, ws, xc, xs, r, w, grp=None):
+        op("P", lambda: pe.matmul_mx(out, wc, ws, xc, xs, True, True), r, w, grp)
+
+    def iota(out, pattern, base, mult, w, flt=True, grp=None):
+        if flt:
+            op("G", lambda: g.iota(out, pattern, base, mult, allow_small_or_imprecise_dtypes=True), (), w, grp)
+        else:
+            op("G", lambda: g.iota(out, pattern, base, mult), (), w, grp)
+
+    sent = [0]
+
+    def send(out, in_, dst, mask, sem, r):
+        rid, pid, _ = topo.addr(dst)
+        sent[0] += bin(mask).count("1")
+        op("G", lambda: g.remote_dma(out, in_, T.sem[sem], T.sem.sent, pid, rid, mask), r, ())
+
+    def codes(buf, a, b):
+        return buf[:, a:b].bitcast(dt.uint8)
+
+    def narrow(a):
+        m = -1
+        for c in cores:
+            if c != a:
+                m &= topo.mask(a, c)
+        return m
+
+    def handed_on(r):
+        return topo.chip(cores[r]) == topo.chip(cores[(r - 1) % n_ranks])
+
+    def wide(a, b):
+        return (topo.mask(a, b) & ~narrow(a)) or narrow(a)
+
+    d0, d1 = cores[(rank - 1) % n_ranks], cores[(rank - 2) % n_ranks]
+    nxt = (rank + 1) % n_ranks
+    in0 = 2 * bin(narrow(cores[nxt])).count("1")
+    if handed_on(nxt):
+        in1 = 2 * bin(wide(cores[nxt], core)).count("1")
+    else:
+        in1 = 2 * bin(narrow(cores[(rank + 2) % n_ranks])).count("1")
+    op(None, None, (), ["w0"], sem=("w0in", in0))
+    op(None, None, (), ["w1"], sem=("w1in", in1))
+
+    dma("Y", T.t0[:, 0:1024], T.x[:, 0:1024], (), ["t0a"])
+    dma("S", T.t0[:, 1024:2048], T.x[:, 1024:2048], (), ["t0b"])
+    dma("Y", T.ut[:], T.u[:], (), ["ut"])
+    dma("S", T.wos[:], T.ws[:], (), ["wos"])
+    dma("Y", codes(T.woc, 0, 512), T.wc[:], (), ["woc"])
+
+    iota(T.pi[:, 0:1], [[0, 1]], 0, 1, ["pi0"], False)
+    iota(T.wrow[:], [[0, 2], [1, 24]], 0, 0, ["wrow"])
+    iota(T.jrow[:], [[1, 128]], 0, -1, ["jrow"])
+    iota(T.r1[:, 0:32], [[16, 2], [0, 16]], 0, 0, ["r1a"], grp="r1")
+    iota(T.r1[:, 32:192], [[16, 5], [0, 32]], 32, 0, ["r1b"], grp="r1")
+    iota(T.r2[:], [[16, 7], [1000, 2], [1, 16]], 0, 0, ["r2"])
+    fill(T.et[:], 0.0, ["et0", "et1", "et2", "et3"])
+    act(T.jabs[:], T.jrow[:], ["jrow"], ["jabs"], F.Abs)
+    for b in range(4):
+        act(T.et[:, 512 * b + b:512 * b + 512:4], T.jabs[:], ["jabs"], ["et%d" % b], F.Relu, 1.0, -1.0, grp="et")
+    ts(T.pi[:, 1:2], T.pi[:, 0:1], 15, A.bitwise_and, ["pi0"], ["pi1"], grp="pi")
+    ts(T.pi[:, 2:3], T.pi[:, 0:1], 31, A.bitwise_and, ["pi0"], ["pi2"], grp="pi")
+    ts(T.pi[:, 3:4], T.pi[:, 0:1], 16, A.bitwise_and, ["pi0"], ["pi3"], grp="pi")
+    ts(T.pi[:, 4:5], T.pi[:, 0:1], 14, A.bitwise_and, ["pi0"], ["pi4"], grp="pi")
+    fill(T.t0[:, 4 * C:], 0.0, ["t0p"], "z")
+    fill(T.keep1[:], 1.0, ["keep1"], "z")
+    fill(T.k1[:], 1.0, ["k1"], "z")
+    cp(T.pf[:, 1:5], T.pi[:, 1:5], ["pi1", "pi2", "pi3", "pi4"], ["pf"])
+    fill(T.lb[:, 0:1], 0.0, ["lb0"], "y")
+    fill(T.ub[:, 0:1], 0.0, ["ub0"], "y")
+    fill(T.ub[:, 32:33], 1000.0, ["ub32"], "y")
+    fill(T.mf[:, 32:64], 0.0, ["mfp"], "y")
+    fill(T.k1[:, 3:12:2], 17.0, ["k1"], "y")
+    qc = T.pf[:, 1:2]
+    ts(T.pf[:, 6:7], T.pf[:, 2:3], 16.0, A.mult, ["pf"], ["i16"], grp="c")
+    ts(T.pf[:, 5:6], qc, 64.0, A.mult, ["pf"], ["q64"], grp="c")
+    steps = [(12.0, -736.0, 0.0), (8.0, -784.0, 288.0), (4.0, -736.0, 528.0)]
+    for k in range(3):
+        ts(T.cf[:, k:k + 1], qc, steps[k][0], A.is_ge, ["pf"], ["cf%d" % k], steps[k][1], A.mult, grp="c")
+    ts(T.pf[:, 7:8], T.pf[:, 3:4], -62.5, A.mult, ["pf"], ["par"], grp="c")
+    ts(T.cf[:, 3:4], T.pf[:, 4:5], 16.0, A.mult, ["pf"], ["cf3"], -1.0, A.add, grp="c")
+    ts(T.ob[:, 0:1], qc, 0.0, A.add, ["pf"], ["ob0"], grp="d")
+    ts(T.ob[:, 1:2], qc, 24.0, A.add, ["pf"], ["ob1"], grp="d")
+    ts(T.a0[:], T.wrow[:], T.pf[:, 6:7], A.add, ["i16", "wrow"], ["a0"])
+
+    def score_list(t):
+        for k in range(3):
+            ts(T.ox[:, 4 * t + k:4 * t + k + 1], T.cf[:, k:k + 1], T.pf[:, 5:6], A.add, ["cf%d" % k, "q64"],
+               ["ox%d%d" % (t, k)], steps[k][2] + t, A.add, grp="ox%d" % t)
+
+    score_list(0)
+    ts(T.capf[:], T.a0[:], float(C), A.is_ge, ["a0"], ["capf"], 2 * BIG, A.mult)
+    ts(T.o1[:], T.k1[:], qc, A.add, ["pf", "k1"], ["o1"], grp="d")
+    ts(T.op[:, 0:1], T.cf[:, 3:4], 15.0, A.max, ["cf3"], ["op"], 191.0, A.min, grp="d")
+    ts(T.cap[:], T.capf[:], -BIG, A.add, ["capf"], ["cap"], grp="d")
+    act(T.slot1[:], T.r1[:], ["r1a", "r1b", "pf"], ["slot1"], F.Identity, qc)
+    act(T.slot2[:], T.r2[:], ["r2", "par"], ["slot2"], F.Identity, T.pf[:, 7:8])
+
+    send(T.w0s[:], T.wos[:], d0, narrow(core), "w0in", ["wos"])
+    send(codes(T.w0c, 0, 512), codes(T.woc, 0, 512), d0, narrow(core), "w0in", ["woc"])
+    if not handed_on((rank - 1) % n_ranks):
+        send(codes(T.w1c, 0, 512), codes(T.woc, 0, 512), d1, narrow(core), "w1in", ["woc", "w0"])
+        send(T.w1s[:], T.wos[:], d1, narrow(core), "w1in", ["wos", "w0"])
+    if handed_on(rank):
+        send(codes(T.w1c, 0, 512), codes(T.w0c, 0, 512), d0, wide(core, d0), "w1in", ["w0"])
+        send(T.w1s[:], T.w0s[:], d0, wide(core, d0), "w1in", ["w0"])
+
+    quant(T.q0[:, 0:256], T.s0[:, 0:256], T.t0[:, 0:1024], ["t0a"], ["q00"])
+    quant(T.q0[:, 256:C + PAD], T.s0[:, 256:C + PAD], T.t0[:, 1024:], ["t0b", "t0p"], ["q01"])
+    quant(T.uq[:], T.us[:], T.ut[:], ["ut"], ["uq"])
+    quant(T.eq[:], T.es[:], T.et[:], ["et0", "et1", "et2", "et3"], ["eq"])
+    fill(T.keep1[:, 0:17:16], 0.0, ["keep1"], "x")
+    fill(T.keep1[:, 32:192:32], 0.0, ["keep1x"], "x", ["t0p"])
+    fill(T.ob[:, 2:3], 16, ["ob2"], "x")
+    fill(T.ob[:, 3:4], 40, ["ob3"], "x")
+
+    tiles = [(T.t0, T.q0, T.s0), (T.t1, T.q1, T.s1), (T.t2, T.q2, T.s2)]
+    layer = [(T.w0c, T.w0s), (T.w1c, T.w1s)]
+    qk = ["q00", "q01"]
+    stores = []
+    for t in range(ROUNDS):
+        _, qt, sc = tiles[t]
+        tn, qn, sn = tiles[t + 1]
+        last = t == ROUNDS - 1
+        mm(T.psR[:, 0:512], T.uq[:], T.us[:], qt[:, 0:C], sc[:, 0:C], ["uq"] + qk, ["psR0"], "s%d" % t)
+        mm(T.psR[:, 512:1024], T.uq[:], T.us[:], qt[:, PAD:C + PAD], sc[:, PAD:C + PAD], ["uq"] + qk, ["psR1"], "s%d" % t)
+        for b in range(4):
+            mm(T.psF[:, 512 * b:512 * b + 512], T.eq[:, 128 * b:128 * b + 128], T.es[:, 128 * b:128 * b + 128],
+               qt[:, 0:C], sc[:, 0:C], ["eq"] + qk, ["psF%d" % b])
+        for b in range(4):
+            act(T.fs[:, FW * b:FW * b + C], T.psF[:, 512 * b:512 * b + 512], ["psF%d" % b], ["fs%d" % b])
+        for b in range(PAD):
+            turn(T.st[:, 64 * b:64 * b + 64], T.psR[:, b:1024:16], ["psR0", "psR1"], ["st%d" % b], "tr%d" % t)
+        if t == 0:
+            ts(T.keep[:], T.wrow[:, 0:40], 23.0, A.not_equal, ["wrow"], ["keep"])
+        tt(T.xs[:], T.st[:].indirect(T.ox[:, 4 * t:4 * t + 3]), T.cap[:], A.max,
+           ["st%d" % b for b in range(PAD)] + ["cap"] + ["ox%d%d" % (t, k) for k in range(3)], ["xs"])
+        if t == 0:
+            dma("Y", T.vt[:], T.v[:], ["xs"], ["vt"])
+            fill(T.pt[:, 4 * CAP:], 0.0, ["ptp"])
+        tt(T.c1[:, 0:47], T.xs[:, 1:48], T.xs[:, 0:47], A.is_lt, ["xs"], ["c1"])
+        tt(T.m1[:, 0:47], T.xs[:, 0:47], T.xs[:, 1:48], A.min, ["xs"], ["m1"])
+        tt(T.a1[:, 0:47], T.c1[:, 0:47], T.a0[:, 0:47], A.add, ["c1", "a0"], ["a1"])
+        tt(T.c2[:, 0:45], T.m1[:, 2:47], T.m1[:, 0:45], A.is_lt, ["m1"], ["c2"])
+        tt(T.m2[:, 0:45], T.m1[:, 0:45], T.m1[:, 2:47], A.min, ["m1"], ["m2"])
+        tt(T.u2[:, 0:45], T.c2[:, 0:45], T.a1[:, 2:47], A.mult, ["c2", "a1"], ["u2"])
+        tt(T.c3[:, 0:41], T.m2[:, 4:45], T.m2[:, 0:41], A.is_lt, ["m2"], ["c3"])
+        tt(T.a2[:, 0:45], T.u2[:, 0:45], T.a1[:, 0:45], A.max, ["u2", "a1"], ["a2"])
+        if t == 0:
+            fill(T.t1[:, 4 * C:], 0.0, ["t1p"])
+        tt(T.u3[:, 0:41], T.c3[:, 0:41], T.a2[:, 4:45], A.mult, ["c3", "a2"], ["u3"])
+        if t == 0:
+            fill(T.fs[:, C:4 * FW:FW], 0.0, ["fsp"])
+        tt(T.a3[:, 0:41], T.u3[:, 0:41], T.a2[:, 0:41], A.max, ["u3", "a2"], ["a3"])
+        tt(T.chg[:], T.a3[:, 1:41], T.a3[:, 0:40], A.not_equal, ["a3"], ["chg"])
+        ts(T.mf[:, 0:32], T.a3[:, 0:41].indirect(T.ob[:, 0:2]), 1.0 / 1024, A.mult, ["a3", "ob0", "ob1"], ["mf"])
+        scan(T.lb[:, 1:41], T.chg[:], T.keep[:], A.add, A.mult, ["chg", "keep"], ["lb"])
+        tt(T.bt[:], T.lb[:, 0:41].indirect(T.ob[:]), T.mf[:], A.add, ["lb", "lb0", "mf", "mfp", "ob2", "ob3"], ["bt"])
+        turn(T.wt[:], T.bt[:], ["bt"], ["wt"])
+        scan(T.ub[:, 1:32], T.mf[:, 32:63], T.wt[:, 32:63], A.add, A.add, ["wt", "mfp"], ["ub"])
+        tt(T.f1[:], T.ub[:, 0:33].indirect(T.o1[:]), T.slot1[:], A.is_le, ["ub", "ub0", "ub32", "o1", "slot1"], ["f1"])
+        tt(T.vw[:], T.wt[:, 0:32], T.ub[:, 0:32], A.add, ["wt", "ub", "ub0"], ["vw"])
+        scan(T.g1[:], T.keep1[:], T.f1[:], A.mult, A.add, ["f1", "keep1", "keep1x"], ["g1"])
+        ts(T.n16[:], T.vw[:], float(CAP), A.min, ["vw"], ["n16"])
+        cp(T.kap[:], T.g1[:].indirect(T.op[:, 0:1]), ["g1", "op"], ["kap"])
+        if last:
+            turn(T.va[:], T.vw[:], ["vw"], ["va"])
+        tt(T.dd[:], T.vw[:].indirect(T.kap[:, 0:14]), T.slot2[:], A.subtract, ["vw", "kap", "slot2"], ["dd"])
+        if last:
+            tt(T.na[:], T.va[:], T.mf[:, 0:32], A.subtract, ["va", "mf"], ["na"])
+            for h in range(2):
+                dma("Y", T.ol[h:8:2, 0:C], T.a3[:, 24 * h:24 * h + 16], ["a3"], ["olm%d" % h], "ol")
+                dma("Y", T.ol[h:8:2, C:2 * C], T.na[:, 16 * h:16 * h + 16], ["na"], ["oln%d" % h], "ol")
+            stores += ["olm0", "olm1", "oln0", "oln1"]
+        turn(T.dt2[:], T.dd[:], ["dd"], ["dt2"])
+        for c in range(7):
+            op("V", lambda c=c: v.tensor_reduce(T.em[:, c:c + 1], T.dt2[:, 32 * c:32 * c + 32], AxisListType.X, A.min,
+                                                apply_absolute_value=True), ["dt2"], ["em%d" % c], "em%d" % t)
+        ts(T.e16[:, 0:7], T.em[:, 0:7], 1024.0, A.mult, ["em%d" % c for c in range(7)], ["e16"], float(C), A.min)
+        for b in range(4):
+            win = T.fs[:, FW * b:FW * b + C + 1].indirect(T.e16[:, 0:7])
+            rd = ["fs%d" % b, "fsp", "e16"]
+            if b < 2:
+                cp(T.pt[:, b:4 * CAP:4], win, rd, ["pt%d" % b], "pv%d" % t)
+            else:
+                act(T.pt[:, b:4 * CAP:4], win, rd, ["pt%d" % b], grp="ps%d" % t)
+        quant(T.pq[:], T.ps[:], T.pt[:], ["pt0", "pt1", "pt2", "pt3", "ptp"], ["pq"])
+        if not last:
+            score_list(t + 1)
+        wq, wsc = layer[t]
+        for b in range(4):
+            mm(T.psR[:, 512 * b:512 * b + 128], wq[:, 128 * b:128 * b + 128], wsc[:, 128 * b:128 * b + 128],
+               T.pq[:], T.ps[:], ["w%d" % t, "pq"], ["psR%d" % b])
+        for b in range(4):
+            src = T.psR[:, 512 * b:512 * b + 128]
+            if b % 2:
+                ts(T.ht[:, b:512:4], src, 0.03125, A.mult, ["psR%d" % b], ["ht%d" % b], grp="hv%d" % t)
+            else:
+                act(T.ht[:, b:512:4], src, ["psR%d" % b], ["ht%d" % b], None, 0.0, 0.03125, grp="hs%d" % t)
+        quant(T.hq[:], T.hs[:], T.ht[:], ["ht0", "ht1", "ht2", "ht3"], ["hq"])
+        if not last:
+            quant(T.vq[:], T.vs[:], T.vt[:], ["vt"], ["vq"])
+        for b in (1, 0, 2, 3):
+            mm(T.psR[:, 512 * b:512 * b + 128], T.eq[:, 128 * b:128 * b + 128], T.es[:, 128 * b:128 * b + 128],
+               T.hq[:], T.hs[:], ["eq", "hq"], ["psR%d" % b])
+        wd = CAP + 2
+        for b in (1, 0, 2, 3):
+            (act if b == 1 else cp)(T.dh[:, 128 * b:128 * b + wd], T.psR[:, 512 * b:512 * b + wd], ["psR%d" % b], ["dh%d" % b])
+        s_plan, v_plan = plan(CUT[t], DIRECT[t])
+        for _, b, c0, c1 in s_plan:
+            act(T.tmp[:, C * b + c0:C * b + c1], T.dh[:, 128 * b:128 * b + wd].indirect(T.n16[:, c0 // 16:c1 // 16]),
+                ["dh%d" % b, "n16"], ["tmp%d_%d" % (b, c0)])
+        qk = []
+        for p in v_plan:
+            if p[0] == "q":
+                k = p[1]
+                c0, c1 = CUT[t][k], CUT[t][k + 1]
+                rd = ["t%d_%d_%d" % (t + 1, x[1], x[2]) for x in v_plan if x[0] != "q" and c0 <= x[2] < c1]
+                key = "q%d%d" % (t + 1, k)
+                qk.append(key)
+                if c1 == C and not last:
+                    c1 += PAD
+                    rd.append("t1p")
+                quant(qn[:, c0:c1], sn[:, c0:c1], tn[:, 4 * c0:4 * c1], rd, [key])
+                if last:
+                    bank = T.psR[:, 512 * k:512 * k + c1 - c0]
+                    mm(bank, T.vq[:], T.vs[:], qn[:, c0:c1], sn[:, c0:c1], ["vq", key], ["psR%d" % k])
+                    dma("Y", T.oc[:, 4 * c0:4 * c1], codes(qn, c0, c1), [key], ["oc%d" % k])
+                    if c1 == C:
+                        for r in range(4):
+                            dma("S" if r % 2 else "Y", T.osc[4 * r:4 * r + 4, :], sn[32 * r:32 * r + 4, :], qk, ["osc%d" % r])
+                            stores.append("osc%d" % r)
+                    (cp if c1 == C else act)(T.ys[:, c0:c1], bank, ["psR%d" % k], ["ys%d" % k])
+                    dma("S" if c1 == C else "Y", T.y[:, c0:c1], T.ys[:, c0:c1], ["ys%d" % k], ["y%d" % k])
+                    stores += ["oc%d" % k, "y%d" % k]
+            else:
+                e, b, c0, c1 = p
+                out = tn[:, 4 * c0 + b:4 * c1:4]
+                key = ["t%d_%d_%d" % (t + 1, b, c0)]
+                grp = "n%d%d" % (t, sum(c0 >= x for x in CUT[t]))
+                if e == "d":
+                    tt(out, T.dh[:, 128 * b:128 * b + wd].indirect(T.n16[:, c0 // 16:c1 // 16]),
+                       T.fs[:, FW * b + c0:FW * b + c1], A.add, ["dh%d" % b, "n16", "fs%d" % b], key, grp)
+                else:
+                    tt(out, T.tmp[:, C * b + c0:C * b + c1], T.psF[:, 512 * b + c0:512 * b + c1], A.add,
+                       ["tmp%d_%d" % (b, c0), "psF%d" % b], key, grp)
+
+    op(None, None, (), ["sent"], sem=("sent", sent[0]))
+    op("G", None, ["sent"] + stores)
+    emit(ops, queues, T)

@@ -17,19 +17,19 @@ SCRATCH = {
     **_sb(CODE, q0=C + PAD, q1=C + PAD, q2=C, uq=128, vq=128, eq=512, woc=512, w0c=512, w1c=512, pq=128, hq=128),
     **_sb("uint8", s0=C + PAD, s1=C + PAD, s2=C, us=128, vs=128, es=512, wos=512, w0s=512, w1s=512, ps=128, hs=128),
     **_sb("int32", pi=8),
-    **_sb("uint16", ox=8, ob=4, o1=12, op=2, kap=16, e16=8, n16=32),
+    **_sb("uint16", ox=8, ob=4, om=2, o1=12, op=2, kap=16, e16=8, n16=32),
     **_sb("float32", ys=C, pf=8, cf=8, jrow=128, jabs=128, wrow=48, a0=48, cap=48, capf=48, keep=40, r1=192, slot1=192,
-          r2=224, slot2=224, k1=12, st=768, xs=48, m1=48, m2=48, c1=48, c2=48, c3=48, a1=48, a2=48, a3=48, u2=48, u3=48,
+          r2=224, slot2=224, k1=12, st=768, xs=48, m1=48, m2=48, c1=48, c2=48, z0=164, z1=188, a3=164, ma=32,
           chg=40, lb=48, mf=64, bt=64, wt=64, ub=40, vw=32, dd=224, dt2=224, em=8, va=32, na=32),
 }
-POOL = {"V": 30, "S": 20, "P": 20, "G": 12, "D": 40}
+POOL = {"V": 40, "S": 20, "P": 20, "G": 12, "D": 40}
 SEMAPHORES = [k + str(i) for k in POOL for i in range(POOL[k])] + ["w0in", "w1in", "sent"]
 
 CUT = [[0, 384, 512], [0, 256, 384, 512]]
-DIRECT = [[640, 32], [384, 192, 128]]
+DIRECT = [[704, 128], [448, 192, 128]]
 
 
-def plan(cuts, direct):
+def plan(cuts, direct, late):
     sc, ve, held = [], [], []
     for k in range(len(cuts) - 1):
         c0, c1, d = cuts[k], cuts[k + 1], direct[k]
@@ -42,7 +42,8 @@ def plan(cuts, direct):
             if c0 + j < c1:
                 far.insert(0, (b, c0 + j, c1))
         sc += [("g",) + x for x in far]
-        ve += own[:1] + held + own[1:] + [("a",) + x for x in far]
+        adds = [("a",) + x for x in far]
+        ve += own + adds + held if late else own[:1] + held + own[1:] + adds
         held = [("q", k)]
     return sc, ve + held
 
@@ -201,9 +202,9 @@ def rank_program(g, core, T, topo):
     op(None, None, (), ["w1"], sem=("w1in", in1))
 
     dma("Y", T.t0[:, 0:1024], T.x[:, 0:1024], (), ["t0a"])
-    dma("S", T.t0[:, 1024:2048], T.x[:, 1024:2048], (), ["t0b"])
+    dma("Y", T.t0[:, 1024:2048], T.x[:, 1024:2048], (), ["t0b"])
     dma("Y", T.ut[:], T.u[:], (), ["ut"])
-    dma("S", T.wos[:], T.ws[:], (), ["wos"])
+    dma("Y", T.wos[:], T.ws[:], (), ["wos"])
     dma("Y", codes(T.woc, 0, 512), T.wc[:], (), ["woc"])
 
     iota(T.pi[:, 0:1], [[0, 1]], 0, 1, ["pi0"], False)
@@ -212,33 +213,24 @@ def rank_program(g, core, T, topo):
     iota(T.r1[:, 0:32], [[16, 2], [0, 16]], 0, 0, ["r1a"], grp="r1")
     iota(T.r1[:, 32:192], [[16, 5], [0, 32]], 32, 0, ["r1b"], grp="r1")
     iota(T.r2[:], [[16, 7], [1000, 2], [1, 16]], 0, 0, ["r2"])
-    fill(T.et[:], 0.0, ["et0", "et1", "et2", "et3"])
-    act(T.jabs[:], T.jrow[:], ["jrow"], ["jabs"], F.Abs)
-    for b in range(4):
-        act(T.et[:, 512 * b + b:512 * b + 512:4], T.jabs[:], ["jabs"], ["et%d" % b], F.Relu, 1.0, -1.0, grp="et")
+    fill(T.et[:, 0:512], 0.0, ["et0"], "e")
     ts(T.pi[:, 1:2], T.pi[:, 0:1], 15, A.bitwise_and, ["pi0"], ["pi1"], grp="pi")
     ts(T.pi[:, 2:3], T.pi[:, 0:1], 31, A.bitwise_and, ["pi0"], ["pi2"], grp="pi")
     ts(T.pi[:, 3:4], T.pi[:, 0:1], 16, A.bitwise_and, ["pi0"], ["pi3"], grp="pi")
     ts(T.pi[:, 4:5], T.pi[:, 0:1], 14, A.bitwise_and, ["pi0"], ["pi4"], grp="pi")
-    fill(T.t0[:, 4 * C:], 0.0, ["t0p"], "z")
-    fill(T.keep1[:], 1.0, ["keep1"], "z")
-    fill(T.k1[:], 1.0, ["k1"], "z")
+    fill(T.et[:, 512:1024], 0.0, ["et1"], "e")
     cp(T.pf[:, 1:5], T.pi[:, 1:5], ["pi1", "pi2", "pi3", "pi4"], ["pf"])
-    fill(T.lb[:, 0:1], 0.0, ["lb0"], "y")
-    fill(T.ub[:, 0:1], 0.0, ["ub0"], "y")
-    fill(T.ub[:, 32:33], 1000.0, ["ub32"], "y")
-    fill(T.mf[:, 32:64], 0.0, ["mfp"], "y")
-    fill(T.k1[:, 3:12:2], 17.0, ["k1"], "y")
+    fill(T.et[:, 1024:1536], 0.0, ["et2"], "e")
     qc = T.pf[:, 1:2]
     ts(T.pf[:, 6:7], T.pf[:, 2:3], 16.0, A.mult, ["pf"], ["i16"], grp="c")
     ts(T.pf[:, 5:6], qc, 64.0, A.mult, ["pf"], ["q64"], grp="c")
     steps = [(12.0, -736.0, 0.0), (8.0, -784.0, 288.0), (4.0, -736.0, 528.0)]
     for k in range(3):
         ts(T.cf[:, k:k + 1], qc, steps[k][0], A.is_ge, ["pf"], ["cf%d" % k], steps[k][1], A.mult, grp="c")
-    ts(T.pf[:, 7:8], T.pf[:, 3:4], -62.5, A.mult, ["pf"], ["par"], grp="c")
-    ts(T.cf[:, 3:4], T.pf[:, 4:5], 16.0, A.mult, ["pf"], ["cf3"], -1.0, A.add, grp="c")
-    ts(T.ob[:, 0:1], qc, 0.0, A.add, ["pf"], ["ob0"], grp="d")
-    ts(T.ob[:, 1:2], qc, 24.0, A.add, ["pf"], ["ob1"], grp="d")
+    fill(T.et[:, 1536:2048], 0.0, ["et3"], "e")
+    act(T.jabs[:], T.jrow[:], ["jrow"], ["jabs"], F.Abs)
+    for b in range(4):
+        act(T.et[:, 512 * b + b:512 * b + 512:4], T.jabs[:], ["jabs"], ["et%d" % b], F.Relu, 1.0, -1.0, grp="et")
     ts(T.a0[:], T.wrow[:], T.pf[:, 6:7], A.add, ["i16", "wrow"], ["a0"])
 
     def score_list(t):
@@ -248,11 +240,14 @@ def rank_program(g, core, T, topo):
 
     score_list(0)
     ts(T.capf[:], T.a0[:], float(C), A.is_ge, ["a0"], ["capf"], 2 * BIG, A.mult)
-    ts(T.o1[:], T.k1[:], qc, A.add, ["pf", "k1"], ["o1"], grp="d")
-    ts(T.op[:, 0:1], T.cf[:, 3:4], 15.0, A.max, ["cf3"], ["op"], 191.0, A.min, grp="d")
-    ts(T.cap[:], T.capf[:], -BIG, A.add, ["capf"], ["cap"], grp="d")
-    act(T.slot1[:], T.r1[:], ["r1a", "r1b", "pf"], ["slot1"], F.Identity, qc)
-    act(T.slot2[:], T.r2[:], ["r2", "par"], ["slot2"], F.Identity, T.pf[:, 7:8])
+    fill(T.t0[:, 4 * C:], 0.0, ["t0p"], "z")
+    fill(T.z0[:, 0:164:4], 0.0, ["zk0"], "z")
+    fill(T.z0[:, 1:164:2], 1.0, ["zk1"], "z")
+    fill(T.keep1[:], 1.0, ["keep1"], "z")
+    fill(T.k1[:], 1.0, ["k1"], "z")
+    ts(T.cap[:], T.capf[:], -BIG, A.add, ["capf"], ["cap"], grp="z")
+    ts(T.pf[:, 7:8], T.pf[:, 3:4], -62.5, A.mult, ["pf"], ["par"], grp="z")
+    ts(T.cf[:, 3:4], T.pf[:, 4:5], 16.0, A.mult, ["pf"], ["cf3"], -1.0, A.add, grp="z")
 
     send(T.w0s[:], T.wos[:], d0, narrow(core), "w0in", ["wos"])
     send(codes(T.w0c, 0, 512), codes(T.woc, 0, 512), d0, narrow(core), "w0in", ["woc"])
@@ -267,11 +262,33 @@ def rank_program(g, core, T, topo):
     quant(T.q0[:, 256:C + PAD], T.s0[:, 256:C + PAD], T.t0[:, 1024:], ["t0b", "t0p"], ["q01"])
     quant(T.uq[:], T.us[:], T.ut[:], ["ut"], ["uq"])
     quant(T.eq[:], T.es[:], T.et[:], ["et0", "et1", "et2", "et3"], ["eq"])
-    fill(T.keep1[:, 0:17:16], 0.0, ["keep1"], "x")
-    fill(T.keep1[:, 32:192:32], 0.0, ["keep1x"], "x", ["t0p"])
-    fill(T.ob[:, 2:3], 16, ["ob2"], "x")
-    fill(T.ob[:, 3:4], 40, ["ob3"], "x")
+    spare = [
+        lambda: fill(T.k1[:, 3:12:2], 17.0, ["k1"], "y"),
+        lambda: ts(T.om[:, 0:1], qc, 4.0, A.mult, ["pf"], ["om0"], 3.0, A.add, grp="v"),
+        lambda: ts(T.om[:, 1:2], qc, 4.0, A.mult, ["pf"], ["om1"], 99.0, A.add, grp="v"),
+        lambda: fill(T.mf[:, 32:64], 0.0, ["mfp"], "y"),
+        lambda: fill(T.lb[:, 0:1], 0.0, ["lb0"], "y"),
+        lambda: ts(T.keep[:], T.wrow[:, 0:40], 23.0, A.not_equal, ["wrow"], ["keep"], grp="y"),
+        lambda: ts(T.ob[:, 0:1], qc, 0.0, A.add, ["pf"], ["ob0"], grp="y"),
+        lambda: ts(T.ob[:, 1:2], qc, 24.0, A.add, ["pf"], ["ob1"], grp="y"),
+        lambda: fill(T.ob[:, 2:3], 16, ["ob2"], "y"),
+        lambda: fill(T.ob[:, 3:4], 40, ["ob3"], "y"),
+        lambda: fill(T.ub[:, 0:1], 0.0, ["ub0"], "x"),
+        lambda: fill(T.ub[:, 32:33], 1000.0, ["ub32"], "x"),
+        lambda: ts(T.o1[:], T.k1[:], qc, A.add, ["pf", "k1"], ["o1"], grp="x"),
+        lambda: fill(T.keep1[:, 0:17:16], 0.0, ["keep1"], "x"),
+        lambda: fill(T.keep1[:, 32:192:32], 0.0, ["keep1x"], "x", ["t0p"]),
+        lambda: ts(T.op[:, 0:1], T.cf[:, 3:4], 15.0, A.max, ["cf3"], ["op"], 191.0, A.min, grp="u"),
+        lambda: fill(T.fs[:, C:4 * FW:FW], 0.0, ["fsp"], "w"),
+        lambda: fill(T.pt[:, 4 * CAP:], 0.0, ["ptp"], "w"),
+        lambda: fill(T.t1[:, 4 * C:], 0.0, ["t1p"], "w"),
+    ]
 
+    def gap(n=1):
+        for _ in range(min(n, len(spare))):
+            spare.pop(0)()
+
+    gap(3)
     tiles = [(T.t0, T.q0, T.s0), (T.t1, T.q1, T.s1), (T.t2, T.q2, T.s2)]
     layer = [(T.w0c, T.w0s), (T.w1c, T.w1s)]
     qk = ["q00", "q01"]
@@ -289,48 +306,58 @@ def rank_program(g, core, T, topo):
             act(T.fs[:, FW * b:FW * b + C], T.psF[:, 512 * b:512 * b + 512], ["psF%d" % b], ["fs%d" % b])
         for b in range(PAD):
             turn(T.st[:, 64 * b:64 * b + 64], T.psR[:, b:1024:16], ["psR0", "psR1"], ["st%d" % b], "tr%d" % t)
-        if t == 0:
-            ts(T.keep[:], T.wrow[:, 0:40], 23.0, A.not_equal, ["wrow"], ["keep"])
+        gap()
         tt(T.xs[:], T.st[:].indirect(T.ox[:, 4 * t:4 * t + 3]), T.cap[:], A.max,
            ["st%d" % b for b in range(PAD)] + ["cap"] + ["ox%d%d" % (t, k) for k in range(3)], ["xs"])
+        gap()
         if t == 0:
             dma("Y", T.vt[:], T.v[:], ["xs"], ["vt"])
-            fill(T.pt[:, 4 * CAP:], 0.0, ["ptp"])
+            act(T.slot1[:], T.r1[:], ["r1a", "r1b", "pf"], ["slot1"], F.Identity, qc)
+            act(T.slot2[:], T.r2[:], ["r2", "par"], ["slot2"], F.Identity, T.pf[:, 7:8])
         tt(T.c1[:, 0:47], T.xs[:, 1:48], T.xs[:, 0:47], A.is_lt, ["xs"], ["c1"])
         tt(T.m1[:, 0:47], T.xs[:, 0:47], T.xs[:, 1:48], A.min, ["xs"], ["m1"])
-        tt(T.a1[:, 0:47], T.c1[:, 0:47], T.a0[:, 0:47], A.add, ["c1", "a0"], ["a1"])
+        gap()
+        tt(T.z1[:, 2:188:4], T.c1[:, 0:47], T.a0[:, 0:47], A.add, ["c1", "a0"], ["z2"])
         tt(T.c2[:, 0:45], T.m1[:, 2:47], T.m1[:, 0:45], A.is_lt, ["m1"], ["c2"])
         tt(T.m2[:, 0:45], T.m1[:, 0:45], T.m1[:, 2:47], A.min, ["m1"], ["m2"])
-        tt(T.u2[:, 0:45], T.c2[:, 0:45], T.a1[:, 2:47], A.mult, ["c2", "a1"], ["u2"])
-        tt(T.c3[:, 0:41], T.m2[:, 4:45], T.m2[:, 0:41], A.is_lt, ["m2"], ["c3"])
-        tt(T.a2[:, 0:45], T.u2[:, 0:45], T.a1[:, 0:45], A.max, ["u2", "a1"], ["a2"])
-        if t == 0:
-            fill(T.t1[:, 4 * C:], 0.0, ["t1p"])
-        tt(T.u3[:, 0:41], T.c3[:, 0:41], T.a2[:, 4:45], A.mult, ["c3", "a2"], ["u3"])
-        if t == 0:
-            fill(T.fs[:, C:4 * FW:FW], 0.0, ["fsp"])
-        tt(T.a3[:, 0:41], T.u3[:, 0:41], T.a2[:, 0:41], A.max, ["u3", "a2"], ["a3"])
-        tt(T.chg[:], T.a3[:, 1:41], T.a3[:, 0:40], A.not_equal, ["a3"], ["chg"])
-        ts(T.mf[:, 0:32], T.a3[:, 0:41].indirect(T.ob[:, 0:2]), 1.0 / 1024, A.mult, ["a3", "ob0", "ob1"], ["mf"])
+        tt(T.z1[:, 0:164:4], T.c1[:, 4:45], T.a0[:, 4:45], A.add, ["c1", "a0"], ["z0"], "zz%d" % t)
+        tt(T.z1[:, 3:164:4], T.c2[:, 0:41], T.z1[:, 10:172:4], A.mult, ["c2", "z2"], ["z3"], "zz%d" % t)
+        tt(T.z1[:, 1:164:4], T.c2[:, 4:45], T.z1[:, 26:188:4], A.mult, ["c2", "z2"], ["z1"], "zz%d" % t)
+        tt(T.z0[:, 2:164:4], T.m2[:, 4:45], T.m2[:, 0:41], A.is_lt, ["m2"], ["c3"], "zz%d" % t)
+        gap(2)
+        scan(T.a3[:], T.z0[:], T.z1[:, 0:164], A.mult, A.max, ["z0", "z1", "z2", "z3", "c3", "zk0", "zk1"], ["a3"])
+        gap(2)
+        tt(T.chg[:], T.a3[:, 7:164:4], T.a3[:, 3:160:4], A.not_equal, ["a3"], ["chg"])
+        ts(T.mf[:, 0:32], T.a3[:].indirect(T.om[:]), 1.0 / 1024, A.mult, ["a3", "om0", "om1"], ["mf"])
         scan(T.lb[:, 1:41], T.chg[:], T.keep[:], A.add, A.mult, ["chg", "keep"], ["lb"])
-        tt(T.bt[:], T.lb[:, 0:41].indirect(T.ob[:]), T.mf[:], A.add, ["lb", "lb0", "mf", "mfp", "ob2", "ob3"], ["bt"])
+        gap(2)
+        tt(T.bt[:], T.lb[:, 0:41].indirect(T.ob[:]), T.mf[:], A.add,
+           ["lb", "lb0", "mf", "mfp", "ob0", "ob1", "ob2", "ob3"], ["bt"])
+        gap(2)
+        if last:
+            ts(T.ma[:], T.mf[:, 0:32], 1024.0, A.mult, ["mf"], ["ma"])
         turn(T.wt[:], T.bt[:], ["bt"], ["wt"])
+        gap()
         scan(T.ub[:, 1:32], T.mf[:, 32:63], T.wt[:, 32:63], A.add, A.add, ["wt", "mfp"], ["ub"])
+        gap()
         tt(T.f1[:], T.ub[:, 0:33].indirect(T.o1[:]), T.slot1[:], A.is_le, ["ub", "ub0", "ub32", "o1", "slot1"], ["f1"])
         tt(T.vw[:], T.wt[:, 0:32], T.ub[:, 0:32], A.add, ["wt", "ub", "ub0"], ["vw"])
         scan(T.g1[:], T.keep1[:], T.f1[:], A.mult, A.add, ["f1", "keep1", "keep1x"], ["g1"])
         ts(T.n16[:], T.vw[:], float(CAP), A.min, ["vw"], ["n16"])
         cp(T.kap[:], T.g1[:].indirect(T.op[:, 0:1]), ["g1", "op"], ["kap"])
+        gap()
         if last:
             turn(T.va[:], T.vw[:], ["vw"], ["va"])
         tt(T.dd[:], T.vw[:].indirect(T.kap[:, 0:14]), T.slot2[:], A.subtract, ["vw", "kap", "slot2"], ["dd"])
+        gap()
         if last:
             tt(T.na[:], T.va[:], T.mf[:, 0:32], A.subtract, ["va", "mf"], ["na"])
             for h in range(2):
-                dma("Y", T.ol[h:8:2, 0:C], T.a3[:, 24 * h:24 * h + 16], ["a3"], ["olm%d" % h], "ol")
+                dma("Y", T.ol[h:8:2, 0:C], T.ma[:, 16 * h:16 * h + 16], ["ma"], ["olm%d" % h], "ol")
                 dma("Y", T.ol[h:8:2, C:2 * C], T.na[:, 16 * h:16 * h + 16], ["na"], ["oln%d" % h], "ol")
             stores += ["olm0", "olm1", "oln0", "oln1"]
         turn(T.dt2[:], T.dd[:], ["dd"], ["dt2"])
+        gap()
         for c in range(7):
             op("V", lambda c=c: v.tensor_reduce(T.em[:, c:c + 1], T.dt2[:, 32 * c:32 * c + 32], AxisListType.X, A.min,
                                                 apply_absolute_value=True), ["dt2"], ["em%d" % c], "em%d" % t)
@@ -358,13 +385,13 @@ def rank_program(g, core, T, topo):
         quant(T.hq[:], T.hs[:], T.ht[:], ["ht0", "ht1", "ht2", "ht3"], ["hq"])
         if not last:
             quant(T.vq[:], T.vs[:], T.vt[:], ["vt"], ["vq"])
-        for b in (1, 0, 2, 3):
+        for b in (1, 0, 3, 2):
             mm(T.psR[:, 512 * b:512 * b + 128], T.eq[:, 128 * b:128 * b + 128], T.es[:, 128 * b:128 * b + 128],
                T.hq[:], T.hs[:], ["eq", "hq"], ["psR%d" % b])
         wd = CAP + 2
-        for b in (1, 0, 2, 3):
-            (act if b == 1 else cp)(T.dh[:, 128 * b:128 * b + wd], T.psR[:, 512 * b:512 * b + wd], ["psR%d" % b], ["dh%d" % b])
-        s_plan, v_plan = plan(CUT[t], DIRECT[t])
+        for b in (1, 0, 3, 2):
+            (act if b % 2 else cp)(T.dh[:, 128 * b:128 * b + wd], T.psR[:, 512 * b:512 * b + wd], ["psR%d" % b], ["dh%d" % b])
+        s_plan, v_plan = plan(CUT[t], DIRECT[t], not last)
         for _, b, c0, c1 in s_plan:
             act(T.tmp[:, C * b + c0:C * b + c1], T.dh[:, 128 * b:128 * b + wd].indirect(T.n16[:, c0 // 16:c1 // 16]),
                 ["dh%d" % b, "n16"], ["tmp%d_%d" % (b, c0)])

@@ -17,35 +17,24 @@ SCRATCH = {
     **_sb(CODE, q0=C + PAD, q1=C + PAD, q2=C, uq=128, vq=128, eq=512, woc=512, w0c=512, w1c=512, pq=128, hq=128),
     **_sb("uint8", s0=C + PAD, s1=C + PAD, s2=C, us=128, vs=128, es=512, wos=512, w0s=512, w1s=512, ps=128, hs=128),
     **_sb("int32", pi=8),
-    **_sb("uint16", ox=8, ob=4, om=2, o1=12, op=2, kap=16, e16=8, n16=32),
-    **_sb("float32", ys=C, pf=8, cf=8, jrow=128, jabs=128, wrow=48, a0=48, cap=48, capf=48, keep=40, r1=192, slot1=192,
+    **_sb("uint16", ox=8, om=2, o1=12, op=4, kap=32, e16=8, n16=32),
+    **_sb("float32", ys=C, pf=8, cf=8, jrow=128, jabs=128, wrow=48, a0=48, cap=48, capf=48, keep=96, r1=192, slot1=192,
           r2=224, slot2=224, k1=12, st=768, xs=48, m1=48, m2=48, c1=48, c2=48, z0=164, z1=188, a3=164, ma=32,
-          chg=40, lb=48, mf=64, bt=64, wt=64, ub=40, vw=32, dd=224, dt2=224, em=8, va=32, na=32),
+          chg=96, lb=96, mf=32, mt=32, wt=96, ub=64, vu=32, vw=32, dd=224, dt2=224, em=8, va=32, na=32),
 }
-POOL = {"V": 40, "S": 20, "P": 20, "G": 12, "D": 40}
+POOL = {"V": 48, "S": 24, "P": 20, "G": 12, "D": 40}
 SEMAPHORES = [k + str(i) for k in POOL for i in range(POOL[k])] + ["w0in", "w1in", "sent"]
 
 CUT = [[0, 384, 512], [0, 256, 384, 512]]
-DIRECT = [[704, 128], [448, 192, 128]]
-
-
-def plan(cuts, direct, late):
-    sc, ve, held = [], [], []
-    for k in range(len(cuts) - 1):
-        c0, c1, d = cuts[k], cuts[k + 1], direct[k]
-        own, far = [], []
-        for b in (0, 2, 3, 1):
-            j = min(d, c1 - c0)
-            d -= j
-            if j:
-                own.append(("d", b, c0, c0 + j))
-            if c0 + j < c1:
-                far.insert(0, (b, c0 + j, c1))
-        sc += [("g",) + x for x in far]
-        adds = [("a",) + x for x in far]
-        ve += own + adds + held if late else own[:1] + held + own[1:] + adds
-        held = [("q", k)]
-    return sc, ve + held
+PLAN = [
+    [("g", 1, 0, 384), ("g", 3, 0, 384), ("g", 2, 256, 512), ("g", 1, 384, 512), ("g", 3, 384, 512),
+     ("d", 0, 0, 512), ("d", 2, 0, 256), ("a", 1, 0, 384), ("a", 3, 0, 384), ("a", 2, 256, 512), ("a", 1, 384, 512),
+     ("q", 0), ("a", 3, 384, 512), ("q", 1)],
+    [("g", 1, 0, 256), ("g", 3, 0, 256), ("g", 1, 256, 512), ("g", 3, 256, 384), ("g", 2, 256, 384),
+     ("g", 3, 384, 512), ("g", 2, 384, 512),
+     ("d", 0, 0, 512), ("d", 2, 0, 256), ("a", 1, 0, 256), ("a", 3, 0, 256), ("a", 1, 256, 512), ("q", 0),
+     ("a", 3, 256, 384), ("a", 2, 256, 384), ("a", 3, 384, 512), ("q", 1), ("a", 2, 384, 512), ("q", 2)],
+]
 
 
 def emit(ops, queues, T):
@@ -244,7 +233,7 @@ def rank_program(g, core, T, topo):
     fill(T.z0[:, 0:164:4], 0.0, ["zk0"], "z")
     fill(T.z0[:, 1:164:2], 1.0, ["zk1"], "z")
     fill(T.keep1[:], 1.0, ["keep1"], "z")
-    fill(T.k1[:], 1.0, ["k1"], "z")
+    fill(T.k1[:], 0.0, ["k1"], "z")
     ts(T.cap[:], T.capf[:], -BIG, A.add, ["capf"], ["cap"], grp="z")
     ts(T.pf[:, 7:8], T.pf[:, 3:4], -62.5, A.mult, ["pf"], ["par"], grp="z")
     ts(T.cf[:, 3:4], T.pf[:, 4:5], 16.0, A.mult, ["pf"], ["cf3"], -1.0, A.add, grp="z")
@@ -263,25 +252,23 @@ def rank_program(g, core, T, topo):
     quant(T.uq[:], T.us[:], T.ut[:], ["ut"], ["uq"])
     quant(T.eq[:], T.es[:], T.et[:], ["et0", "et1", "et2", "et3"], ["eq"])
     spare = [
-        lambda: fill(T.k1[:, 3:12:2], 17.0, ["k1"], "y"),
+        lambda: fill(T.keep[:], 1.0, ["keep"]),
         lambda: ts(T.om[:, 0:1], qc, 4.0, A.mult, ["pf"], ["om0"], 3.0, A.add, grp="v"),
         lambda: ts(T.om[:, 1:2], qc, 4.0, A.mult, ["pf"], ["om1"], 99.0, A.add, grp="v"),
-        lambda: fill(T.mf[:, 32:64], 0.0, ["mfp"], "y"),
+        lambda: fill(T.chg[:], 0.0, ["chg0", "chg1"], "y"),
+        lambda: fill(T.keep[:, 47:48], 0.0, ["keep"], "y"),
+        lambda: fill(T.k1[:, 3:12:2], 16.0, ["k1"], "y"),
+        lambda: ts(T.pf[:, 0:1], T.pf[:, 2:3], T.pf[:, 3:4], A.add, ["pf"], ["qh"], grp="y"),
         lambda: fill(T.lb[:, 0:1], 0.0, ["lb0"], "y"),
-        lambda: ts(T.keep[:], T.wrow[:, 0:40], 23.0, A.not_equal, ["wrow"], ["keep"], grp="y"),
-        lambda: ts(T.ob[:, 0:1], qc, 0.0, A.add, ["pf"], ["ob0"], grp="y"),
-        lambda: ts(T.ob[:, 1:2], qc, 24.0, A.add, ["pf"], ["ob1"], grp="y"),
-        lambda: fill(T.ob[:, 2:3], 16, ["ob2"], "y"),
-        lambda: fill(T.ob[:, 3:4], 40, ["ob3"], "y"),
         lambda: fill(T.ub[:, 0:1], 0.0, ["ub0"], "x"),
-        lambda: fill(T.ub[:, 32:33], 1000.0, ["ub32"], "x"),
-        lambda: ts(T.o1[:], T.k1[:], qc, A.add, ["pf", "k1"], ["o1"], grp="x"),
+        lambda: ts(T.o1[:], T.k1[:], T.pf[:, 0:1], A.add, ["qh", "k1"], ["o1"], grp="x"),
         lambda: fill(T.keep1[:, 0:17:16], 0.0, ["keep1"], "x"),
         lambda: fill(T.keep1[:, 32:192:32], 0.0, ["keep1x"], "x", ["t0p"]),
-        lambda: ts(T.op[:, 0:1], T.cf[:, 3:4], 15.0, A.max, ["cf3"], ["op"], 191.0, A.min, grp="u"),
+        lambda: ts(T.op[:, 0:1], T.cf[:, 3:4], 15.0, A.max, ["cf3"], ["op0"], 95.0, A.min, grp="u"),
+        lambda: ts(T.op[:, 2:3], T.cf[:, 3:4], 32.0, A.add, ["cf3"], ["op1"], 95.0, A.min, grp="u"),
         lambda: fill(T.fs[:, C:4 * FW:FW], 0.0, ["fsp"], "w"),
         lambda: fill(T.pt[:, 4 * CAP:], 0.0, ["ptp"], "w"),
-        lambda: fill(T.t1[:, 4 * C:], 0.0, ["t1p"], "w"),
+        lambda: fill(T.t1[:, 4 * C:], 0.0, ["t1p"]),
     ]
 
     def gap(n=1):
@@ -291,6 +278,7 @@ def rank_program(g, core, T, topo):
     gap(3)
     tiles = [(T.t0, T.q0, T.s0), (T.t1, T.q1, T.s1), (T.t2, T.q2, T.s2)]
     layer = [(T.w0c, T.w0s), (T.w1c, T.w1s)]
+    halves = [(0, 4), (4, 7)]
     qk = ["q00", "q01"]
     stores = []
     for t in range(ROUNDS):
@@ -306,10 +294,10 @@ def rank_program(g, core, T, topo):
             act(T.fs[:, FW * b:FW * b + C], T.psF[:, 512 * b:512 * b + 512], ["psF%d" % b], ["fs%d" % b])
         for b in range(PAD):
             turn(T.st[:, 64 * b:64 * b + 64], T.psR[:, b:1024:16], ["psR0", "psR1"], ["st%d" % b], "tr%d" % t)
-        gap()
+        gap(2)
         tt(T.xs[:], T.st[:].indirect(T.ox[:, 4 * t:4 * t + 3]), T.cap[:], A.max,
            ["st%d" % b for b in range(PAD)] + ["cap"] + ["ox%d%d" % (t, k) for k in range(3)], ["xs"])
-        gap()
+        gap(2)
         if t == 0:
             dma("Y", T.vt[:], T.v[:], ["xs"], ["vt"])
             act(T.slot1[:], T.r1[:], ["r1a", "r1b", "pf"], ["slot1"], F.Identity, qc)
@@ -327,49 +315,72 @@ def rank_program(g, core, T, topo):
         gap(2)
         scan(T.a3[:], T.z0[:], T.z1[:, 0:164], A.mult, A.max, ["z0", "z1", "z2", "z3", "c3", "zk0", "zk1"], ["a3"])
         gap(2)
-        tt(T.chg[:], T.a3[:, 7:164:4], T.a3[:, 3:160:4], A.not_equal, ["a3"], ["chg"])
-        ts(T.mf[:, 0:32], T.a3[:].indirect(T.om[:]), 1.0 / 1024, A.mult, ["a3", "om0", "om1"], ["mf"])
-        scan(T.lb[:, 1:41], T.chg[:], T.keep[:], A.add, A.mult, ["chg", "keep"], ["lb"])
-        gap(2)
-        tt(T.bt[:], T.lb[:, 0:41].indirect(T.ob[:]), T.mf[:], A.add,
-           ["lb", "lb0", "mf", "mfp", "ob0", "ob1", "ob2", "ob3"], ["bt"])
-        gap(2)
+        for h in range(2):
+            tt(T.chg[:, 48 * h:48 * h + 16], T.a3[:, 96 * h + 7:96 * h + 68:4], T.a3[:, 96 * h + 3:96 * h + 64:4],
+               A.not_equal, ["a3"], ["chg%d" % h], "ch%d" % t)
+        ts(T.mf[:], T.a3[:].indirect(T.om[:]), 1.0 / 1024, A.mult, ["a3", "om0", "om1"], ["mf"])
+        scan(T.lb[:, 1:96], T.chg[:, 0:95], T.keep[:, 0:95], A.add, A.mult, ["chg0", "chg1", "keep"], ["lb"])
+        turn(T.mt[:], T.mf[:], ["mf"], ["mt"])
         if last:
-            ts(T.ma[:], T.mf[:, 0:32], 1024.0, A.mult, ["mf"], ["ma"])
-        turn(T.wt[:], T.bt[:], ["bt"], ["wt"])
+            ts(T.ma[:], T.mf[:], 1024.0, A.mult, ["mf"], ["ma"])
         gap()
-        scan(T.ub[:, 1:32], T.mf[:, 32:63], T.wt[:, 32:63], A.add, A.add, ["wt", "mfp"], ["ub"])
+        turn(T.wt[:], T.lb[:], ["lb", "lb0"], ["wt"])
+        gap(2)
+        scan(T.ub[:, 1:64], T.wt[:, 32:95], T.keep[:, 16:79], A.add, A.mult, ["wt", "keep"], ["ub"])
+        tt(T.vu[:], T.wt[:, 0:64].indirect(T.o1[:, 2:4]), T.mt[:], A.add, ["wt", "mt", "o1"], ["vu"])
         gap()
-        tt(T.f1[:], T.ub[:, 0:33].indirect(T.o1[:]), T.slot1[:], A.is_le, ["ub", "ub0", "ub32", "o1", "slot1"], ["f1"])
-        tt(T.vw[:], T.wt[:, 0:32], T.ub[:, 0:32], A.add, ["wt", "ub", "ub0"], ["vw"])
-        scan(T.g1[:], T.keep1[:], T.f1[:], A.mult, A.add, ["f1", "keep1", "keep1x"], ["g1"])
-        ts(T.n16[:], T.vw[:], float(CAP), A.min, ["vw"], ["n16"])
-        cp(T.kap[:], T.g1[:].indirect(T.op[:, 0:1]), ["g1", "op"], ["kap"])
+        for i in range(2):
+            tt(T.f1[:, 96 * i:96 * i + 96], T.ub[:].indirect(T.o1[:, 6 * i:6 * i + 6]), T.slot1[:, 96 * i:96 * i + 96],
+               A.is_le, ["ub", "ub0", "o1", "slot1"], ["f1%d" % i])
+        for i in range(2):
+            scan(T.g1[:, 96 * i:96 * i + 96], T.keep1[:, 96 * i:96 * i + 96], T.f1[:, 96 * i:96 * i + 96], A.mult, A.add,
+                 ["f1%d" % i, "keep1", "keep1x"], ["g1%d" % i])
+            if i == 0:
+                tt(T.vw[:], T.ub[:].indirect(T.o1[:, 2:4]), T.vu[:], A.add, ["ub", "ub0", "vu", "o1"], ["vw"])
+        for i in range(2):
+            ts(T.kap[:, 16 * i:16 * i + 16], T.g1[:, 96 * i:96 * i + 96].indirect(T.op[:, 2 * i:2 * i + 1]), -1.0, A.add,
+               ["g1%d" % i, "op%d" % i], ["kap%d" % i])
+            if i == 0:
+                ts(T.n16[:], T.vw[:], float(CAP), A.min, ["vw"], ["n16"])
+        for i, (c0, c1) in enumerate(halves):
+            tt(T.dd[:, 32 * c0:32 * c1], T.vw[:].indirect(T.kap[:, 16 * i:16 * i + 2 * (c1 - c0)]),
+               T.slot2[:, 32 * c0:32 * c1], A.subtract, ["vw", "kap%d" % i, "slot2"], ["dd%d" % i])
+        for i, (c0, c1) in enumerate(halves):
+            turn(T.dt2[:, 32 * c0:32 * c1], T.dd[:, 32 * c0:32 * c1], ["dd%d" % i], ["dt2%d" % i])
+
+        def least(c):
+            op("V", lambda: v.tensor_reduce(T.em[:, c:c + 1], T.dt2[:, 32 * c:32 * c + 32], AxisListType.X, A.min,
+                                            apply_absolute_value=True),
+               ["dt2%d" % (c // 4)], ["em%d" % c], "em%d%d" % (t, c // 4))
+
+        def column(i):
+            c0, c1 = halves[i]
+            ts(T.e16[:, c0:c1], T.em[:, c0:c1], 1024.0, A.mult, ["em%d" % c for c in range(c0, c1)], ["e16%d" % i],
+               float(C), A.min)
+
+        def pack(i, b):
+            c0, c1 = halves[i]
+            (cp if b < 2 else act)(T.pt[:, 64 * c0 + b:64 * c1:4], T.fs[:, FW * b:FW * b + C + 1].indirect(T.e16[:, c0:c1]),
+                                   ["fs%d" % b, "fsp", "e16%d" % i], ["pt%d%d" % (i, b)], grp="p%d%d" % (t, b // 2))
+
+        for c in range(7):
+            least(c)
+        column(0)
         gap()
         if last:
             turn(T.va[:], T.vw[:], ["vw"], ["va"])
-        tt(T.dd[:], T.vw[:].indirect(T.kap[:, 0:14]), T.slot2[:], A.subtract, ["vw", "kap", "slot2"], ["dd"])
-        gap()
+        column(1)
+        for i in range(2):
+            for b in range(4):
+                pack(i, b)
         if last:
-            tt(T.na[:], T.va[:], T.mf[:, 0:32], A.subtract, ["va", "mf"], ["na"])
+            tt(T.na[:], T.va[:], T.mf[:], A.subtract, ["va", "mf"], ["na"])
             for h in range(2):
                 dma("Y", T.ol[h:8:2, 0:C], T.ma[:, 16 * h:16 * h + 16], ["ma"], ["olm%d" % h], "ol")
                 dma("Y", T.ol[h:8:2, C:2 * C], T.na[:, 16 * h:16 * h + 16], ["na"], ["oln%d" % h], "ol")
             stores += ["olm0", "olm1", "oln0", "oln1"]
-        turn(T.dt2[:], T.dd[:], ["dd"], ["dt2"])
         gap()
-        for c in range(7):
-            op("V", lambda c=c: v.tensor_reduce(T.em[:, c:c + 1], T.dt2[:, 32 * c:32 * c + 32], AxisListType.X, A.min,
-                                                apply_absolute_value=True), ["dt2"], ["em%d" % c], "em%d" % t)
-        ts(T.e16[:, 0:7], T.em[:, 0:7], 1024.0, A.mult, ["em%d" % c for c in range(7)], ["e16"], float(C), A.min)
-        for b in range(4):
-            win = T.fs[:, FW * b:FW * b + C + 1].indirect(T.e16[:, 0:7])
-            rd = ["fs%d" % b, "fsp", "e16"]
-            if b < 2:
-                cp(T.pt[:, b:4 * CAP:4], win, rd, ["pt%d" % b], "pv%d" % t)
-            else:
-                act(T.pt[:, b:4 * CAP:4], win, rd, ["pt%d" % b], grp="ps%d" % t)
-        quant(T.pq[:], T.ps[:], T.pt[:], ["pt0", "pt1", "pt2", "pt3", "ptp"], ["pq"])
+        quant(T.pq[:], T.ps[:], T.pt[:], ["pt%d%d" % (i, b) for i in range(2) for b in range(4)] + ["ptp"], ["pq"])
         if not last:
             score_list(t + 1)
         wq, wsc = layer[t]
@@ -391,16 +402,16 @@ def rank_program(g, core, T, topo):
         wd = CAP + 2
         for b in (1, 0, 3, 2):
             (act if b % 2 else cp)(T.dh[:, 128 * b:128 * b + wd], T.psR[:, 512 * b:512 * b + wd], ["psR%d" % b], ["dh%d" % b])
-        s_plan, v_plan = plan(CUT[t], DIRECT[t], not last)
-        for _, b, c0, c1 in s_plan:
-            act(T.tmp[:, C * b + c0:C * b + c1], T.dh[:, 128 * b:128 * b + wd].indirect(T.n16[:, c0 // 16:c1 // 16]),
-                ["dh%d" % b, "n16"], ["tmp%d_%d" % (b, c0)])
         qk = []
-        for p in v_plan:
-            if p[0] == "q":
+        for p in PLAN[t]:
+            if p[0] == "g":
+                _, b, c0, c1 = p
+                act(T.tmp[:, C * b + c0:C * b + c1], T.dh[:, 128 * b:128 * b + wd].indirect(T.n16[:, c0 // 16:c1 // 16]),
+                    ["dh%d" % b, "n16"], ["tmp%d_%d" % (b, c0)])
+            elif p[0] == "q":
                 k = p[1]
                 c0, c1 = CUT[t][k], CUT[t][k + 1]
-                rd = ["t%d_%d_%d" % (t + 1, x[1], x[2]) for x in v_plan if x[0] != "q" and c0 <= x[2] < c1]
+                rd = ["t%d_%d_%d" % (t + 1, x[1], x[2]) for x in PLAN[t] if x[0] in "ad" and x[2] < c1 and c0 < x[3]]
                 key = "q%d%d" % (t + 1, k)
                 qk.append(key)
                 if c1 == C and not last:

@@ -2,8 +2,10 @@ from concourse.mybir import dt, AluOpType, AxisListType, ActivationFunctionType
 
 C, CAP, ROUNDS, PAD = 512, 112, 2, 12
 FW = 528
-BIG = 4.0e29
+BIG = 8.0e29
 CODE = "float8_e4m3fn_x4"
+LATE = 160
+MID = 320
 
 
 def _sb(dtype, **widths):
@@ -12,28 +14,31 @@ def _sb(dtype, **widths):
 
 SCRATCH = {
     "psF": ("psum", [128, 2048], "float32"), "psR": ("psum", [128, 2048], "float32"),
-    **_sb("bfloat16", t0=4 * (C + PAD), t1=4 * (C + PAD), t2=4 * C, ut=512, vt=512, et=2048, fs=4 * FW, pt=512, ht=512,
-          dh=512, tmp=4 * C, keep1=192, f1=192, g1=192),
-    **_sb(CODE, q0=C + PAD, q1=C + PAD, q2=C, uq=128, vq=128, eq=512, woc=512, w0c=512, w1c=512, pq=128, hq=128),
-    **_sb("uint8", s0=C + PAD, s1=C + PAD, s2=C, us=128, vs=128, es=512, wos=512, w0s=512, w1s=512, ps=128, hs=128),
+    **_sb("bfloat16", t0=4 * (C + PAD), t1=4 * (C + PAD), t2=4 * C, ut=512, vt=512, et=516, zt=1024, fs=4 * FW, pt=512,
+          ht=512, dh=512, tmp=4 * C),
+    **_sb(CODE, qa=C + PAD, qb=256, q2=C, uq=128, vq=128, eq=512, woc=512, w0c=512, w1c=512, pq=128, hq=128),
+    **_sb("uint8", sa=C + PAD, sb=256, s2=C, us=128, vs=128, es=512, wos=512, w0s=512, w1s=512, ps=128, hs=128),
     **_sb("int32", pi=8),
-    **_sb("uint16", ox=8, om=2, o1=12, op=4, kap=32, e16=8, n16=32),
-    **_sb("float32", ys=C, pf=8, cf=8, jrow=128, jabs=128, wrow=48, a0=48, cap=48, capf=48, keep=96, r1=192, slot1=192,
-          r2=224, slot2=224, k1=12, st=768, xs=48, m1=48, m2=48, c1=48, c2=48, z0=164, z1=188, a3=164, ma=32,
-          chg=96, lb=96, mf=32, mt=32, wt=96, ub=64, vu=32, vw=32, dd=224, dt2=224, em=8, va=32, na=32),
+    **_sb("uint16", ox=8, om=2, o1=2, od=2, kap=64, e16=16, n16=32),
+    **_sb("float32", ys=C, pf=16, wrow=48, a0=48, cap=48, xrow=64, keep=64, r1=8, slot1=8, r2=224, slot2=224, st=768,
+          xs=48, m1=48, m2=48, m8=36, c1=48, c2=48, z0=128, z1=184, a3=128, ma=32, xy=192, lb=96, mf=32, mt=32, wt=96,
+          ub=64, kf=32, sg=448, f1=448, vu=32, vw=32, dd=224, dt2=224, em=8, va=32, na=32),
 }
 POOL = {"V": 48, "S": 24, "P": 20, "G": 12, "D": 40}
 SEMAPHORES = [k + str(i) for k in POOL for i in range(POOL[k])] + ["w0in", "w1in", "sent"]
 
-CUT = [[0, 384, 512], [0, 256, 384, 512]]
-PLAN = [
-    [("g", 1, 0, 384), ("g", 3, 0, 384), ("g", 2, 256, 512), ("g", 1, 384, 512), ("g", 3, 384, 512),
-     ("d", 0, 0, 512), ("d", 2, 0, 256), ("a", 1, 0, 384), ("a", 3, 0, 384), ("a", 2, 256, 512), ("a", 1, 384, 512),
-     ("q", 0), ("a", 3, 384, 512), ("q", 1)],
-    [("g", 1, 0, 256), ("g", 3, 0, 256), ("g", 1, 256, 512), ("g", 3, 256, 384), ("g", 2, 256, 384),
-     ("g", 3, 384, 512), ("g", 2, 384, 512),
-     ("d", 0, 0, 512), ("d", 2, 0, 256), ("a", 1, 0, 256), ("a", 3, 0, 256), ("a", 1, 256, 512), ("q", 0),
-     ("a", 3, 256, 384), ("a", 2, 256, 384), ("a", 3, 384, 512), ("q", 1), ("a", 2, 384, 512), ("q", 2)],
+PARTS = [(0, 4), (4, 7)]
+LISTS = [
+    "f0 o1b xs fsp ptp m1 c1 m2 c2 z2 z0 m8 c3 f1 z3 z1 x f2 y a3 lb1 lb0 mf wt f3 mt ub s3s vu s6v s5v s4v vw s2s r6 "
+    "s0s r5 r4 s1s k0 k1 d0 d1 t0 t1 e1 e0 e3 e2 e6 e5 e4 l0 p02s l1 p03s p01v p00v p10v n16 p13s p11v p12s pq W0 htp W1 "
+    "W3 h1v h0s W2 h2s h3v t1p hq ox1 D1 D0 D3 D2 u1s u0v u2v u3s G1.160.512 G3.160.512 G2.352.512 G1.0.160 G3.0.160 "
+    "G0.0.160 B0.160.512 B2.160.352 A1.160.512 A3.160.512 A2.352.512 B2.0.160 Q160.512 early A1.0.160 A3.0.160 A0.0.160 "
+    "Q0.160 vq",
+    "xs m1 f0 c1 m2 c2 z2 z0 m8 c3 z3 z1 y f1 x a3 lb1 lb0 f2 mf wt f3 mt ma ub s2s s3s vu s0s s5v s4v s6v s1s vw r5 r4 "
+    "r6 k0 k1 d0 d1 t0 t1 e3 e0 e1 e2 e6 e4 e5 l0 p02s l1 p01v p00v p03s p10v p11v p12s p13s va pq W0 na W1 h1v W2 h0s "
+    "W3 h3v h2s hq D0 D1 n16 u1s u0v D3 u3s D2 G1.0.256 G3.0.256 u2v G1.256.512 B0.0.384 G3.256.512 G2.256.384 "
+    "G0.384.512 B2.0.256 A1.0.256 A3.0.64 A3.64.256 A1.256.416 Q0.256 B2.384.512 A3.256.512 A2.256.384 Y0.256s "
+    "A1.416.512 A0.384.512 Q256.384 Q384.512 osc Y256.384v Y384.512v",
 ]
 
 
@@ -57,6 +62,8 @@ def emit(ops, queues, T):
             deps.update(readers.get(k, []))
         deps.discard(i)
         have = known.setdefault(q, set())
+        if o["adds"]:
+            have.update(writer[k] for k in o["w"])
         waits = []
         for j in sorted(deps, reverse=True):
             if j in have:
@@ -114,9 +121,12 @@ def rank_program(g, core, T, topo):
     v, s, pe = g.vector, g.scalar, g.tensor
     queues = {"V": v, "S": s, "P": pe, "G": g, "Y": g.sync}
     ops = []
+    stale = set()
 
-    def op(q, fn, r=(), w=(), grp=None, dma=False, sem=None):
-        ops.append({"q": q, "fn": fn, "r": list(r), "w": list(w), "grp": grp, "dma": dma, "sem": sem})
+    def op(q, fn, r=(), w=(), grp=None, dma=False, sem=None, adds=False):
+        assert not stale & set(r)
+        stale.difference_update(w)
+        ops.append({"q": q, "fn": fn, "r": list(r), "w": list(w), "grp": grp, "dma": dma, "sem": sem, "adds": adds})
 
     def dma(q, out, in_, r, w, grp=None):
         op(q, lambda: queues[q].dma_start(out, in_), r, w, grp, True)
@@ -142,14 +152,18 @@ def rank_program(g, core, T, topo):
     def turn(out, a, r, w, grp=None):
         op("V", lambda: v.transpose(out, a), r, w, grp)
 
-    def act(out, a, r, w, func=None, bias=0.0, scale=1.0, grp=None):
-        op("S", lambda: s.activation(out, a, F.Copy if func is None else func, bias=bias, scale=scale), r, w, grp)
+    def reduce(out, a, alu, r, w, size=False):
+        op("V", lambda: v.tensor_reduce(out, a, AxisListType.X, alu, apply_absolute_value=size), r, w)
 
-    def quant(qc, qs, tile, r, w):
-        op("V", lambda: v.quantize_mx(qc, qs, tile), r, w)
+    def act(out, a, r, w, func=None, bias=0.0, scale=1.0, grp=None, total=None):
+        op("S", lambda: s.activation(out, a, F.Copy if func is None else func, bias=bias, scale=scale, accum_out=total),
+           r, w, grp)
 
-    def mm(out, wc, ws, xc, xs, r, w, grp=None):
-        op("P", lambda: pe.matmul_mx(out, wc, ws, xc, xs, True, True), r, w, grp)
+    def quant(qc, qs, tile, r, w, grp=None):
+        op("V", lambda: v.quantize_mx(qc, qs, tile), r, w, grp)
+
+    def mm(out, wc, ws, xc, xs, r, w, grp=None, start=True, stop=True):
+        op("P", lambda: pe.matmul_mx(out, wc, ws, xc, xs, start, stop), r, w, grp, adds=not start)
 
     def iota(out, pattern, base, mult, w, flt=True, grp=None):
         if flt:
@@ -190,53 +204,48 @@ def rank_program(g, core, T, topo):
     op(None, None, (), ["w0"], sem=("w0in", in0))
     op(None, None, (), ["w1"], sem=("w1in", in1))
 
-    dma("Y", T.t0[:, 0:1024], T.x[:, 0:1024], (), ["t0a"])
-    dma("Y", T.t0[:, 1024:2048], T.x[:, 1024:2048], (), ["t0b"])
+    dma("Y", T.t0[:, 4 * MID:4 * C], T.x[:, 4 * MID:4 * C], (), ["t0a"])
     dma("Y", T.ut[:], T.u[:], (), ["ut"])
+    dma("Y", T.t0[:, 4 * LATE:4 * MID], T.x[:, 4 * LATE:4 * MID], (), ["t0b"])
+    dma("Y", T.t0[:, 0:4 * LATE], T.x[:, 0:4 * LATE], (), ["t0c"])
     dma("Y", T.wos[:], T.ws[:], (), ["wos"])
     dma("Y", codes(T.woc, 0, 512), T.wc[:], (), ["woc"])
 
+    fill(T.et[:], 0.0, ["et"])
     iota(T.pi[:, 0:1], [[0, 1]], 0, 1, ["pi0"], False)
-    iota(T.wrow[:], [[0, 2], [1, 24]], 0, 0, ["wrow"])
-    iota(T.jrow[:], [[1, 128]], 0, -1, ["jrow"])
-    iota(T.r1[:, 0:32], [[16, 2], [0, 16]], 0, 0, ["r1a"], grp="r1")
-    iota(T.r1[:, 32:192], [[16, 5], [0, 32]], 32, 0, ["r1b"], grp="r1")
+    one = T.et[:, 3:515:4]
+    op("G", lambda: g.affine_select(one, one, [[-1, 128]], A.not_equal, 1.0, 0, 1), ["et"], ["et"])
+    iota(T.wrow[:], [[1, 24], [0, 2]], 0, 0, ["wrow"])
+    iota(T.z0[:], [[0, 64], [1, 2]], 0, 0, ["zk"])
+    iota(T.xrow[:], [[1, 64]], -31, 0, ["xrow"])
+    iota(T.r1[:], [[16, 8]], 0, 0, ["r1"])
     iota(T.r2[:], [[16, 7], [1000, 2], [1, 16]], 0, 0, ["r2"])
-    fill(T.et[:, 0:512], 0.0, ["et0"], "e")
-    ts(T.pi[:, 1:2], T.pi[:, 0:1], 15, A.bitwise_and, ["pi0"], ["pi1"], grp="pi")
-    ts(T.pi[:, 2:3], T.pi[:, 0:1], 31, A.bitwise_and, ["pi0"], ["pi2"], grp="pi")
-    ts(T.pi[:, 3:4], T.pi[:, 0:1], 16, A.bitwise_and, ["pi0"], ["pi3"], grp="pi")
-    ts(T.pi[:, 4:5], T.pi[:, 0:1], 14, A.bitwise_and, ["pi0"], ["pi4"], grp="pi")
-    fill(T.et[:, 512:1024], 0.0, ["et1"], "e")
-    cp(T.pf[:, 1:5], T.pi[:, 1:5], ["pi1", "pi2", "pi3", "pi4"], ["pf"])
-    fill(T.et[:, 1024:1536], 0.0, ["et2"], "e")
-    qc = T.pf[:, 1:2]
-    ts(T.pf[:, 6:7], T.pf[:, 2:3], 16.0, A.mult, ["pf"], ["i16"], grp="c")
-    ts(T.pf[:, 5:6], qc, 64.0, A.mult, ["pf"], ["q64"], grp="c")
-    steps = [(12.0, -736.0, 0.0), (8.0, -784.0, 288.0), (4.0, -736.0, 528.0)]
-    for k in range(3):
-        ts(T.cf[:, k:k + 1], qc, steps[k][0], A.is_ge, ["pf"], ["cf%d" % k], steps[k][1], A.mult, grp="c")
-    fill(T.et[:, 1536:2048], 0.0, ["et3"], "e")
-    act(T.jabs[:], T.jrow[:], ["jrow"], ["jabs"], F.Abs)
-    for b in range(4):
-        act(T.et[:, 512 * b + b:512 * b + 512:4], T.jabs[:], ["jabs"], ["et%d" % b], F.Relu, 1.0, -1.0, grp="et")
-    ts(T.a0[:], T.wrow[:], T.pf[:, 6:7], A.add, ["i16", "wrow"], ["a0"])
+    fill(T.t0[:, 4 * C:], 0.0, ["t0p"])
+    fill(T.zt[:, 0:4 * LATE], 0.0, ["zt"])
+    for k, m in enumerate((15, 16, 1)):
+        ts(T.pi[:, k + 1:k + 2], T.pi[:, 0:1], m, A.bitwise_and, ["pi0"], ["pi%d" % (k + 1)], grp="pi")
+    fill(T.xy[:, 32:192], 0.0, ["xy"])
+    cp(T.pf[:, 1:4], T.pi[:, 1:4], ["pi1", "pi2", "pi3"], ["pf"])
+    fill(T.lb[:, 0:49:48], 0.0, ["lbz"], "y")
+    fill(T.ub[:, 0:1], 0.0, ["ub0"], "y")
+    fill(T.kf[:], 0.0, ["kfz"], "y")
+    qc, hc, bc = T.pf[:, 1:2], T.pf[:, 2:3], T.pf[:, 3:4]
+    ts(T.pf[:, 4:5], qc, hc, A.add, ["pf"], ["i16"], 16.0, A.mult, grp="c")
+    ts(T.pf[:, 5:6], bc, -0.5, A.mult, ["pf"], ["odd"], qc, A.add, grp="c")
+    ts(T.pf[:, 6:7], qc, 8.0, A.is_ge, ["pf"], ["far"], -23.0, A.mult, grp="c")
+    ts(T.pf[:, 7:8], hc, -62.5, A.mult, ["pf"], ["par"], grp="c")
+    ts(T.pf[:, 8:9], hc, 0.125, A.mult, ["pf"], ["sgn"], -1.0, A.add, grp="c")
+    ts(T.pf[:, 9:10], qc, 0.5, A.add, ["pf"], ["qh"], grp="c")
 
-    def score_list(t):
-        for k in range(3):
-            ts(T.ox[:, 4 * t + k:4 * t + k + 1], T.cf[:, k:k + 1], T.pf[:, 5:6], A.add, ["cf%d" % k, "q64"],
-               ["ox%d%d" % (t, k)], steps[k][2] + t, A.add, grp="ox%d" % t)
+    def unit(b):
+        quant(T.eq[:, 128 * b:128 * b + 128], T.es[:, 128 * b:128 * b + 128], T.et[:, 3 - b:515 - b], ["et"], ["eq%d" % b])
 
-    score_list(0)
-    ts(T.capf[:], T.a0[:], float(C), A.is_ge, ["a0"], ["capf"], 2 * BIG, A.mult)
-    fill(T.t0[:, 4 * C:], 0.0, ["t0p"], "z")
-    fill(T.z0[:, 0:164:4], 0.0, ["zk0"], "z")
-    fill(T.z0[:, 1:164:2], 1.0, ["zk1"], "z")
-    fill(T.keep1[:], 1.0, ["keep1"], "z")
-    fill(T.k1[:], 0.0, ["k1"], "z")
-    ts(T.cap[:], T.capf[:], -BIG, A.add, ["capf"], ["cap"], grp="z")
-    ts(T.pf[:, 7:8], T.pf[:, 3:4], -62.5, A.mult, ["pf"], ["par"], grp="z")
-    ts(T.cf[:, 3:4], T.pf[:, 4:5], 16.0, A.mult, ["pf"], ["cf3"], -1.0, A.add, grp="z")
+    unit(0)
+    unit(1)
+    quant(T.qa[:, 0:LATE], T.sa[:, 0:LATE], T.zt[:, 0:4 * LATE], ["zt"], ["qs"])
+    act(T.a0[:], T.wrow[:], ["wrow", "i16"], ["a0"], F.Identity, T.pf[:, 4:5])
+    act(T.slot1[:], T.r1[:], ["r1", "qh"], ["slot1"], F.Identity, T.pf[:, 9:10])
+    act(T.slot2[:], T.r2[:], ["r2", "par"], ["slot2"], F.Identity, T.pf[:, 7:8])
 
     send(T.w0s[:], T.wos[:], d0, narrow(core), "w0in", ["wos"])
     send(codes(T.w0c, 0, 512), codes(T.woc, 0, 512), d0, narrow(core), "w0in", ["woc"])
@@ -247,200 +256,241 @@ def rank_program(g, core, T, topo):
         send(codes(T.w1c, 0, 512), codes(T.w0c, 0, 512), d0, wide(core, d0), "w1in", ["w0"])
         send(T.w1s[:], T.w0s[:], d0, wide(core, d0), "w1in", ["w0"])
 
-    quant(T.q0[:, 0:256], T.s0[:, 0:256], T.t0[:, 0:1024], ["t0a"], ["q00"])
-    quant(T.q0[:, 256:C + PAD], T.s0[:, 256:C + PAD], T.t0[:, 1024:], ["t0b", "t0p"], ["q01"])
+    def early(keys):
+        mm(T.psR[:, 0:512], T.uq[:], T.us[:], T.qa[:, 0:C], T.sa[:, 0:C], ["uq", "qs"] + keys, ["psR0"], stop=False)
+        mm(T.psR[:, 512:1024], T.uq[:], T.us[:], T.qa[:, PAD:C + PAD], T.sa[:, PAD:C + PAD], ["uq", "qs"] + keys, ["psR1"],
+           stop=False)
+
+    quant(T.qa[:, MID:], T.sa[:, MID:], T.t0[:, 4 * MID:], ["t0a", "t0p"], ["q00"])
     quant(T.uq[:], T.us[:], T.ut[:], ["ut"], ["uq"])
-    quant(T.eq[:], T.es[:], T.et[:], ["et0", "et1", "et2", "et3"], ["eq"])
-    spare = [
-        lambda: fill(T.keep[:], 1.0, ["keep"]),
-        lambda: ts(T.om[:, 0:1], qc, 4.0, A.mult, ["pf"], ["om0"], 3.0, A.add, grp="v"),
-        lambda: ts(T.om[:, 1:2], qc, 4.0, A.mult, ["pf"], ["om1"], 99.0, A.add, grp="v"),
-        lambda: fill(T.chg[:], 0.0, ["chg0", "chg1"], "y"),
-        lambda: fill(T.keep[:, 47:48], 0.0, ["keep"], "y"),
-        lambda: fill(T.k1[:, 3:12:2], 16.0, ["k1"], "y"),
-        lambda: ts(T.pf[:, 0:1], T.pf[:, 2:3], T.pf[:, 3:4], A.add, ["pf"], ["qh"], grp="y"),
-        lambda: fill(T.lb[:, 0:1], 0.0, ["lb0"], "y"),
-        lambda: fill(T.ub[:, 0:1], 0.0, ["ub0"], "x"),
-        lambda: ts(T.o1[:], T.k1[:], T.pf[:, 0:1], A.add, ["qh", "k1"], ["o1"], grp="x"),
-        lambda: fill(T.keep1[:, 0:17:16], 0.0, ["keep1"], "x"),
-        lambda: fill(T.keep1[:, 32:192:32], 0.0, ["keep1x"], "x", ["t0p"]),
-        lambda: ts(T.op[:, 0:1], T.cf[:, 3:4], 15.0, A.max, ["cf3"], ["op0"], 95.0, A.min, grp="u"),
-        lambda: ts(T.op[:, 2:3], T.cf[:, 3:4], 32.0, A.add, ["cf3"], ["op1"], 95.0, A.min, grp="u"),
-        lambda: fill(T.fs[:, C:4 * FW:FW], 0.0, ["fsp"], "w"),
-        lambda: fill(T.pt[:, 4 * CAP:], 0.0, ["ptp"], "w"),
-        lambda: fill(T.t1[:, 4 * C:], 0.0, ["t1p"]),
-    ]
+    quant(T.qa[:, LATE:MID], T.sa[:, LATE:MID], T.t0[:, 4 * LATE:4 * MID], ["t0b"], ["q01"])
+    early(["q00", "q01"])
+    unit(2)
+    unit(3)
+    quant(T.qb[:, 0:LATE], T.sb[:, 0:LATE], T.t0[:, 0:4 * LATE], ["t0c"], ["qb"])
+    odd = T.pf[:, 5:6]
+    ts(T.ox[:, 0:1], odd, 32.0, A.mult, ["odd"], ["oxa"], grp="ox")
+    ts(T.ox[:, 2:3], odd, 9.0, A.add, ["odd"], ["oxc"], 32.0, A.mult, grp="ox")
+    ts(T.pf[:, 10:11], odd, T.pf[:, 6:7], A.add, ["odd", "far"], ["oxf"], 16.0, A.add)
+    ts(T.cap[:], T.a0[:], 0.5 - C, A.add, ["a0"], ["cap"], BIG, A.mult)
+    ts(T.keep[:], T.xrow[:], T.pf[:, 8:9], A.mult, ["xrow", "sgn"], ["keep"], 0.0, A.is_gt)
+    ts(T.om[:, 0:1], qc, 8.0, A.mult, ["pf"], ["om0"], 3.0, A.add, grp="v")
+    ts(T.om[:, 1:2], qc, 8.0, A.mult, ["pf"], ["om1"], 7.0, A.add, grp="v")
+    ts(T.ox[:, 1:2], T.pf[:, 10:11], 32.0, A.mult, ["oxf"], ["oxb"])
+    ts(T.o1[:, 0:1], hc, 2.0, A.mult, ["pf"], ["o1a"], qc, A.add, grp="u")
+    ts(T.od[:, 0:1], qc, bc, A.subtract, ["pf"], ["od"], 0.5, A.mult, grp="u")
 
-    def gap(n=1):
-        for _ in range(min(n, len(spare))):
-            spare.pop(0)()
-
-    gap(3)
-    tiles = [(T.t0, T.q0, T.s0), (T.t1, T.q1, T.s1), (T.t2, T.q2, T.s2)]
     layer = [(T.w0c, T.w0s), (T.w1c, T.w1s)]
-    halves = [(0, 4), (4, 7)]
-    qk = ["q00", "q01"]
+    part_of = {c: i for i, (c0, c1) in enumerate(PARTS) for c in range(c0, c1)}
     stores = []
+    wd = CAP + 2
+
+    def runs(name, c0, c1, width=32):
+        return ["%s_%d" % (name, k) for k in range(c0 // width, c1 // width)]
+
+    qk = ["q00", "q01"]
     for t in range(ROUNDS):
-        _, qt, sc = tiles[t]
-        tn, qn, sn = tiles[t + 1]
+        tn, qn, sn = [(T.t1, T.qa, T.sa), (T.t2, T.q2, T.s2)][t]
+        wq, wsc = layer[t]
         last = t == ROUNDS - 1
-        mm(T.psR[:, 0:512], T.uq[:], T.us[:], qt[:, 0:C], sc[:, 0:C], ["uq"] + qk, ["psR0"], "s%d" % t)
-        mm(T.psR[:, 512:1024], T.uq[:], T.us[:], qt[:, PAD:C + PAD], sc[:, PAD:C + PAD], ["uq"] + qk, ["psR1"], "s%d" % t)
+        first = len(ops)
+        names = LISTS[t].split()
+        mm(T.psR[:, 0:LATE], T.uq[:], T.us[:], T.qb[:, 0:LATE], T.sb[:, 0:LATE], ["qb"], ["psR0"], "s%d" % t, False)
+        mm(T.psR[:, 512:512 + LATE - PAD], T.uq[:], T.us[:], T.qb[:, PAD:LATE], T.sb[:, PAD:LATE], ["qb"], ["psR1"],
+           "s%d" % t, False)
         for b in range(4):
-            mm(T.psF[:, 512 * b:512 * b + 512], T.eq[:, 128 * b:128 * b + 128], T.es[:, 128 * b:128 * b + 128],
-               qt[:, 0:C], sc[:, 0:C], ["eq"] + qk, ["psF%d" % b])
-        for b in range(4):
-            act(T.fs[:, FW * b:FW * b + C], T.psF[:, 512 * b:512 * b + 512], ["psF%d" % b], ["fs%d" % b])
+            e, es = T.eq[:, 128 * b:128 * b + 128], T.es[:, 128 * b:128 * b + 128]
+            mm(T.psF[:, 512 * b:512 * b + 512], e, es, T.qa[:, 0:C], T.sa[:, 0:C], ["eq%d" % b, "qs"] + qk, ["psF%d" % b],
+               stop=False)
+            mm(T.psF[:, 512 * b:512 * b + LATE], e, es, T.qb[:, 0:LATE], T.sb[:, 0:LATE], ["qb"], ["psF%d" % b],
+               start=False)
         for b in range(PAD):
             turn(T.st[:, 64 * b:64 * b + 64], T.psR[:, b:1024:16], ["psR0", "psR1"], ["st%d" % b], "tr%d" % t)
-        gap(2)
-        tt(T.xs[:], T.st[:].indirect(T.ox[:, 4 * t:4 * t + 3]), T.cap[:], A.max,
-           ["st%d" % b for b in range(PAD)] + ["cap"] + ["ox%d%d" % (t, k) for k in range(3)], ["xs"])
-        gap(2)
         if t == 0:
-            dma("Y", T.vt[:], T.v[:], ["xs"], ["vt"])
-            act(T.slot1[:], T.r1[:], ["r1a", "r1b", "pf"], ["slot1"], F.Identity, qc)
-            act(T.slot2[:], T.r2[:], ["r2", "par"], ["slot2"], F.Identity, T.pf[:, 7:8])
-        tt(T.c1[:, 0:47], T.xs[:, 1:48], T.xs[:, 0:47], A.is_lt, ["xs"], ["c1"])
-        tt(T.m1[:, 0:47], T.xs[:, 0:47], T.xs[:, 1:48], A.min, ["xs"], ["m1"])
-        gap()
-        tt(T.z1[:, 2:188:4], T.c1[:, 0:47], T.a0[:, 0:47], A.add, ["c1", "a0"], ["z2"])
-        tt(T.c2[:, 0:45], T.m1[:, 2:47], T.m1[:, 0:45], A.is_lt, ["m1"], ["c2"])
-        tt(T.m2[:, 0:45], T.m1[:, 0:45], T.m1[:, 2:47], A.min, ["m1"], ["m2"])
-        tt(T.z1[:, 0:164:4], T.c1[:, 4:45], T.a0[:, 4:45], A.add, ["c1", "a0"], ["z0"], "zz%d" % t)
-        tt(T.z1[:, 3:164:4], T.c2[:, 0:41], T.z1[:, 10:172:4], A.mult, ["c2", "z2"], ["z3"], "zz%d" % t)
-        tt(T.z1[:, 1:164:4], T.c2[:, 4:45], T.z1[:, 26:188:4], A.mult, ["c2", "z2"], ["z1"], "zz%d" % t)
-        tt(T.z0[:, 2:164:4], T.m2[:, 4:45], T.m2[:, 0:41], A.is_lt, ["m2"], ["c3"], "zz%d" % t)
-        gap(2)
-        scan(T.a3[:], T.z0[:], T.z1[:, 0:164], A.mult, A.max, ["z0", "z1", "z2", "z3", "c3", "zk0", "zk1"], ["a3"])
-        gap(2)
-        for h in range(2):
-            tt(T.chg[:, 48 * h:48 * h + 16], T.a3[:, 96 * h + 7:96 * h + 68:4], T.a3[:, 96 * h + 3:96 * h + 64:4],
-               A.not_equal, ["a3"], ["chg%d" % h], "ch%d" % t)
-        ts(T.mf[:], T.a3[:].indirect(T.om[:]), 1.0 / 1024, A.mult, ["a3", "om0", "om1"], ["mf"])
-        scan(T.lb[:, 1:96], T.chg[:, 0:95], T.keep[:, 0:95], A.add, A.mult, ["chg0", "chg1", "keep"], ["lb"])
-        turn(T.mt[:], T.mf[:], ["mf"], ["mt"])
-        if last:
-            ts(T.ma[:], T.mf[:], 1024.0, A.mult, ["mf"], ["ma"])
-        gap()
-        turn(T.wt[:], T.lb[:], ["lb", "lb0"], ["wt"])
-        gap(2)
-        scan(T.ub[:, 1:64], T.wt[:, 32:95], T.keep[:, 16:79], A.add, A.mult, ["wt", "keep"], ["ub"])
-        tt(T.vu[:], T.wt[:, 0:64].indirect(T.o1[:, 2:4]), T.mt[:], A.add, ["wt", "mt", "o1"], ["vu"])
-        gap()
-        for i in range(2):
-            tt(T.f1[:, 96 * i:96 * i + 96], T.ub[:].indirect(T.o1[:, 6 * i:6 * i + 6]), T.slot1[:, 96 * i:96 * i + 96],
-               A.is_le, ["ub", "ub0", "o1", "slot1"], ["f1%d" % i])
-        for i in range(2):
-            scan(T.g1[:, 96 * i:96 * i + 96], T.keep1[:, 96 * i:96 * i + 96], T.f1[:, 96 * i:96 * i + 96], A.mult, A.add,
-                 ["f1%d" % i, "keep1", "keep1x"], ["g1%d" % i])
-            if i == 0:
-                tt(T.vw[:], T.ub[:].indirect(T.o1[:, 2:4]), T.vu[:], A.add, ["ub", "ub0", "vu", "o1"], ["vw"])
-        for i in range(2):
-            ts(T.kap[:, 16 * i:16 * i + 16], T.g1[:, 96 * i:96 * i + 96].indirect(T.op[:, 2 * i:2 * i + 1]), -1.0, A.add,
-               ["g1%d" % i, "op%d" % i], ["kap%d" % i])
-            if i == 0:
-                ts(T.n16[:], T.vw[:], float(CAP), A.min, ["vw"], ["n16"])
-        for i, (c0, c1) in enumerate(halves):
+            dma("Y", T.vt[:], T.v[:], ["st0"], ["vt"])
+        qk = runs("q", 0 if last else LATE, C)
+
+        def held(b):
+            act(T.fs[:, FW * b:FW * b + C], T.psF[:, 512 * b:512 * b + 512], ["psF%d" % b], ["fs%d" % b])
+
+        def kf(c):
+            i = part_of[c]
+            k = 8 * i + c - PARTS[i][0]
+            return T.kf[:, k:k + 1]
+
+        def search(c, e):
+            if e == "v":
+                ts(T.f1[:, 64 * c:64 * c + 64], T.ub[:], T.slot1[:, c:c + 1], A.is_lt, ["ub", "ub0", "slot1"], ["f1%d" % c],
+                   2.0, A.mult)
+            else:
+                act(T.sg[:, 64 * c:64 * c + 64], T.ub[:], ["ub", "ub0", "slot1", "kfz"], ["kf%d" % c, "sg%d" % c], F.Sign,
+                    T.slot1[:, c:c + 1], -1.0, total=kf(c))
+
+        def count(c):
+            reduce(kf(c), T.f1[:, 64 * c:64 * c + 64], A.add, ["f1%d" % c, "kfz"], ["kf%d" % c])
+
+        def run_list(i):
+            c0, c1 = PARTS[i]
+            on_v = ["s%dv" % c in names for c in range(c0, c1)]
+            assert all(on_v) or not any(on_v)
+            ts(T.kap[:, 16 * i:16 * i + 16], T.kf[:, 8 * i:8 * i + 8].indirect(T.od[:, 0:1]), 0.5, A.mult,
+               ["od"] + ["kf%d" % c for c in range(c0, c1)], ["kap%d" % i], -33.0 if on_v[0] else -1.0, A.add)
+
+        def candidates(i):
+            c0, c1 = PARTS[i]
             tt(T.dd[:, 32 * c0:32 * c1], T.vw[:].indirect(T.kap[:, 16 * i:16 * i + 2 * (c1 - c0)]),
                T.slot2[:, 32 * c0:32 * c1], A.subtract, ["vw", "kap%d" % i, "slot2"], ["dd%d" % i])
-        for i, (c0, c1) in enumerate(halves):
+
+        def across(i):
+            c0, c1 = PARTS[i]
             turn(T.dt2[:, 32 * c0:32 * c1], T.dd[:, 32 * c0:32 * c1], ["dd%d" % i], ["dt2%d" % i])
 
+        def listed(i):
+            c0, c1 = PARTS[i]
+            k = sum(2 * ((b - a + 1) // 2) for a, b in PARTS[:i])
+            return T.e16[:, k:k + c1 - c0]
+
         def least(c):
-            op("V", lambda: v.tensor_reduce(T.em[:, c:c + 1], T.dt2[:, 32 * c:32 * c + 32], AxisListType.X, A.min,
-                                            apply_absolute_value=True),
-               ["dt2%d" % (c // 4)], ["em%d" % c], "em%d%d" % (t, c // 4))
+            reduce(T.em[:, c:c + 1], T.dt2[:, 32 * c:32 * c + 32], A.min, ["dt2%d" % part_of[c]], ["em%d" % c], True)
 
         def column(i):
-            c0, c1 = halves[i]
-            ts(T.e16[:, c0:c1], T.em[:, c0:c1], 1024.0, A.mult, ["em%d" % c for c in range(c0, c1)], ["e16%d" % i],
+            c0, c1 = PARTS[i]
+            ts(listed(i), T.em[:, c0:c1], 1024.0, A.mult, ["em%d" % c for c in range(c0, c1)], ["e16%d" % i],
                float(C), A.min)
 
-        def pack(i, b):
-            c0, c1 = halves[i]
-            (cp if b < 2 else act)(T.pt[:, 64 * c0 + b:64 * c1:4], T.fs[:, FW * b:FW * b + C + 1].indirect(T.e16[:, c0:c1]),
-                                   ["fs%d" % b, "fsp", "e16%d" % i], ["pt%d%d" % (i, b)], grp="p%d%d" % (t, b // 2))
+        def pack(i, b, e):
+            c0, c1 = PARTS[i]
+            (cp if e == "v" else act)(T.pt[:, 64 * c0 + b:64 * c1:4], T.fs[:, FW * b:FW * b + C + 1].indirect(listed(i)),
+                                      ["fs%d" % b, "fsp", "e16%d" % i], ["pt%d%d" % (i, b)], grp="p%d%s" % (t, e))
 
-        for c in range(7):
-            least(c)
-        column(0)
-        gap()
-        if last:
-            turn(T.va[:], T.vw[:], ["vw"], ["va"])
-        column(1)
-        for i in range(2):
-            for b in range(4):
-                pack(i, b)
-        if last:
+        def product(b):
+            mm(T.psR[:, 512 * b:512 * b + 128], wq[:, 128 * b:128 * b + 128], wsc[:, 128 * b:128 * b + 128],
+               T.pq[:], T.ps[:], ["w%d" % t, "pq"], ["psR%d" % b, "R%d" % b])
+
+        def scaled(b, e):
+            src = T.psR[:, 512 * b:512 * b + CAP]
+            if e == "v":
+                ts(T.ht[:, b:4 * CAP:4], src, 0.03125, A.mult, ["psR%d" % b, "R%d" % b], ["ht%d" % b], grp="hv%d" % t)
+            else:
+                act(T.ht[:, b:4 * CAP:4], src, ["psR%d" % b, "R%d" % b], ["ht%d" % b], None, 0.0, 0.03125, grp="hs%d" % t)
+
+        def unpack(b):
+            mm(T.psR[:, 512 * b:512 * b + 128], T.eq[:, 128 * b:128 * b + 128], T.es[:, 128 * b:128 * b + 128],
+               T.hq[:], T.hs[:], ["eq%d" % b, "hq"], ["psR%d" % b, "D%d" % b])
+
+        def unpacked(b, e):
+            (act if e == "s" else cp)(T.dh[:, 128 * b:128 * b + wd], T.psR[:, 512 * b:512 * b + wd],
+                                      ["psR%d" % b, "D%d" % b], ["dh%d" % b])
+
+        def window(b, c0, c1):
+            return T.dh[:, 128 * b:128 * b + wd].indirect(T.n16[:, c0 // 16:c1 // 16])
+
+        def gather(b, c0, c1):
+            act(T.tmp[:, C * b + c0:C * b + c1], window(b, c0, c1), ["dh%d" % b, "n16"], runs("tmp%d" % b, c0, c1))
+
+        def add(b, c0, c1):
+            tt(tn[:, 4 * c0 + b:4 * c1:4], T.tmp[:, C * b + c0:C * b + c1], T.psF[:, 512 * b + c0:512 * b + c1], A.add,
+               runs("tmp%d" % b, c0, c1) + ["psF%d" % b], runs("t%d%d" % (t + 1, b), c0, c1))
+
+        def both(b, c0, c1):
+            tt(tn[:, 4 * c0 + b:4 * c1:4], window(b, c0, c1), T.fs[:, FW * b + c0:FW * b + c1], A.add,
+               ["dh%d" % b, "n16", "fs%d" % b], runs("t%d%d" % (t + 1, b), c0, c1))
+
+        def state(c0, c1):
+            rd = [k for b in range(4) for k in runs("t%d%d" % (t + 1, b), c0, c1)]
+            if c0 == 0 and not last:
+                assert c1 == LATE
+                quant(T.qb[:, 0:c1], T.sb[:, 0:c1], tn[:, 0:4 * c1], rd, ["qb"])
+                return
+            keys = runs("q", c0, c1)
+            end = c1
+            if c1 == C and not last:
+                end += PAD
+                rd.append("t1p")
+            quant(qn[:, c0:end], sn[:, c0:end], tn[:, 4 * c0:4 * end], rd, keys + ([] if last else ["q00", "q01"]))
+            if last:
+                k = c0 // 128
+                mm(T.psR[:, 512 * k:512 * k + c1 - c0], T.vq[:], T.vs[:], qn[:, c0:c1], sn[:, c0:c1], ["vq"] + keys,
+                   ["psR%d" % k, "Y%d" % k])
+                dma("Y", T.oc[:, 4 * c0:4 * c1], codes(qn, c0, c1), keys, ["oc%d" % k])
+                stores.append("oc%d" % k)
+
+        def result(c0, c1, e):
+            k = c0 // 128
+            (cp if e == "v" else act)(T.ys[:, c0:c1], T.psR[:, 512 * k:512 * k + c1 - c0], ["psR%d" % k, "Y%d" % k],
+                                      ["ys%d" % k])
+            dma("S" if c1 == C else "Y", T.y[:, c0:c1], T.ys[:, c0:c1], ["ys%d" % k], ["y%d" % k])
+            stores.append("y%d" % k)
+
+        def scales():
+            for r in range(4):
+                dma("S" if r % 2 else "Y", T.osc[4 * r:4 * r + 4, :], sn[32 * r:32 * r + 4, :], qk, ["osc%d" % r])
+                stores.append("osc%d" % r)
+
+        def lists_out():
             tt(T.na[:], T.va[:], T.mf[:], A.subtract, ["va", "mf"], ["na"])
             for h in range(2):
                 dma("Y", T.ol[h:8:2, 0:C], T.ma[:, 16 * h:16 * h + 16], ["ma"], ["olm%d" % h], "ol")
                 dma("Y", T.ol[h:8:2, C:2 * C], T.na[:, 16 * h:16 * h + 16], ["na"], ["oln%d" % h], "ol")
-            stores += ["olm0", "olm1", "oln0", "oln1"]
-        gap()
-        quant(T.pq[:], T.ps[:], T.pt[:], ["pt%d%d" % (i, b) for i in range(2) for b in range(4)] + ["ptp"], ["pq"])
-        if not last:
-            score_list(t + 1)
-        wq, wsc = layer[t]
-        for b in range(4):
-            mm(T.psR[:, 512 * b:512 * b + 128], wq[:, 128 * b:128 * b + 128], wsc[:, 128 * b:128 * b + 128],
-               T.pq[:], T.ps[:], ["w%d" % t, "pq"], ["psR%d" % b])
-        for b in range(4):
-            src = T.psR[:, 512 * b:512 * b + 128]
-            if b % 2:
-                ts(T.ht[:, b:512:4], src, 0.03125, A.mult, ["psR%d" % b], ["ht%d" % b], grp="hv%d" % t)
-            else:
-                act(T.ht[:, b:512:4], src, ["psR%d" % b], ["ht%d" % b], None, 0.0, 0.03125, grp="hs%d" % t)
-        quant(T.hq[:], T.hs[:], T.ht[:], ["ht0", "ht1", "ht2", "ht3"], ["hq"])
-        if not last:
-            quant(T.vq[:], T.vs[:], T.vt[:], ["vt"], ["vq"])
-        for b in (1, 0, 3, 2):
-            mm(T.psR[:, 512 * b:512 * b + 128], T.eq[:, 128 * b:128 * b + 128], T.es[:, 128 * b:128 * b + 128],
-               T.hq[:], T.hs[:], ["eq", "hq"], ["psR%d" % b])
-        wd = CAP + 2
-        for b in (1, 0, 3, 2):
-            (act if b % 2 else cp)(T.dh[:, 128 * b:128 * b + wd], T.psR[:, 512 * b:512 * b + wd], ["psR%d" % b], ["dh%d" % b])
-        qk = []
-        for p in PLAN[t]:
-            if p[0] == "g":
-                _, b, c0, c1 = p
-                act(T.tmp[:, C * b + c0:C * b + c1], T.dh[:, 128 * b:128 * b + wd].indirect(T.n16[:, c0 // 16:c1 // 16]),
-                    ["dh%d" % b, "n16"], ["tmp%d_%d" % (b, c0)])
-            elif p[0] == "q":
-                k = p[1]
-                c0, c1 = CUT[t][k], CUT[t][k + 1]
-                rd = ["t%d_%d_%d" % (t + 1, x[1], x[2]) for x in PLAN[t] if x[0] in "ad" and x[2] < c1 and c0 < x[3]]
-                key = "q%d%d" % (t + 1, k)
-                qk.append(key)
-                if c1 == C and not last:
-                    c1 += PAD
-                    rd.append("t1p")
-                quant(qn[:, c0:c1], sn[:, c0:c1], tn[:, 4 * c0:4 * c1], rd, [key])
-                if last:
-                    bank = T.psR[:, 512 * k:512 * k + c1 - c0]
-                    mm(bank, T.vq[:], T.vs[:], qn[:, c0:c1], sn[:, c0:c1], ["vq", key], ["psR%d" % k])
-                    dma("Y", T.oc[:, 4 * c0:4 * c1], codes(qn, c0, c1), [key], ["oc%d" % k])
-                    if c1 == C:
-                        for r in range(4):
-                            dma("S" if r % 2 else "Y", T.osc[4 * r:4 * r + 4, :], sn[32 * r:32 * r + 4, :], qk, ["osc%d" % r])
-                            stores.append("osc%d" % r)
-                    (cp if c1 == C else act)(T.ys[:, c0:c1], bank, ["psR%d" % k], ["ys%d" % k])
-                    dma("S" if c1 == C else "Y", T.y[:, c0:c1], T.ys[:, c0:c1], ["ys%d" % k], ["y%d" % k])
-                    stores += ["oc%d" % k, "y%d" % k]
-            else:
-                e, b, c0, c1 = p
-                out = tn[:, 4 * c0 + b:4 * c1:4]
-                key = ["t%d_%d_%d" % (t + 1, b, c0)]
-                grp = "n%d%d" % (t, sum(c0 >= x for x in CUT[t]))
-                if e == "d":
-                    tt(out, T.dh[:, 128 * b:128 * b + wd].indirect(T.n16[:, c0 // 16:c1 // 16]),
-                       T.fs[:, FW * b + c0:FW * b + c1], A.add, ["dh%d" % b, "n16", "fs%d" % b], key, grp)
-                else:
-                    tt(out, T.tmp[:, C * b + c0:C * b + c1], T.psF[:, 512 * b + c0:512 * b + c1], A.add,
-                       ["tmp%d_%d" % (b, c0), "psF%d" % b], key, grp)
+            stores.extend(["olm0", "olm1", "oln0", "oln1"])
 
+        oxk = ["oxa", "oxb", "oxc"] if t == 0 else ["ox1"]
+        X, Y = T.xy[:, 0:32], T.xy[:, 96:128]
+        step = {
+            "o1b": lambda: ts(T.o1[:, 1:2], T.o1[:, 0:1], 16.0, A.add, ["o1a"], ["o1b"]),
+            "fsp": lambda: fill(T.fs[:, C:4 * FW:FW], 0.0, ["fsp"]),
+            "ptp": lambda: fill(T.pt[:, 4 * CAP:], 0.0, ["ptp"]),
+            "htp": lambda: fill(T.ht[:, 4 * CAP:], 0.0, ["htp"]),
+            "t1p": lambda: fill(T.t1[:, 4 * C:], 0.0, ["t1p"]),
+            "ox1": lambda: ts(T.ox[:, 4:7], T.ox[:, 0:3], 1.0, A.add, ["oxa", "oxb", "oxc"], ["ox1"]),
+            "xs": lambda: tt(T.xs[:], T.st[:].indirect(T.ox[:, 4 * t:4 * t + 3]), T.cap[:], A.max,
+                             ["st%d" % b for b in range(PAD)] + ["cap"] + oxk, ["xs"]),
+            "m1": lambda: tt(T.m1[:, 0:46], T.xs[:, 0:46], T.xs[:, 2:48], A.min, ["xs"], ["m1"]),
+            "c1": lambda: tt(T.c1[:, 0:46], T.xs[:, 2:48], T.xs[:, 0:46], A.is_lt, ["xs"], ["c1"]),
+            "m2": lambda: tt(T.m2[:, 0:42], T.m1[:, 0:42], T.m1[:, 4:46], A.min, ["m1"], ["m2"]),
+            "c2": lambda: tt(T.c2[:, 0:42], T.m1[:, 4:46], T.m1[:, 0:42], A.is_lt, ["m1"], ["c2"]),
+            "m8": lambda: tt(T.m8[:, 0:34], T.m2[:, 0:34], T.m2[:, 8:42], A.min, ["m2"], ["m8"]),
+            "c3": lambda: tt(T.z0[:, 2:128:4], T.m2[:, 8:40], T.m2[:, 0:32], A.is_lt, ["m2", "zk"], ["c3"]),
+            "z2": lambda: tt(T.z1[:, 2:184:4], T.c1[:, 0:46], T.a0[:, 0:46], A.add, ["c1", "a0"], ["z2"]),
+            "z0": lambda: tt(T.z1[:, 0:128:4], T.c1[:, 8:40], T.a0[:, 8:40], A.add, ["c1", "a0"], ["z0"]),
+            "z3": lambda: tt(T.z1[:, 3:128:4], T.c2[:, 0:32], T.z1[:, 18:146:4], A.mult, ["c2", "z2"], ["z3"]),
+            "z1": lambda: tt(T.z1[:, 1:128:4], T.c2[:, 8:40], T.z1[:, 50:178:4], A.mult, ["c2", "z2"], ["z1"]),
+            "a3": lambda: scan(T.a3[:], T.z0[:], T.z1[:, 0:128], A.mult, A.max, ["z0", "z1", "z2", "z3", "c3"], ["a3"]),
+            "x": lambda: tt(X, T.xs[:, 0:32], T.m8[:, 2:34], A.is_le, ["xs", "m8", "xy"], ["x"]),
+            "y": lambda: tt(Y, T.xs[:, 16:48], T.m8[:, 0:32], A.is_lt, ["xs", "m8", "xy"], ["y"]),
+            "lb0": lambda: scan(T.lb[:, 1:48], T.xy[:, 0:94:2], T.xy[:, 96:190:2], A.add, A.add, ["x", "y", "lbz"], ["lb0"]),
+            "lb1": lambda: scan(T.lb[:, 49:96], T.xy[:, 1:95:2], T.xy[:, 97:191:2], A.add, A.add, ["x", "y", "lbz"], ["lb1"]),
+            "mf": lambda: ts(T.mf[:], T.a3[:].indirect(T.om[:]), 1.0 / 1024, A.mult, ["a3", "om0", "om1"], ["mf"]),
+            "ma": lambda: act(T.ma[:], T.mf[:], ["mf"], ["ma"], None, 0.0, 1024.0),
+            "mt": lambda: turn(T.mt[:], T.mf[:], ["mf"], ["mt"]),
+            "wt": lambda: turn(T.wt[:], T.lb[:], ["lb0", "lb1"], ["wt"]),
+            "ub": lambda: scan(T.ub[:, 1:64], T.wt[:, 32:95], T.keep[:, 0:63], A.add, A.mult, ["wt", "keep"], ["ub"]),
+            "vu": lambda: tt(T.vu[:], T.wt[:, 0:64].indirect(T.o1[:]), T.mt[:], A.add, ["wt", "mt", "o1a", "o1b"], ["vu"]),
+            "vw": lambda: tt(T.vw[:], T.ub[:].indirect(T.o1[:]), T.vu[:], A.add, ["ub", "ub0", "vu", "o1a", "o1b"], ["vw"]),
+            "n16": lambda: ts(T.n16[:], T.vw[:], float(CAP), A.min, ["vw"], ["n16"]),
+            "pq": lambda: quant(T.pq[:], T.ps[:], T.pt[:],
+                                ["pt%d%d" % (i, b) for i in range(len(PARTS)) for b in range(4)] + ["ptp"], ["pq"]),
+            "hq": lambda: quant(T.hq[:], T.hs[:], T.ht[:], ["ht0", "ht1", "ht2", "ht3", "htp"], ["hq"]),
+            "vq": lambda: quant(T.vq[:], T.vs[:], T.vt[:], ["vt"], ["vq"]),
+            "va": lambda: turn(T.va[:], T.vw[:], ["vw"], ["va"]),
+            "na": lists_out,
+            "osc": scales,
+            "early": lambda: early(qk),
+        }
+        by_letter = {"f": held, "s": search, "r": count, "k": run_list, "d": candidates, "t": across, "e": least,
+                     "l": column, "p": pack, "W": product, "h": scaled, "D": unpack, "u": unpacked, "G": gather, "A": add,
+                     "B": both, "Q": state, "Y": result}
+        for name in names:
+            if name in step:
+                step[name]()
+                continue
+            engine = [name[-1]] if name[-1] in "sv" else []
+            rest = name[1:len(name) - len(engine)]
+            by_letter[name[0]](*([int(x) for x in (rest.split(".") if "." in rest else rest)] + engine))
+        lasting = set(qk) | {"qb", "q00", "q01", "vq", "o1b", "fsp", "ptp", "htp", "t1p", "ox1"}
+        stale.update(k for o in ops[first:] for k in o["w"] if k not in lasting)
+
+    stale.clear()
     op(None, None, (), ["sent"], sem=("sent", sent[0]))
     op("G", None, ["sent"] + stores)
     emit(ops, queues, T)

@@ -4,8 +4,8 @@ C, CAP, ROUNDS, PAD = 512, 112, 2, 12
 FW = 528
 BIG = 8.0e29
 CODE = "float8_e4m3fn_x4"
-LATE = 160
-MID = 320
+LATE = 192
+MID = 352
 
 
 def _sb(dtype, **widths):
@@ -14,31 +14,38 @@ def _sb(dtype, **widths):
 
 SCRATCH = {
     "psF": ("psum", [128, 2048], "float32"), "psR": ("psum", [128, 2048], "float32"),
-    **_sb("bfloat16", t0=4 * (C + PAD), t1=4 * (C + PAD), t2=4 * C, ut=512, vt=512, et=516, zt=1024, fs=4 * FW, pt=512,
-          ht=512, dh=512, tmp=4 * C),
-    **_sb(CODE, qa=C + PAD, qb=256, q2=C, uq=128, vq=128, eq=512, woc=512, w0c=512, w1c=512, pq=128, hq=128),
-    **_sb("uint8", sa=C + PAD, sb=256, s2=C, us=128, vs=128, es=512, wos=512, w0s=512, w1s=512, ps=128, hs=128),
+    **_sb("bfloat16", t0=4 * (C + PAD), t1=4 * (C + PAD), t2=4 * C, ut=512, vt=512, et=516, eh=516, zt=1024, fs=4 * FW,
+          pt=512, ht=512, dh=512, tmp=4 * C),
+    **_sb(CODE, qa=C + PAD, qb=256, q2=C, uq=128, vq=128, eq=512, woc=512, w0c=512, w1c=512, pq=128, hq0=128, hq1=128,
+          eg=512, pa0=768, pa1=768),
+    **_sb("uint8", sa=C + PAD, sb=256, s2=C, us=128, vs=128, es=512, wos=512, w0s=512, w1s=512, ps=128, hs0=128, hs1=128,
+          egs=512, pb0=768, pb1=768),
     **_sb("int32", pi=8),
-    **_sb("uint16", ox=8, om=2, o1=2, od=2, kap=64, e16=16, n16=32),
-    **_sb("float32", ys=C, pf=16, wrow=48, a0=48, cap=48, xrow=64, keep=64, r1=8, slot1=8, r2=224, slot2=224, st=768,
-          xs=48, m1=48, m2=48, m8=36, c1=48, c2=48, z0=128, z1=184, a3=128, ma=32, xy=192, lb=96, mf=32, mt=32, wt=96,
-          ub=64, kf=32, sg=448, f1=448, vu=32, vw=32, dd=224, dt2=224, em=8, va=32, na=32),
+    **_sb("uint16", ox=8, om=2, ol2=2, od=2, kap=64, e16=16, n16=32, o2=2, n2=64),
+    **_sb("float32", ys=C, pf=16, wrow=64, a0=64, cap=64, a1=64, tb=32, keep=64, r1=8, slot1=8, r2=224, slot2=224, st=768,
+          xs=64, pm=56, sm=56, rz=64, m8=48, ff=56, nf=56, lk=32, mfl=32, z0=96, z1=128, a3=96, ma=32, xy=192, lb=96,
+          mf=32, mt=32, wt=32, ub=32, kf=32, sg=448, f1=504, vw=32, dd=224, dt2=224, em=8, va=32, na=32, nn=32, nt=32),
 }
-POOL = {"V": 48, "S": 24, "P": 20, "G": 12, "D": 40}
+POOL = {"V": 48, "S": 28, "P": 20, "G": 12, "D": 36}
 SEMAPHORES = [k + str(i) for k in POOL for i in range(POOL[k])] + ["w0in", "w1in", "sent"]
 
-PARTS = [(0, 4), (4, 7)]
+JUMPS = [(9, -64, 0, 0), (14, -736, 0, 1), (2, -64, 1, 0), (11, -848, 1, 1), (4, -64, 2, 0), (9, -736, 2, 0), (13, -64, 2, 1)]
+BASES = [-64.0, 160.0, 272.0]
+PARTS = [(0, 3), (3, 7)]
 LISTS = [
-    "f0 o1b xs fsp ptp m1 c1 m2 c2 z2 z0 m8 c3 f1 z3 z1 x f2 y a3 lb1 lb0 mf wt f3 mt ub s3s vu s6v s5v s4v vw s2s r6 "
-    "s0s r5 r4 s1s k0 k1 d0 d1 t0 t1 e1 e0 e3 e2 e6 e5 e4 l0 p02s l1 p03s p01v p00v p10v n16 p13s p11v p12s pq W0 htp W1 "
-    "W3 h1v h0s W2 h2s h3v t1p hq ox1 D1 D0 D3 D2 u1s u0v u2v u3s G1.160.512 G3.160.512 G2.352.512 G1.0.160 G3.0.160 "
-    "G0.0.160 B0.160.512 B2.160.352 A1.160.512 A3.160.512 A2.352.512 B2.0.160 Q160.512 early A1.0.160 A3.0.160 A0.0.160 "
-    "Q0.160 vq",
-    "xs m1 f0 c1 m2 c2 z2 z0 m8 c3 z3 z1 y f1 x a3 lb1 lb0 f2 mf wt f3 mt ma ub s2s s3s vu s0s s5v s4v s6v s1s vw r5 r4 "
-    "r6 k0 k1 d0 d1 t0 t1 e3 e0 e1 e2 e6 e4 e5 l0 p02s l1 p01v p00v p03s p10v p11v p12s p13s va pq W0 na W1 h1v W2 h0s "
-    "W3 h3v h2s hq D0 D1 n16 u1s u0v D3 u3s D2 G1.0.256 G3.0.256 u2v G1.256.512 B0.0.384 G3.256.512 G2.256.384 "
-    "G0.384.512 B2.0.256 A1.0.256 A3.0.64 A3.64.256 A1.256.416 Q0.256 B2.384.512 A3.256.512 A2.256.384 Y0.256s "
-    "A1.416.512 A0.384.512 Q256.384 Q384.512 osc Y256.384v Y384.512v",
+    "F0 unit1 xs unit2 sm pm unit3 m8 nf ff F1 x0 y1 y0 x1 F2 c3 b0 b1 f0 lr lf wt f1 a3 f2 lk ub mfl s2s s0s s1s s6v mt r6 "
+    "F3 k0 vw s4s s3s s5s k1 d0 d1 f3 t0 t1 e1 e2 e0 e4 e3 e6 e5 l0 l1 va p01v p03s p00v p10v p02s p13s p12s nns p11v n20 "
+    "pq W1 h1s half3 W0 half0 half1 nt h0v W2 h2v W3 n16 n21 ox1 h3s hq half2 D0 D1 S1s D3 P1 u0v D2 S0s H0 u2s u1s u3s H2 "
+    "P0 J00 J10 B0.192.512 G2.192.512 B1.192.512 H1 J01 A2.192.512 G3.192.416 G3.416.512 J12 C0.0.192s J11 A3.288.384 "
+    "A3.192.288 C1.0.192s J02 H3 J13 A3.384.512 Q192.512 J03 C2.0.192s early C3.0.192s vq Q0.192",
+    "xs sm pm nf m8 c3 F0 F1 ff f0 y1 x0 y0 f1 x1 lr b0 F2 b1 lf f2 wt a3 lk F3 ub mfl s1s s6v s0s s5v mt r6 r5 s2s s3s vw "
+    "s4s k0 k1 d0 d1 mf t0 t1 ma e0 e1 e2 e4 f3 e6 e5 e3 l0 p03s n16 va l1 p02s p12s p00v p01v p10v p11v p13s na n20 pq W1 "
+    "W0 nn W2 W3 nt h1v h0s h2s h3v hq D0 n21 D3 D1 P0 S0s D2 u0s H0 J00 P1 S1s u2s J10 u1s u3s C0.0.192s H2 J02 H1 J11 "
+    "B0.192.512 J12 B2.192.512 J01 H3 J13 J03 B1.192.512 B3.384.512 B3.192.384 C2.0.192s C1.0.192s C3.0.192s Q384.512 "
+    "O384.512s Y384.512s Q0.192 O0.192v Q192.384 O192.384s Y0.192v Z384.512s Z0.192v osc Y192.384v Z192.384v",
+    "pi0 zt row2 row1 bits3 bits2 bits1 t0p zk pf et sign4 qh q8 xyz wrow qs om0 sign5 rz sign3 base0 qx0 sign0 i16 ol1 ol0 "
+    "sign2 base2 q6 jump0 uq base1 a0 par one hone sign1 qx1 t1p capf jump2 hcap jump4 kfz first layers cap fsp sign6 jump1 "
+    "qx2 xrow jump5 cape om1 ub0 ptp slot2 f1p od oxd capd eh o2 lbz jump3 jump6 htp unit0 slot1",
 ]
 
 
@@ -63,7 +70,7 @@ def emit(ops, queues, T):
         deps.discard(i)
         have = known.setdefault(q, set())
         if o["adds"]:
-            have.update(writer[k] for k in o["w"])
+            have.update(writer[k] for k in o["w"] + o["r"] if k.startswith("ps") or k[0] == "H")
         waits = []
         for j in sorted(deps, reverse=True):
             if j in have:
@@ -74,7 +81,7 @@ def emit(ops, queues, T):
             for m in who:
                 have |= done[m]
                 signal.add(m)
-        o["waits"] = waits
+        o["waits"] = waits[::-1]
         o["have"] = set(have)
         done.append(set(have) | {i})
         for k in o["r"]:
@@ -131,23 +138,23 @@ def rank_program(g, core, T, topo):
     def dma(q, out, in_, r, w, grp=None):
         op(q, lambda: queues[q].dma_start(out, in_), r, w, grp, True)
 
-    def tt(out, a, b, alu, r, w, grp=None):
-        op("V", lambda: v.tensor_tensor(out, a, b, alu), r, w, grp)
+    def tt(out, a, b, alu, r, w):
+        op("V", lambda: v.tensor_tensor(out, a, b, alu), r, w)
 
-    def ts(out, a, s1, o0, r, w, s2=None, o1=None, grp=None):
+    def ts(out, a, s1, o0, r, w, s2=None, o1=None):
         if o1 is None:
-            op("V", lambda: v.tensor_scalar(out, a, s1, None, o0), r, w, grp)
+            op("V", lambda: v.tensor_scalar(out, a, s1, None, o0), r, w)
         else:
-            op("V", lambda: v.tensor_scalar(out, a, s1, s2, o0, o1), r, w, grp)
+            op("V", lambda: v.tensor_scalar(out, a, s1, s2, o0, o1), r, w)
 
-    def cp(out, a, r, w, grp=None):
-        op("V", lambda: v.tensor_copy(out, a), r, w, grp)
+    def cp(out, a, r, w):
+        op("V", lambda: v.tensor_copy(out, a), r, w)
 
-    def fill(ap, c, w, grp=None, r=()):
-        op("V", lambda: v.memset(ap, c), r, w, grp)
+    def fill(ap, c, w):
+        op("V", lambda: v.memset(ap, c), (), w)
 
-    def scan(out, d0, d1, o0, o1, r, w, grp=None):
-        op("V", lambda: v.tensor_tensor_scan(out, d0, d1, 0.0, o0, o1), r, w, grp)
+    def scan(out, d0, d1, o0, o1, r, w):
+        op("V", lambda: v.tensor_tensor_scan(out, d0, d1, 0.0, o0, o1), r, w)
 
     def turn(out, a, r, w, grp=None):
         op("V", lambda: v.transpose(out, a), r, w, grp)
@@ -155,21 +162,24 @@ def rank_program(g, core, T, topo):
     def reduce(out, a, alu, r, w, size=False):
         op("V", lambda: v.tensor_reduce(out, a, AxisListType.X, alu, apply_absolute_value=size), r, w)
 
-    def act(out, a, r, w, func=None, bias=0.0, scale=1.0, grp=None, total=None):
+    def act(out, a, r, w, func=None, bias=0.0, scale=1.0, total=None):
         op("S", lambda: s.activation(out, a, F.Copy if func is None else func, bias=bias, scale=scale, accum_out=total),
-           r, w, grp)
+           r, w)
 
-    def quant(qc, qs, tile, r, w, grp=None):
-        op("V", lambda: v.quantize_mx(qc, qs, tile), r, w, grp)
+    def move(out, a, r, w):
+        op("S", lambda: s.activation(out, a, F.Copy), r, w)
+
+    def quant(qc, qs, tile, r, w):
+        op("V", lambda: v.quantize_mx(qc, qs, tile), r, w)
 
     def mm(out, wc, ws, xc, xs, r, w, grp=None, start=True, stop=True):
         op("P", lambda: pe.matmul_mx(out, wc, ws, xc, xs, start, stop), r, w, grp, adds=not start)
 
-    def iota(out, pattern, base, mult, w, flt=True, grp=None):
+    def iota(out, pattern, base, mult, w, flt=True):
         if flt:
-            op("G", lambda: g.iota(out, pattern, base, mult, allow_small_or_imprecise_dtypes=True), (), w, grp)
+            op("G", lambda: g.iota(out, pattern, base, mult, allow_small_or_imprecise_dtypes=True), (), w)
         else:
-            op("G", lambda: g.iota(out, pattern, base, mult), (), w, grp)
+            op("G", lambda: g.iota(out, pattern, base, mult), (), w)
 
     sent = [0]
 
@@ -211,107 +221,163 @@ def rank_program(g, core, T, topo):
     dma("Y", T.wos[:], T.ws[:], (), ["wos"])
     dma("Y", codes(T.woc, 0, 512), T.wc[:], (), ["woc"])
 
-    fill(T.et[:], 0.0, ["et"])
-    iota(T.pi[:, 0:1], [[0, 1]], 0, 1, ["pi0"], False)
-    one = T.et[:, 3:515:4]
-    op("G", lambda: g.affine_select(one, one, [[-1, 128]], A.not_equal, 1.0, 0, 1), ["et"], ["et"])
-    iota(T.wrow[:], [[1, 24], [0, 2]], 0, 0, ["wrow"])
-    iota(T.z0[:], [[0, 64], [1, 2]], 0, 0, ["zk"])
-    iota(T.xrow[:], [[1, 64]], -31, 0, ["xrow"])
-    iota(T.r1[:], [[16, 8]], 0, 0, ["r1"])
-    iota(T.r2[:], [[16, 7], [1000, 2], [1, 16]], 0, 0, ["r2"])
-    fill(T.t0[:, 4 * C:], 0.0, ["t0p"])
-    fill(T.zt[:, 0:4 * LATE], 0.0, ["zt"])
-    for k, m in enumerate((15, 16, 1)):
-        ts(T.pi[:, k + 1:k + 2], T.pi[:, 0:1], m, A.bitwise_and, ["pi0"], ["pi%d" % (k + 1)], grp="pi")
-    fill(T.xy[:, 32:192], 0.0, ["xy"])
-    cp(T.pf[:, 1:4], T.pi[:, 1:4], ["pi1", "pi2", "pi3"], ["pf"])
-    fill(T.lb[:, 0:49:48], 0.0, ["lbz"], "y")
-    fill(T.ub[:, 0:1], 0.0, ["ub0"], "y")
-    fill(T.kf[:], 0.0, ["kfz"], "y")
     qc, hc, bc = T.pf[:, 1:2], T.pf[:, 2:3], T.pf[:, 3:4]
-    ts(T.pf[:, 4:5], qc, hc, A.add, ["pf"], ["i16"], 16.0, A.mult, grp="c")
-    ts(T.pf[:, 5:6], bc, -0.5, A.mult, ["pf"], ["odd"], qc, A.add, grp="c")
-    ts(T.pf[:, 6:7], qc, 8.0, A.is_ge, ["pf"], ["far"], -23.0, A.mult, grp="c")
-    ts(T.pf[:, 7:8], hc, -62.5, A.mult, ["pf"], ["par"], grp="c")
-    ts(T.pf[:, 8:9], hc, 0.125, A.mult, ["pf"], ["sgn"], -1.0, A.add, grp="c")
-    ts(T.pf[:, 9:10], qc, 0.5, A.add, ["pf"], ["qh"], grp="c")
+    one = T.et[:, 3:515:4]
 
     def unit(b):
         quant(T.eq[:, 128 * b:128 * b + 128], T.es[:, 128 * b:128 * b + 128], T.et[:, 3 - b:515 - b], ["et"], ["eq%d" % b])
 
-    unit(0)
-    unit(1)
-    quant(T.qa[:, 0:LATE], T.sa[:, 0:LATE], T.zt[:, 0:4 * LATE], ["zt"], ["qs"])
-    act(T.a0[:], T.wrow[:], ["wrow", "i16"], ["a0"], F.Identity, T.pf[:, 4:5])
-    act(T.slot1[:], T.r1[:], ["r1", "qh"], ["slot1"], F.Identity, T.pf[:, 9:10])
-    act(T.slot2[:], T.r2[:], ["r2", "par"], ["slot2"], F.Identity, T.pf[:, 7:8])
+    def half(b):
+        quant(T.eg[:, 128 * b:128 * b + 128], T.egs[:, 128 * b:128 * b + 128], T.eh[:, 3 - b:515 - b], ["eh"], ["eg%d" % b])
 
-    send(T.w0s[:], T.wos[:], d0, narrow(core), "w0in", ["wos"])
-    send(codes(T.w0c, 0, 512), codes(T.woc, 0, 512), d0, narrow(core), "w0in", ["woc"])
-    if not handed_on((rank - 1) % n_ranks):
-        send(codes(T.w1c, 0, 512), codes(T.woc, 0, 512), d1, narrow(core), "w1in", ["woc", "w0"])
-        send(T.w1s[:], T.wos[:], d1, narrow(core), "w1in", ["wos", "w0"])
-    if handed_on(rank):
-        send(codes(T.w1c, 0, 512), codes(T.w0c, 0, 512), d0, wide(core, d0), "w1in", ["w0"])
-        send(T.w1s[:], T.w0s[:], d0, wide(core, d0), "w1in", ["w0"])
+    def bits(k):
+        ts(T.pi[:, k:k + 1], T.pi[:, 0:1], (15, 16, 1)[k - 1], A.bitwise_and, ["pi0"], ["pi%d" % k])
+
+    def layers():
+        send(T.w0s[:], T.wos[:], d0, narrow(core), "w0in", ["wos"])
+        send(codes(T.w0c, 0, 512), codes(T.woc, 0, 512), d0, narrow(core), "w0in", ["woc"])
+        if not handed_on((rank - 1) % n_ranks):
+            send(codes(T.w1c, 0, 512), codes(T.woc, 0, 512), d1, narrow(core), "w1in", ["woc", "w0"])
+            send(T.w1s[:], T.wos[:], d1, narrow(core), "w1in", ["wos", "w0"])
+        if handed_on(rank):
+            send(codes(T.w1c, 0, 512), codes(T.w0c, 0, 512), d0, wide(core, d0), "w1in", ["w0"])
+            send(T.w1s[:], T.w0s[:], d0, wide(core, d0), "w1in", ["w0"])
 
     def early(keys):
         mm(T.psR[:, 0:512], T.uq[:], T.us[:], T.qa[:, 0:C], T.sa[:, 0:C], ["uq", "qs"] + keys, ["psR0"], stop=False)
         mm(T.psR[:, 512:1024], T.uq[:], T.us[:], T.qa[:, PAD:C + PAD], T.sa[:, PAD:C + PAD], ["uq", "qs"] + keys, ["psR1"],
            stop=False)
 
-    quant(T.qa[:, MID:], T.sa[:, MID:], T.t0[:, 4 * MID:], ["t0a", "t0p"], ["q00"])
-    quant(T.uq[:], T.us[:], T.ut[:], ["ut"], ["uq"])
-    quant(T.qa[:, LATE:MID], T.sa[:, LATE:MID], T.t0[:, 4 * LATE:4 * MID], ["t0b"], ["q01"])
-    early(["q00", "q01"])
-    unit(2)
-    unit(3)
-    quant(T.qb[:, 0:LATE], T.sb[:, 0:LATE], T.t0[:, 0:4 * LATE], ["t0c"], ["qb"])
-    odd = T.pf[:, 5:6]
-    ts(T.ox[:, 0:1], odd, 32.0, A.mult, ["odd"], ["oxa"], grp="ox")
-    ts(T.ox[:, 2:3], odd, 9.0, A.add, ["odd"], ["oxc"], 32.0, A.mult, grp="ox")
-    ts(T.pf[:, 10:11], odd, T.pf[:, 6:7], A.add, ["odd", "far"], ["oxf"], 16.0, A.add)
-    ts(T.cap[:], T.a0[:], 0.5 - C, A.add, ["a0"], ["cap"], BIG, A.mult)
-    ts(T.keep[:], T.xrow[:], T.pf[:, 8:9], A.mult, ["xrow", "sgn"], ["keep"], 0.0, A.is_gt)
-    ts(T.om[:, 0:1], qc, 8.0, A.mult, ["pf"], ["om0"], 3.0, A.add, grp="v")
-    ts(T.om[:, 1:2], qc, 8.0, A.mult, ["pf"], ["om1"], 7.0, A.add, grp="v")
-    ts(T.ox[:, 1:2], T.pf[:, 10:11], 32.0, A.mult, ["oxf"], ["oxb"])
-    ts(T.o1[:, 0:1], hc, 2.0, A.mult, ["pf"], ["o1a"], qc, A.add, grp="u")
-    ts(T.od[:, 0:1], qc, bc, A.subtract, ["pf"], ["od"], 0.5, A.mult, grp="u")
+    def level(ap, n, c, w, r=()):
+        act(ap, T.r2[:, 0:n], ["r2"] + list(r), w, None, c, 0.0)
+
+    def sign(k):
+        act(T.tb[:, 8 + k:9 + k], qc, ["pf"], ["tj%d" % k], F.Sign, 0.5 - JUMPS[k][0])
+
+    def jump(k):
+        a, z, c, end = JUMPS[k]
+        on = k and JUMPS[k - 1][2] == c
+        ts(T.ox[:, c:c + 1] if end else T.tb[:, 16 + k:17 + k], T.tb[:, 8 + k:9 + k], 0.5 * z, A.mult,
+           ["tj%d" % k, "tk%d" % (k - 1) if on else "tc%d" % c], ["ox" + "abc"[c] if end else "tk%d" % k],
+           T.tb[:, 15 + k:16 + k] if on else T.tb[:, 4 + c:5 + c], A.add)
+
+    def base(c):
+        act(T.tb[:, 4 + c:5 + c], qc, ["pf"], ["tc%d" % c], None, BASES[c] + sum(0.5 * z for a, z, k, end in JUMPS if k == c),
+            64.0)
+
+    once = {
+        "et": lambda: fill(T.et[:], 0.0, ["et0"]),
+        "pi0": lambda: iota(T.pi[:, 0:1], [[0, 1]], 0, 1, ["pi0"], False),
+        "one": lambda: op("G", lambda: g.affine_select(one, one, [[-1, 128]], A.not_equal, 1.0, 0, 1), ["et0"], ["et"]),
+        "wrow": lambda: iota(T.wrow[:, 0:54], [[0, 2], [8, 3], [1, 9]], -1, 0, ["wrow"]),
+        "zk": lambda: level(T.z0[:], 96, 0.0, ["zk"]),
+        "xrow": lambda: level(T.keep[:, 0:32], 32, 1.0, ["keep"]),
+        "row1": lambda: iota(T.r1[:], [[16, 8]], 0, 0, ["r1"]),
+        "row2": lambda: iota(T.r2[:], [[16, 7], [1000, 2], [1, 16]], 0, 0, ["r2"]),
+        "layers": layers,
+        "t0p": lambda: fill(T.t0[:, 4 * C:], 0.0, ["t0p"]),
+        "zt": lambda: fill(T.zt[:, 0:4 * LATE], 0.0, ["zt"]),
+        "xyz": lambda: level(T.xy[:], 192, 0.0, ["xy"]),
+        "rz": lambda: op("G", lambda: g.affine_select(T.rz[:, 0:63], T.z0[:, 0:63], [[0, 7], [1, 9]], A.not_equal,
+                                                      BIG * 1.125, 0, 0), ["zk"], ["rz"]),
+        "pf": lambda: cp(T.pf[:, 1:4], T.pi[:, 1:4], ["pi1", "pi2", "pi3"], ["pf"]),
+        "lbz": lambda: level(T.lb[:, 0:70:69], 2, 0.0, ["lbz"]),
+        "ub0": lambda: level(T.ub[:, 0:1], 1, 0.0, ["ub0"]),
+        "kfz": lambda: level(T.kf[:], 32, 0.0, ["kfz"]),
+        "f1p": lambda: level(T.f1[:, 32:504:72], 7, -32.0, ["f1p"]),
+        "i16": lambda: ts(T.pf[:, 4:5], qc, hc, A.add, ["pf"], ["i16"], 1.0 / 64, A.mult),
+        "par": lambda: act(T.pf[:, 7:8], hc, ["pf"], ["par"], None, 0.0, -62.5),
+        "qh": lambda: act(T.pf[:, 9:10], qc, ["pf"], ["qh"], None, 0.5),
+        "hone": lambda: act(T.pf[:, 11:12], hc, ["pf"], ["h1"], None, 0.0, 1.0 / 16),
+        "hcap": lambda: act(T.pf[:, 12:13], hc, ["pf"], ["h7"], None, 0.0, CAP / 16.0),
+        "eh": lambda: act(T.eh[:], T.et[:], ["et", "h1"], ["eh"], F.Identity, 0.0, T.pf[:, 11:12]),
+        "qs": lambda: quant(T.qa[:, 0:LATE], T.sa[:, 0:LATE], T.zt[:, 0:4 * LATE], ["zt"], ["qs"]),
+        "a0": lambda: act(T.a0[:, 0:54], T.wrow[:, 0:54], ["wrow", "i16"], ["a0"], F.Identity, T.pf[:, 4:5], 1.0 / 1024),
+        "slot1": lambda: act(T.slot1[:], T.r1[:], ["r1", "qh"], ["slot1"], F.Identity, T.pf[:, 9:10]),
+        "slot2": lambda: act(T.slot2[:], T.r2[:], ["r2", "par"], ["slot2"], F.Identity, T.pf[:, 7:8]),
+        "qx0": lambda: quant(T.qa[:, MID:], T.sa[:, MID:], T.t0[:, 4 * MID:], ["t0a", "t0p"], ["q00"]),
+        "uq": lambda: quant(T.uq[:], T.us[:], T.ut[:], ["ut"], ["uq"]),
+        "qx1": lambda: quant(T.qa[:, LATE:MID], T.sa[:, LATE:MID], T.t0[:, 4 * LATE:4 * MID], ["t0b"], ["q0"]),
+        "first": lambda: early(["q0", "q00"]),
+        "qx2": lambda: quant(T.qb[:, 0:LATE], T.sb[:, 0:LATE], T.t0[:, 0:4 * LATE], ["t0c"], ["qb"]),
+        "capf": lambda: ts(T.a1[:, 0:54], T.a0[:, 0:54], 0.5, A.is_ge, ["a0"], ["capf"], BIG, A.mult),
+        "cap": lambda: act(T.cap[:, 0:54], T.a1[:, 0:54], ["capf"], ["cap0"], None, -0.5 * BIG),
+        "capd": lambda: level(T.cap[:, 0:55:9], 7, 0.5 * BIG, ["cap1"], ["cap0"]),
+        "cape": lambda: level(T.cap[:, 55:64], 9, 0.5 * BIG, ["cap2"]),
+        "q6": lambda: act(T.pf[:, 14:15], qc, ["pf"], ["q6"], None, 6.75),
+        "oxd": lambda: ts(T.ox[:, 3:4], T.pf[:, 14:15], 11.75, A.min, ["q6"], ["oxd"], 64.0, A.mult),
+        "q8": lambda: ts(T.pf[:, 13:14], qc, 8.0, A.is_ge, ["pf"], ["q8"], qc, A.add),
+        "om0": lambda: ts(T.om[:, 0:1], T.pf[:, 13:14], 2.0, A.mult, ["q8"], ["om0"], 1.0, A.add),
+        "om1": lambda: ts(T.om[:, 1:2], T.pf[:, 13:14], 2.0, A.mult, ["q8"], ["om1"], 55.0, A.add),
+        "ol0": lambda: cp(T.ol2[:, 0:1], T.pf[:, 13:14], ["q8"], ["ol0"]),
+        "ol1": lambda: ts(T.ol2[:, 1:2], T.pf[:, 13:14], -1.0, A.mult, ["q8"], ["ol1"], 69.0, A.add),
+        "od": lambda: ts(T.od[:, 0:1], qc, bc, A.subtract, ["pf"], ["od"], 0.5, A.mult),
+        "o2": lambda: ts(T.o2[:], T.keep[:, 0:2], 15.0, A.add, ["keep", "pf"], ["o2"], qc, A.add),
+        "fsp": lambda: level(T.fs[:, C:4 * FW:FW], 4, 0.0, ["fsp"]),
+        "ptp": lambda: level(T.pt[:, 4 * CAP:], 64, 0.0, ["ptp"]),
+        "htp": lambda: level(T.ht[:, 4 * CAP:], 64, 0.0, ["htp"]),
+        "t1p": lambda: level(T.t1[:, 4 * C:], 48, 0.0, ["t1p"]),
+        "ox1": lambda: ts(T.ox[:, 4:8], T.ox[:, 0:4], 1.0, A.add, ["oxa", "oxb", "oxc", "oxd"], ["ox1"]),
+        "vq": lambda: quant(T.vq[:], T.vs[:], T.vt[:], ["vt"], ["vq"]),
+    }
+    for b in range(7):
+        once["unit%d" % b] = lambda b=b: unit(b)
+        once["half%d" % b] = lambda b=b: half(b)
+        once["bits%d" % b] = lambda b=b: bits(b)
+        once["base%d" % b] = lambda b=b: base(b)
+        once["sign%d" % b] = lambda b=b: sign(b)
+        once["jump%d" % b] = lambda b=b: jump(b)
+    for name in LISTS[ROUNDS].split():
+        once[name]()
 
     layer = [(T.w0c, T.w0s), (T.w1c, T.w1s)]
     part_of = {c: i for i, (c0, c1) in enumerate(PARTS) for c in range(c0, c1)}
     stores = []
     wd = CAP + 2
 
-    def runs(name, c0, c1, width=32):
+    def runs(name, c0, c1, width=16):
         return ["%s_%d" % (name, k) for k in range(c0 // width, c1 // width)]
 
-    qk = ["q00", "q01"]
+    qk = ["q0", "q00"]
+    kept = {"qb", "q0", "q00", "zk"}
     for t in range(ROUNDS):
         tn, qn, sn = [(T.t1, T.qa, T.sa), (T.t2, T.q2, T.s2)][t]
         wq, wsc = layer[t]
+        hq, hs, pa, pb = [(T.hq0, T.hs0, T.pa0, T.pb0), (T.hq1, T.hs1, T.pa1, T.pb1)][t]
         last = t == ROUNDS - 1
         first = len(ops)
         names = LISTS[t].split()
         mm(T.psR[:, 0:LATE], T.uq[:], T.us[:], T.qb[:, 0:LATE], T.sb[:, 0:LATE], ["qb"], ["psR0"], "s%d" % t, False)
         mm(T.psR[:, 512:512 + LATE - PAD], T.uq[:], T.us[:], T.qb[:, PAD:LATE], T.sb[:, PAD:LATE], ["qb"], ["psR1"],
            "s%d" % t, False)
-        for b in range(4):
+        for b in range(PAD):
+            turn(T.st[:, 64 * b:64 * b + 64], T.psR[:, b:1024:16], ["psR0", "psR1"], ["st%d" % b], "tr%d" % t)
+        if t == 0:
+            dma("Y", T.vt[:], T.v[:], ["st0"], ["vt"])
+
+        def hold(b, qk=qk):
             e, es = T.eq[:, 128 * b:128 * b + 128], T.es[:, 128 * b:128 * b + 128]
             mm(T.psF[:, 512 * b:512 * b + 512], e, es, T.qa[:, 0:C], T.sa[:, 0:C], ["eq%d" % b, "qs"] + qk, ["psF%d" % b],
                stop=False)
             mm(T.psF[:, 512 * b:512 * b + LATE], e, es, T.qb[:, 0:LATE], T.sb[:, 0:LATE], ["qb"], ["psF%d" % b],
                start=False)
-        for b in range(PAD):
-            turn(T.st[:, 64 * b:64 * b + 64], T.psR[:, b:1024:16], ["psR0", "psR1"], ["st%d" % b], "tr%d" % t)
-        if t == 0:
-            dma("Y", T.vt[:], T.v[:], ["st0"], ["vt"])
-        qk = runs("q", 0 if last else LATE, C)
+
+        qk = runs("q%d" % (t + 1), 0 if last else LATE, C)
 
         def held(b):
             act(T.fs[:, FW * b:FW * b + C], T.psF[:, 512 * b:512 * b + 512], ["psF%d" % b], ["fs%d" % b])
+
+        def leaves(h):
+            tt(T.xy[:, 48 * h:48 * h + 17], T.xs[:, 27 * h + 1:27 * h + 18], T.m8[:, 27 * h + 2:27 * h + 19], A.is_le,
+               ["xs", "m8", "xy"], ["x%d" % h])
+
+        def enters(h):
+            tt(T.xy[:, 96 + 48 * h:113 + 48 * h], T.xs[:, 27 * h + 10:27 * h + 27], T.m8[:, 27 * h + 1:27 * h + 18], A.is_lt,
+               ["xs", "m8", "xy"], ["y%d" % h])
+
+        def sums(h):
+            scan(T.lb[:, 68:34:-1] if h else T.lb[:, 1:35], T.xy[:, 48 * h:48 * h + 34], T.xy[:, 96 + 48 * h:130 + 48 * h],
+                 A.add, A.add, ["x%d" % h, "y%d" % h, "lbz"], ["lb%d" % h])
 
         def kf(c):
             i = part_of[c]
@@ -320,21 +386,19 @@ def rank_program(g, core, T, topo):
 
         def search(c, e):
             if e == "v":
-                ts(T.f1[:, 64 * c:64 * c + 64], T.ub[:], T.slot1[:, c:c + 1], A.is_lt, ["ub", "ub0", "slot1"], ["f1%d" % c],
+                ts(T.f1[:, 72 * c:72 * c + 32], T.ub[:], T.slot1[:, c:c + 1], A.is_lt, ["ub", "ub0", "slot1"], ["f1%d" % c],
                    2.0, A.mult)
             else:
-                act(T.sg[:, 64 * c:64 * c + 64], T.ub[:], ["ub", "ub0", "slot1", "kfz"], ["kf%d" % c, "sg%d" % c], F.Sign,
-                    T.slot1[:, c:c + 1], -1.0, total=kf(c))
+                act(T.sg[:, 64 * c:64 * c + 32], T.ub[:], ["ub", "ub0", "slot1", "kfz"], ["kf%d" % c, "sg%d" % c], F.Sign,
+                    T.slot1[:, c:c + 1], -1.0, kf(c))
 
         def count(c):
-            reduce(kf(c), T.f1[:, 64 * c:64 * c + 64], A.add, ["f1%d" % c, "kfz"], ["kf%d" % c])
+            reduce(kf(c), T.f1[:, 72 * c:72 * c + 33], A.add, ["f1%d" % c, "kfz", "f1p"], ["kf%d" % c])
 
         def run_list(i):
             c0, c1 = PARTS[i]
-            on_v = ["s%dv" % c in names for c in range(c0, c1)]
-            assert all(on_v) or not any(on_v)
             ts(T.kap[:, 16 * i:16 * i + 16], T.kf[:, 8 * i:8 * i + 8].indirect(T.od[:, 0:1]), 0.5, A.mult,
-               ["od"] + ["kf%d" % c for c in range(c0, c1)], ["kap%d" % i], -33.0 if on_v[0] else -1.0, A.add)
+               ["od"] + ["kf%d" % c for c in range(c0, c1)], ["kap%d" % i], 15.0, A.add)
 
         def candidates(i):
             c0, c1 = PARTS[i]
@@ -361,7 +425,7 @@ def rank_program(g, core, T, topo):
         def pack(i, b, e):
             c0, c1 = PARTS[i]
             (cp if e == "v" else act)(T.pt[:, 64 * c0 + b:64 * c1:4], T.fs[:, FW * b:FW * b + C + 1].indirect(listed(i)),
-                                      ["fs%d" % b, "fsp", "e16%d" % i], ["pt%d%d" % (i, b)], grp="p%d%s" % (t, e))
+                                      ["fs%d" % b, "fsp", "e16%d" % i], ["pt%d%d" % (i, b)])
 
         def product(b):
             mm(T.psR[:, 512 * b:512 * b + 128], wq[:, 128 * b:128 * b + 128], wsc[:, 128 * b:128 * b + 128],
@@ -370,13 +434,13 @@ def rank_program(g, core, T, topo):
         def scaled(b, e):
             src = T.psR[:, 512 * b:512 * b + CAP]
             if e == "v":
-                ts(T.ht[:, b:4 * CAP:4], src, 0.03125, A.mult, ["psR%d" % b, "R%d" % b], ["ht%d" % b], grp="hv%d" % t)
+                ts(T.ht[:, b:4 * CAP:4], src, 0.03125, A.mult, ["psR%d" % b, "R%d" % b], ["ht%d" % b])
             else:
-                act(T.ht[:, b:4 * CAP:4], src, ["psR%d" % b, "R%d" % b], ["ht%d" % b], None, 0.0, 0.03125, grp="hs%d" % t)
+                act(T.ht[:, b:4 * CAP:4], src, ["psR%d" % b, "R%d" % b], ["ht%d" % b], None, 0.0, 0.03125)
 
         def unpack(b):
             mm(T.psR[:, 512 * b:512 * b + 128], T.eq[:, 128 * b:128 * b + 128], T.es[:, 128 * b:128 * b + 128],
-               T.hq[:], T.hs[:], ["eq%d" % b, "hq"], ["psR%d" % b, "D%d" % b])
+               hq[:], hs[:], ["eq%d" % b, "hq"], ["psR%d" % b, "D%d" % b])
 
         def unpacked(b, e):
             (act if e == "s" else cp)(T.dh[:, 128 * b:128 * b + wd], T.psR[:, 512 * b:512 * b + wd],
@@ -396,35 +460,63 @@ def rank_program(g, core, T, topo):
             tt(tn[:, 4 * c0 + b:4 * c1:4], window(b, c0, c1), T.fs[:, FW * b + c0:FW * b + c1], A.add,
                ["dh%d" % b, "n16", "fs%d" % b], runs("t%d%d" % (t + 1, b), c0, c1))
 
+        def pick(h):
+            cp(pa[:, 384 * h:384 * h + LATE].bitcast(dt.uint32),
+               hq[:].bitcast(dt.uint32).indirect(T.n2[:, 32 * h:32 * h + LATE // 16]), ["hq", "n2%d" % h], ["pa%d" % h])
+
+        def pick_scales(h, e):
+            (move if e == "s" else cp)(pb[:, 384 * h:384 * h + LATE], hs[:].indirect(T.n2[:, 32 * h:32 * h + LATE // 16]),
+                                       ["hq", "n2%d" % h], ["pb%d" % h])
+
+        def opened(b):
+            mm(T.psR[:, 512 * b:512 * b + LATE], T.eq[:, 128 * b:128 * b + 128], T.es[:, 128 * b:128 * b + 128],
+               T.qb[:, 0:LATE], T.sb[:, 0:LATE], ["dh%d" % b, "qb"], ["psR%d" % b, "H%d" % b], stop=False)
+
+        def joined(h, b):
+            e, es, key = [(T.eq, T.es, "eq%d"), (T.eg, T.egs, "eg%d")][h]
+            mm(T.psR[:, 512 * b:512 * b + LATE], e[:, 128 * b:128 * b + 128], es[:, 128 * b:128 * b + 128],
+               pa[:, 384 * h:384 * h + LATE], pb[:, 384 * h:384 * h + LATE],
+               [key % b, "pa%d" % h, "pb%d" % h, "H%d" % b], ["psR%d" % b, "J%d%d" % (h, b)], start=False,
+               stop=names.index("J%d%d" % (1 - h, b)) < names.index("J%d%d" % (h, b)))
+
+        def cast(b, c0, c1, e):
+            (act if e == "s" else cp)(tn[:, 4 * c0 + b:4 * c1:4], T.psR[:, 512 * b + c0:512 * b + c1],
+                                      ["psR%d" % b, "J0%d" % b, "J1%d" % b], runs("t%d%d" % (t + 1, b), c0, c1))
+
         def state(c0, c1):
             rd = [k for b in range(4) for k in runs("t%d%d" % (t + 1, b), c0, c1)]
             if c0 == 0 and not last:
                 assert c1 == LATE
                 quant(T.qb[:, 0:c1], T.sb[:, 0:c1], tn[:, 0:4 * c1], rd, ["qb"])
                 return
-            keys = runs("q", c0, c1)
+            keys = runs("q%d" % (t + 1), c0, c1)
             end = c1
             if c1 == C and not last:
                 end += PAD
                 rd.append("t1p")
-            quant(qn[:, c0:end], sn[:, c0:end], tn[:, 4 * c0:4 * end], rd, keys + ([] if last else ["q00", "q01"]))
+            quant(qn[:, c0:end], sn[:, c0:end], tn[:, 4 * c0:4 * end], rd, keys + ([] if last else ["q0", "q00"]))
             if last:
                 k = c0 // 128
-                mm(T.psR[:, 512 * k:512 * k + c1 - c0], T.vq[:], T.vs[:], qn[:, c0:c1], sn[:, c0:c1], ["vq"] + keys,
-                   ["psR%d" % k, "Y%d" % k])
-                dma("Y", T.oc[:, 4 * c0:4 * c1], codes(qn, c0, c1), keys, ["oc%d" % k])
-                stores.append("oc%d" % k)
+                mm(T.psR[:, 512 * k:512 * k + c1 - c0], T.vq[:], T.vs[:], qn[:, c0:c1], sn[:, c0:c1],
+                   ["vq"] + keys + runs("t2%d" % k, 0, LATE), ["psR%d" % k, "Y%d" % k])
 
         def result(c0, c1, e):
             k = c0 // 128
             (cp if e == "v" else act)(T.ys[:, c0:c1], T.psR[:, 512 * k:512 * k + c1 - c0], ["psR%d" % k, "Y%d" % k],
-                                      ["ys%d" % k])
-            dma("S" if c1 == C else "Y", T.y[:, c0:c1], T.ys[:, c0:c1], ["ys%d" % k], ["y%d" % k])
-            stores.append("y%d" % k)
+                                      runs("ys", c0, c1))
+
+        def codes_out(c0, c1, e):
+            dma("S" if e == "s" else "Y", T.oc[:, 4 * c0:4 * c1], codes(qn, c0, c1), runs("q%d" % (t + 1), c0, c1),
+                ["oc%d" % c0])
+            stores.append("oc%d" % c0)
+
+        def result_out(c0, c1, e):
+            dma("S" if e == "s" else "Y", T.y[:, c0:c1], T.ys[:, c0:c1], runs("ys", c0, c1), ["y%d" % c0])
+            stores.append("y%d" % c0)
 
         def scales():
             for r in range(4):
-                dma("S" if r % 2 else "Y", T.osc[4 * r:4 * r + 4, :], sn[32 * r:32 * r + 4, :], qk, ["osc%d" % r])
+                dma("S" if r % 2 else "Y", T.osc[4 * r:4 * r + 4, :], sn[32 * r:32 * r + 4, :], qk, ["osc%d" % r], "osc")
                 stores.append("osc%d" % r)
 
         def lists_out():
@@ -434,61 +526,57 @@ def rank_program(g, core, T, topo):
                 dma("Y", T.ol[h:8:2, C:2 * C], T.na[:, 16 * h:16 * h + 16], ["na"], ["oln%d" % h], "ol")
             stores.extend(["olm0", "olm1", "oln0", "oln1"])
 
-        oxk = ["oxa", "oxb", "oxc"] if t == 0 else ["ox1"]
-        X, Y = T.xy[:, 0:32], T.xy[:, 96:128]
+        oxk = ["oxa", "oxb", "oxc", "oxd"] if t == 0 else ["ox1"]
         step = {
-            "o1b": lambda: ts(T.o1[:, 1:2], T.o1[:, 0:1], 16.0, A.add, ["o1a"], ["o1b"]),
-            "fsp": lambda: fill(T.fs[:, C:4 * FW:FW], 0.0, ["fsp"]),
-            "ptp": lambda: fill(T.pt[:, 4 * CAP:], 0.0, ["ptp"]),
-            "htp": lambda: fill(T.ht[:, 4 * CAP:], 0.0, ["htp"]),
-            "t1p": lambda: fill(T.t1[:, 4 * C:], 0.0, ["t1p"]),
-            "ox1": lambda: ts(T.ox[:, 4:7], T.ox[:, 0:3], 1.0, A.add, ["oxa", "oxb", "oxc"], ["ox1"]),
-            "xs": lambda: tt(T.xs[:], T.st[:].indirect(T.ox[:, 4 * t:4 * t + 3]), T.cap[:], A.max,
-                             ["st%d" % b for b in range(PAD)] + ["cap"] + oxk, ["xs"]),
-            "m1": lambda: tt(T.m1[:, 0:46], T.xs[:, 0:46], T.xs[:, 2:48], A.min, ["xs"], ["m1"]),
-            "c1": lambda: tt(T.c1[:, 0:46], T.xs[:, 2:48], T.xs[:, 0:46], A.is_lt, ["xs"], ["c1"]),
-            "m2": lambda: tt(T.m2[:, 0:42], T.m1[:, 0:42], T.m1[:, 4:46], A.min, ["m1"], ["m2"]),
-            "c2": lambda: tt(T.c2[:, 0:42], T.m1[:, 4:46], T.m1[:, 0:42], A.is_lt, ["m1"], ["c2"]),
-            "m8": lambda: tt(T.m8[:, 0:34], T.m2[:, 0:34], T.m2[:, 8:42], A.min, ["m2"], ["m8"]),
-            "c3": lambda: tt(T.z0[:, 2:128:4], T.m2[:, 8:40], T.m2[:, 0:32], A.is_lt, ["m2", "zk"], ["c3"]),
-            "z2": lambda: tt(T.z1[:, 2:184:4], T.c1[:, 0:46], T.a0[:, 0:46], A.add, ["c1", "a0"], ["z2"]),
-            "z0": lambda: tt(T.z1[:, 0:128:4], T.c1[:, 8:40], T.a0[:, 8:40], A.add, ["c1", "a0"], ["z0"]),
-            "z3": lambda: tt(T.z1[:, 3:128:4], T.c2[:, 0:32], T.z1[:, 18:146:4], A.mult, ["c2", "z2"], ["z3"]),
-            "z1": lambda: tt(T.z1[:, 1:128:4], T.c2[:, 8:40], T.z1[:, 50:178:4], A.mult, ["c2", "z2"], ["z1"]),
-            "a3": lambda: scan(T.a3[:], T.z0[:], T.z1[:, 0:128], A.mult, A.max, ["z0", "z1", "z2", "z3", "c3"], ["a3"]),
-            "x": lambda: tt(X, T.xs[:, 0:32], T.m8[:, 2:34], A.is_le, ["xs", "m8", "xy"], ["x"]),
-            "y": lambda: tt(Y, T.xs[:, 16:48], T.m8[:, 0:32], A.is_lt, ["xs", "m8", "xy"], ["y"]),
-            "lb0": lambda: scan(T.lb[:, 1:48], T.xy[:, 0:94:2], T.xy[:, 96:190:2], A.add, A.add, ["x", "y", "lbz"], ["lb0"]),
-            "lb1": lambda: scan(T.lb[:, 49:96], T.xy[:, 1:95:2], T.xy[:, 97:191:2], A.add, A.add, ["x", "y", "lbz"], ["lb1"]),
-            "mf": lambda: ts(T.mf[:], T.a3[:].indirect(T.om[:]), 1.0 / 1024, A.mult, ["a3", "om0", "om1"], ["mf"]),
+            "xs": lambda: tt(T.xs[:], T.st[:].indirect(T.ox[:, 4 * t:4 * t + 4]), T.cap[:], A.max,
+                             ["st%d" % b for b in range(PAD)] + ["cap1", "cap2"] + oxk, ["xs"]),
+            "pm": lambda: scan(T.pm[:, 0:54], T.rz[:, 0:54], T.xs[:, 0:54], A.add, A.min, ["xs", "rz"], ["pm"]),
+            "sm": lambda: scan(T.sm[:, 53::-1], T.rz[:, 54:0:-1], T.xs[:, 53::-1], A.add, A.min, ["xs", "rz"], ["sm"]),
+            "m8": lambda: tt(T.m8[:, 0:46], T.sm[:, 0:46], T.pm[:, 8:54], A.min, ["sm", "pm"], ["m8"]),
+            "ff": lambda: tt(T.ff[:, 1:54], T.xs[:, 1:54], T.pm[:, 0:53], A.is_lt, ["xs", "pm"], ["ff"]),
+            "nf": lambda: tt(T.nf[:, 0:45], T.xs[:, 0:45], T.sm[:, 0:45], A.not_equal, ["xs", "sm"], ["nf"]),
+            "c3": lambda: tt(T.z0[:, 1:88:2], T.pm[:, 9:53], T.sm[:, 1:45], A.is_lt, ["sm", "pm", "zk"], ["c3", "zk"]),
+            "lf": lambda: scan(T.z1[:, 0:88:2], T.ff[:, 9:53], T.a0[:, 9:53], A.add, A.min, ["ff", "a0"], ["lf"]),
+            "lr": lambda: scan(T.z1[:, 87::-2], T.nf[:, 44:0:-1], T.a0[:, 44:0:-1], A.mult, A.max, ["nf", "a0"], ["lr"]),
+            "a3": lambda: scan(T.a3[:, 0:88], T.z0[:, 0:88], T.z1[:, 0:88], A.mult, A.max, ["c3", "lf", "lr"], ["a3"]),
+            "lk": lambda: act(T.lk[:], T.lb[:, 0:70].indirect(T.ol2[:]), ["lb0", "lb1", "ol0", "ol1"], ["lk"]),
+            "mfl": lambda: tt(T.mfl[:], T.a3[:, 0:88].indirect(T.om[:]), T.lk[:], A.add, ["a3", "om0", "om1", "lk"], ["mfl"]),
+            "mt": lambda: turn(T.mt[:], T.mfl[:], ["mfl"], ["mt"]),
+            "mf": lambda: act(T.mf[:], T.a3[:, 0:88].indirect(T.om[:]), ["a3", "om0", "om1"], ["mf"]),
             "ma": lambda: act(T.ma[:], T.mf[:], ["mf"], ["ma"], None, 0.0, 1024.0),
-            "mt": lambda: turn(T.mt[:], T.mf[:], ["mf"], ["mt"]),
-            "wt": lambda: turn(T.wt[:], T.lb[:], ["lb0", "lb1"], ["wt"]),
-            "ub": lambda: scan(T.ub[:, 1:64], T.wt[:, 32:95], T.keep[:, 0:63], A.add, A.mult, ["wt", "keep"], ["ub"]),
-            "vu": lambda: tt(T.vu[:], T.wt[:, 0:64].indirect(T.o1[:]), T.mt[:], A.add, ["wt", "mt", "o1a", "o1b"], ["vu"]),
-            "vw": lambda: tt(T.vw[:], T.ub[:].indirect(T.o1[:]), T.vu[:], A.add, ["ub", "ub0", "vu", "o1a", "o1b"], ["vw"]),
+            "wt": lambda: turn(T.wt[:], T.lb[:, 19:51], ["lb0", "lb1"], ["wt"]),
+            "ub": lambda: scan(T.ub[:, 1:32], T.wt[:, 0:31], T.keep[:, 0:31], A.add, A.mult, ["wt", "keep"], ["ub"]),
+            "vw": lambda: tt(T.vw[:], T.ub[:], T.mt[:], A.add, ["ub", "ub0", "mt"], ["vw"]),
             "n16": lambda: ts(T.n16[:], T.vw[:], float(CAP), A.min, ["vw"], ["n16"]),
             "pq": lambda: quant(T.pq[:], T.ps[:], T.pt[:],
                                 ["pt%d%d" % (i, b) for i in range(len(PARTS)) for b in range(4)] + ["ptp"], ["pq"]),
-            "hq": lambda: quant(T.hq[:], T.hs[:], T.ht[:], ["ht0", "ht1", "ht2", "ht3", "htp"], ["hq"]),
-            "vq": lambda: quant(T.vq[:], T.vs[:], T.vt[:], ["vt"], ["vq"]),
+            "hq": lambda: quant(hq[:], hs[:], T.ht[:], ["ht0", "ht1", "ht2", "ht3", "htp"], ["hq"]),
             "va": lambda: turn(T.va[:], T.vw[:], ["vw"], ["va"]),
             "na": lists_out,
+            "nn": lambda: cp(T.nn[:], T.va[:].indirect(T.o2[:]), ["va", "o2"], ["nn"]),
+            "nns": lambda: act(T.nn[:], T.va[:].indirect(T.o2[:]), ["va", "o2"], ["nn"]),
+            "nt": lambda: turn(T.nt[:], T.nn[:], ["nn"], ["nt"]),
+            "n20": lambda: ts(T.n2[:, 0:32], T.vw[:], float(CAP), A.min, ["vw", "h7"], ["n20"], T.pf[:, 12:13], A.max),
+            "n21": lambda: ts(T.n2[:, 32:64], T.nt[:], float(CAP), A.min, ["nt"], ["n21"]),
             "osc": scales,
-            "early": lambda: early(qk),
+            "early": lambda: early(qk + runs("t10", 0, LATE) + runs("t11", 0, LATE)),
         }
-        by_letter = {"f": held, "s": search, "r": count, "k": run_list, "d": candidates, "t": across, "e": least,
-                     "l": column, "p": pack, "W": product, "h": scaled, "D": unpack, "u": unpacked, "G": gather, "A": add,
-                     "B": both, "Q": state, "Y": result}
+        by_letter = {"F": hold, "f": held, "x": leaves, "y": enters, "b": sums, "s": search, "r": count, "k": run_list,
+                     "d": candidates, "t": across, "e": least, "l": column, "p": pack, "W": product, "h": scaled,
+                     "D": unpack, "u": unpacked, "G": gather, "A": add, "B": both, "P": pick, "S": pick_scales,
+                     "H": opened, "J": joined, "C": cast, "Q": state, "Y": result, "O": codes_out, "Z": result_out}
         for name in names:
-            if name in step:
+            if name in once:
+                k = len(ops)
+                once[name]()
+                kept.update(x for o in ops[k:] for x in o["w"])
+            elif name in step:
                 step[name]()
-                continue
-            engine = [name[-1]] if name[-1] in "sv" else []
-            rest = name[1:len(name) - len(engine)]
-            by_letter[name[0]](*([int(x) for x in (rest.split(".") if "." in rest else rest)] + engine))
-        lasting = set(qk) | {"qb", "q00", "q01", "vq", "o1b", "fsp", "ptp", "htp", "t1p", "ox1"}
-        stale.update(k for o in ops[first:] for k in o["w"] if k not in lasting)
+            else:
+                engine = [name[-1]] if name[-1] in "sv" else []
+                rest = name[1:len(name) - len(engine)]
+                by_letter[name[0]](*([int(x) for x in (rest.split(".") if "." in rest else rest)] + engine))
+        stale.update(k for o in ops[first:] for k in o["w"] if k not in kept and k not in qk)
 
     stale.clear()
     op(None, None, (), ["sent"], sem=("sent", sent[0]))

from concourse.mybir import dt, AluOpType, AxisListType, ActivationFunctionType

C, CAP, ROUNDS, PAD = 512, 112, 2, 12
FW = 528
BIG = 8.0e29
CODE = "float8_e4m3fn_x4"
LATE = 192
MID = 352


def _sb(dtype, **widths):
    return {k: ("sbuf", [128, n], dtype) for k, n in widths.items()}


SCRATCH = {
    "psF": ("psum", [128, 2048], "float32"), "psR": ("psum", [128, 2048], "float32"),
    **_sb("bfloat16", t0=4 * (C + PAD), t1=4 * (C + PAD), t2=4 * C, ut=512, vt=512, et=516, eh=516, zt=1024, fs=4 * FW,
          pt=512, ht=512, dh=512, tmp=4 * C),
    **_sb(CODE, qa=C + PAD, qb=256, q2=C, uq=128, vq=128, eq=512, woc=512, w0c=512, w1c=512, pq=128, hq0=128, hq1=128,
          eg=512, pa0=768, pa1=768),
    **_sb("uint8", sa=C + PAD, sb=256, s2=C, us=128, vs=128, es=512, wos=512, w0s=512, w1s=512, ps=128, hs0=128, hs1=128,
          egs=512, pb0=768, pb1=768),
    **_sb("int32", pi=8),
    **_sb("uint16", ox=8, om=2, ol2=2, od=2, kap=64, e16=16, n16=32, o2=2, n2=64),
    **_sb("float32", ys=C, pf=16, wrow=64, a0=64, cap=64, a1=64, tb=32, keep=64, r1=8, slot1=8, r2=224, slot2=224, st=768,
          xs=64, pm=56, sm=56, rz=64, m8=48, ff=56, nf=56, lk=32, mfl=32, z0=96, z1=128, a3=96, ma=32, xy=192, lb=96,
          mf=32, mt=32, wt=32, ub=32, kf=32, sg=448, f1=504, vw=32, dd=224, dt2=224, em=8, va=32, na=32, nn=32, nt=32),
}
POOL = {"V": 48, "S": 28, "P": 20, "G": 12, "D": 36}
SEMAPHORES = [k + str(i) for k in POOL for i in range(POOL[k])] + ["w0in", "w1in", "sent"]

JUMPS = [(9, -64, 0, 0), (14, -736, 0, 1), (2, -64, 1, 0), (11, -848, 1, 1), (4, -64, 2, 0), (9, -736, 2, 0), (13, -64, 2, 1)]
BASES = [-64.0, 160.0, 272.0]
PARTS = [(0, 3), (3, 7)]
LISTS = [
    "F0 unit1 xs unit2 sm pm unit3 m8 nf ff F1 x0 y1 y0 x1 F2 c3 b0 b1 f0 lr lf wt f1 a3 f2 lk ub mfl s2s s0s s1s s6v mt r6 "
    "F3 k0 vw s4s s3s s5s k1 d0 d1 f3 t0 t1 e1 e2 e0 e4 e3 e6 e5 l0 l1 va p01v p03s p00v p10v p02s p13s p12s nns p11v n20 "
    "pq W1 h1s half3 W0 half0 half1 nt h0v W2 h2v W3 n16 n21 ox1 h3s hq half2 D0 D1 S1s D3 P1 u0v D2 S0s H0 u2s u1s u3s H2 "
    "P0 J00 J10 B0.192.512 G2.192.512 B1.192.512 H1 J01 A2.192.512 G3.192.416 G3.416.512 J12 C0.0.192s J11 A3.288.384 "
    "A3.192.288 C1.0.192s J02 H3 J13 A3.384.512 Q192.512 J03 C2.0.192s early C3.0.192s vq Q0.192",
    "xs sm pm nf m8 c3 F0 F1 ff f0 y1 x0 y0 f1 x1 lr b0 F2 b1 lf f2 wt a3 lk F3 ub mfl s1s s6v s0s s5v mt r6 r5 s2s s3s vw "
    "s4s k0 k1 d0 d1 mf t0 t1 ma e0 e1 e2 e4 f3 e6 e5 e3 l0 p03s n16 va l1 p02s p12s p00v p01v p10v p11v p13s na n20 pq W1 "
    "W0 nn W2 W3 nt h1v h0s h2s h3v hq D0 n21 D3 D1 P0 S0s D2 u0s H0 J00 P1 S1s u2s J10 u1s u3s C0.0.192s H2 J02 H1 J11 "
    "B0.192.512 J12 B2.192.512 J01 H3 J13 J03 B1.192.512 B3.384.512 B3.192.384 C2.0.192s C1.0.192s C3.0.192s Q384.512 "
    "O384.512s Y384.512s Q0.192 O0.192v Q192.384 O192.384s Y0.192v Z384.512s Z0.192v osc Y192.384v Z192.384v",
    "pi0 zt row2 row1 bits3 bits2 bits1 t0p zk pf et sign4 qh q8 xyz wrow qs om0 sign5 rz sign3 base0 qx0 sign0 i16 ol1 ol0 "
    "sign2 base2 q6 jump0 uq base1 a0 par one hone sign1 qx1 t1p capf jump2 hcap jump4 kfz first layers cap fsp sign6 jump1 "
    "qx2 xrow jump5 cape om1 ub0 ptp slot2 f1p od oxd capd eh o2 lbz jump3 jump6 htp unit0 slot1",
]


def emit(ops, queues, T):
    writer, readers, known, done = {}, {}, {}, []
    members = {}
    for i, o in enumerate(ops):
        if o["grp"]:
            members.setdefault(o["grp"], []).append(i)
    signal = set()
    for i, o in enumerate(ops):
        q = o["q"]
        deps = set()
        for k in o["r"]:
            deps.add(writer[k])
            if k.startswith("ps"):
                deps.update(j for j in readers.get(k, []) if ops[j]["q"] != q)
        for k in o["w"]:
            if k in writer:
                deps.add(writer[k])
            deps.update(readers.get(k, []))
        deps.discard(i)
        have = known.setdefault(q, set())
        if o["adds"]:
            have.update(writer[k] for k in o["w"] + o["r"] if k.startswith("ps") or k[0] == "H")
        waits = []
        for j in sorted(deps, reverse=True):
            if j in have:
                continue
            who = members[ops[j]["grp"]] if ops[j]["grp"] else [j]
            assert max(who) < i
            waits.append(who[0])
            for m in who:
                have |= done[m]
                signal.add(m)
        o["waits"] = waits[::-1]
        o["have"] = set(have)
        done.append(set(have) | {i})
        for k in o["r"]:
            readers.setdefault(k, []).append(i)
        for k in o["w"]:
            writer[k] = i
            readers[k] = []
    last, count, ticket = {}, {}, {}
    for i, o in enumerate(ops):
        if o["q"] is None:
            ticket[i] = o["sem"]
            continue
        eng = queues[o["q"]]
        for j in o["waits"]:
            eng.wait_ge(T.sem[ticket[j][0]], ticket[j][1])
        if o["fn"] is None:
            continue
        ins = o["fn"]()
        if i not in signal:
            continue
        step = 16 if o["dma"] else 1
        pool = "D" if o["dma"] else o["q"]
        who = members[o["grp"]] if o["grp"] else [i]
        if who[0] == i:
            name = None
            for n in range(POOL[pool]):
                s = pool + str(n)
                if s not in last or (not o["dma"] and all(m in o["have"] for m in last[s])):
                    name = s
                    break
            last[name] = who
            count[name] = count.get(name, 0) + step * len(who)
            ticket[i] = (name, count[name])
        ins.then_inc(T.sem[ticket[who[0]][0]], step)


def rank_program(g, core, T, topo):
    rank = T.rank_of(core)
    if rank is None:
        return
    cores = T.cores
    n_ranks = len(cores)
    A, F = AluOpType, ActivationFunctionType
    v, s, pe = g.vector, g.scalar, g.tensor
    queues = {"V": v, "S": s, "P": pe, "G": g, "Y": g.sync}
    ops = []
    stale = set()

    def op(q, fn, r=(), w=(), grp=None, dma=False, sem=None, adds=False):
        assert not stale & set(r)
        stale.difference_update(w)
        ops.append({"q": q, "fn": fn, "r": list(r), "w": list(w), "grp": grp, "dma": dma, "sem": sem, "adds": adds})

    def dma(q, out, in_, r, w, grp=None):
        op(q, lambda: queues[q].dma_start(out, in_), r, w, grp, True)

    def tt(out, a, b, alu, r, w):
        op("V", lambda: v.tensor_tensor(out, a, b, alu), r, w)

    def ts(out, a, s1, o0, r, w, s2=None, o1=None):
        if o1 is None:
            op("V", lambda: v.tensor_scalar(out, a, s1, None, o0), r, w)
        else:
            op("V", lambda: v.tensor_scalar(out, a, s1, s2, o0, o1), r, w)

    def cp(out, a, r, w):
        op("V", lambda: v.tensor_copy(out, a), r, w)

    def fill(ap, c, w):
        op("V", lambda: v.memset(ap, c), (), w)

    def scan(out, d0, d1, o0, o1, r, w):
        op("V", lambda: v.tensor_tensor_scan(out, d0, d1, 0.0, o0, o1), r, w)

    def turn(out, a, r, w, grp=None):
        op("V", lambda: v.transpose(out, a), r, w, grp)

    def reduce(out, a, alu, r, w, size=False):
        op("V", lambda: v.tensor_reduce(out, a, AxisListType.X, alu, apply_absolute_value=size), r, w)

    def act(out, a, r, w, func=None, bias=0.0, scale=1.0, total=None):
        op("S", lambda: s.activation(out, a, F.Copy if func is None else func, bias=bias, scale=scale, accum_out=total),
           r, w)

    def move(out, a, r, w):
        op("S", lambda: s.activation(out, a, F.Copy), r, w)

    def quant(qc, qs, tile, r, w):
        op("V", lambda: v.quantize_mx(qc, qs, tile), r, w)

    def mm(out, wc, ws, xc, xs, r, w, grp=None, start=True, stop=True):
        op("P", lambda: pe.matmul_mx(out, wc, ws, xc, xs, start, stop), r, w, grp, adds=not start)

    def iota(out, pattern, base, mult, w, flt=True):
        if flt:
            op("G", lambda: g.iota(out, pattern, base, mult, allow_small_or_imprecise_dtypes=True), (), w)
        else:
            op("G", lambda: g.iota(out, pattern, base, mult), (), w)

    sent = [0]

    def send(out, in_, dst, mask, sem, r):
        rid, pid, _ = topo.addr(dst)
        sent[0] += bin(mask).count("1")
        op("G", lambda: g.remote_dma(out, in_, T.sem[sem], T.sem.sent, pid, rid, mask), r, ())

    def codes(buf, a, b):
        return buf[:, a:b].bitcast(dt.uint8)

    def narrow(a):
        m = -1
        for c in cores:
            if c != a:
                m &= topo.mask(a, c)
        return m

    def handed_on(r):
        return topo.chip(cores[r]) == topo.chip(cores[(r - 1) % n_ranks])

    def wide(a, b):
        return (topo.mask(a, b) & ~narrow(a)) or narrow(a)

    d0, d1 = cores[(rank - 1) % n_ranks], cores[(rank - 2) % n_ranks]
    nxt = (rank + 1) % n_ranks
    in0 = 2 * bin(narrow(cores[nxt])).count("1")
    if handed_on(nxt):
        in1 = 2 * bin(wide(cores[nxt], core)).count("1")
    else:
        in1 = 2 * bin(narrow(cores[(rank + 2) % n_ranks])).count("1")
    op(None, None, (), ["w0"], sem=("w0in", in0))
    op(None, None, (), ["w1"], sem=("w1in", in1))

    dma("Y", T.t0[:, 4 * MID:4 * C], T.x[:, 4 * MID:4 * C], (), ["t0a"])
    dma("Y", T.ut[:], T.u[:], (), ["ut"])
    dma("Y", T.t0[:, 4 * LATE:4 * MID], T.x[:, 4 * LATE:4 * MID], (), ["t0b"])
    dma("Y", T.t0[:, 0:4 * LATE], T.x[:, 0:4 * LATE], (), ["t0c"])
    dma("Y", T.wos[:], T.ws[:], (), ["wos"])
    dma("Y", codes(T.woc, 0, 512), T.wc[:], (), ["woc"])

    qc, hc, bc = T.pf[:, 1:2], T.pf[:, 2:3], T.pf[:, 3:4]
    one = T.et[:, 3:515:4]

    def unit(b):
        quant(T.eq[:, 128 * b:128 * b + 128], T.es[:, 128 * b:128 * b + 128], T.et[:, 3 - b:515 - b], ["et"], ["eq%d" % b])

    def half(b):
        quant(T.eg[:, 128 * b:128 * b + 128], T.egs[:, 128 * b:128 * b + 128], T.eh[:, 3 - b:515 - b], ["eh"], ["eg%d" % b])

    def bits(k):
        ts(T.pi[:, k:k + 1], T.pi[:, 0:1], (15, 16, 1)[k - 1], A.bitwise_and, ["pi0"], ["pi%d" % k])

    def layers():
        send(T.w0s[:], T.wos[:], d0, narrow(core), "w0in", ["wos"])
        send(codes(T.w0c, 0, 512), codes(T.woc, 0, 512), d0, narrow(core), "w0in", ["woc"])
        if not handed_on((rank - 1) % n_ranks):
            send(codes(T.w1c, 0, 512), codes(T.woc, 0, 512), d1, narrow(core), "w1in", ["woc", "w0"])
            send(T.w1s[:], T.wos[:], d1, narrow(core), "w1in", ["wos", "w0"])
        if handed_on(rank):
            send(codes(T.w1c, 0, 512), codes(T.w0c, 0, 512), d0, wide(core, d0), "w1in", ["w0"])
            send(T.w1s[:], T.w0s[:], d0, wide(core, d0), "w1in", ["w0"])

    def early(keys):
        mm(T.psR[:, 0:512], T.uq[:], T.us[:], T.qa[:, 0:C], T.sa[:, 0:C], ["uq", "qs"] + keys, ["psR0"], stop=False)
        mm(T.psR[:, 512:1024], T.uq[:], T.us[:], T.qa[:, PAD:C + PAD], T.sa[:, PAD:C + PAD], ["uq", "qs"] + keys, ["psR1"],
           stop=False)

    def level(ap, n, c, w, r=()):
        act(ap, T.r2[:, 0:n], ["r2"] + list(r), w, None, c, 0.0)

    def sign(k):
        act(T.tb[:, 8 + k:9 + k], qc, ["pf"], ["tj%d" % k], F.Sign, 0.5 - JUMPS[k][0])

    def jump(k):
        a, z, c, end = JUMPS[k]
        on = k and JUMPS[k - 1][2] == c
        ts(T.ox[:, c:c + 1] if end else T.tb[:, 16 + k:17 + k], T.tb[:, 8 + k:9 + k], 0.5 * z, A.mult,
           ["tj%d" % k, "tk%d" % (k - 1) if on else "tc%d" % c], ["ox" + "abc"[c] if end else "tk%d" % k],
           T.tb[:, 15 + k:16 + k] if on else T.tb[:, 4 + c:5 + c], A.add)

    def base(c):
        act(T.tb[:, 4 + c:5 + c], qc, ["pf"], ["tc%d" % c], None, BASES[c] + sum(0.5 * z for a, z, k, end in JUMPS if k == c),
            64.0)

    once = {
        "et": lambda: fill(T.et[:], 0.0, ["et0"]),
        "pi0": lambda: iota(T.pi[:, 0:1], [[0, 1]], 0, 1, ["pi0"], False),
        "one": lambda: op("G", lambda: g.affine_select(one, one, [[-1, 128]], A.not_equal, 1.0, 0, 1), ["et0"], ["et"]),
        "wrow": lambda: iota(T.wrow[:, 0:54], [[0, 2], [8, 3], [1, 9]], -1, 0, ["wrow"]),
        "zk": lambda: level(T.z0[:], 96, 0.0, ["zk"]),
        "xrow": lambda: level(T.keep[:, 0:32], 32, 1.0, ["keep"]),
        "row1": lambda: iota(T.r1[:], [[16, 8]], 0, 0, ["r1"]),
        "row2": lambda: iota(T.r2[:], [[16, 7], [1000, 2], [1, 16]], 0, 0, ["r2"]),
        "layers": layers,
        "t0p": lambda: fill(T.t0[:, 4 * C:], 0.0, ["t0p"]),
        "zt": lambda: fill(T.zt[:, 0:4 * LATE], 0.0, ["zt"]),
        "xyz": lambda: level(T.xy[:], 192, 0.0, ["xy"]),
        "rz": lambda: op("G", lambda: g.affine_select(T.rz[:, 0:63], T.z0[:, 0:63], [[0, 7], [1, 9]], A.not_equal,
                                                      BIG * 1.125, 0, 0), ["zk"], ["rz"]),
        "pf": lambda: cp(T.pf[:, 1:4], T.pi[:, 1:4], ["pi1", "pi2", "pi3"], ["pf"]),
        "lbz": lambda: level(T.lb[:, 0:70:69], 2, 0.0, ["lbz"]),
        "ub0": lambda: level(T.ub[:, 0:1], 1, 0.0, ["ub0"]),
        "kfz": lambda: level(T.kf[:], 32, 0.0, ["kfz"]),
        "f1p": lambda: level(T.f1[:, 32:504:72], 7, -32.0, ["f1p"]),
        "i16": lambda: ts(T.pf[:, 4:5], qc, hc, A.add, ["pf"], ["i16"], 1.0 / 64, A.mult),
        "par": lambda: act(T.pf[:, 7:8], hc, ["pf"], ["par"], None, 0.0, -62.5),
        "qh": lambda: act(T.pf[:, 9:10], qc, ["pf"], ["qh"], None, 0.5),
        "hone": lambda: act(T.pf[:, 11:12], hc, ["pf"], ["h1"], None, 0.0, 1.0 / 16),
        "hcap": lambda: act(T.pf[:, 12:13], hc, ["pf"], ["h7"], None, 0.0, CAP / 16.0),
        "eh": lambda: act(T.eh[:], T.et[:], ["et", "h1"], ["eh"], F.Identity, 0.0, T.pf[:, 11:12]),
        "qs": lambda: quant(T.qa[:, 0:LATE], T.sa[:, 0:LATE], T.zt[:, 0:4 * LATE], ["zt"], ["qs"]),
        "a0": lambda: act(T.a0[:, 0:54], T.wrow[:, 0:54], ["wrow", "i16"], ["a0"], F.Identity, T.pf[:, 4:5], 1.0 / 1024),
        "slot1": lambda: act(T.slot1[:], T.r1[:], ["r1", "qh"], ["slot1"], F.Identity, T.pf[:, 9:10]),
        "slot2": lambda: act(T.slot2[:], T.r2[:], ["r2", "par"], ["slot2"], F.Identity, T.pf[:, 7:8]),
        "qx0": lambda: quant(T.qa[:, MID:], T.sa[:, MID:], T.t0[:, 4 * MID:], ["t0a", "t0p"], ["q00"]),
        "uq": lambda: quant(T.uq[:], T.us[:], T.ut[:], ["ut"], ["uq"]),
        "qx1": lambda: quant(T.qa[:, LATE:MID], T.sa[:, LATE:MID], T.t0[:, 4 * LATE:4 * MID], ["t0b"], ["q0"]),
        "first": lambda: early(["q0", "q00"]),
        "qx2": lambda: quant(T.qb[:, 0:LATE], T.sb[:, 0:LATE], T.t0[:, 0:4 * LATE], ["t0c"], ["qb"]),
        "capf": lambda: ts(T.a1[:, 0:54], T.a0[:, 0:54], 0.5, A.is_ge, ["a0"], ["capf"], BIG, A.mult),
        "cap": lambda: act(T.cap[:, 0:54], T.a1[:, 0:54], ["capf"], ["cap0"], None, -0.5 * BIG),
        "capd": lambda: level(T.cap[:, 0:55:9], 7, 0.5 * BIG, ["cap1"], ["cap0"]),
        "cape": lambda: level(T.cap[:, 55:64], 9, 0.5 * BIG, ["cap2"]),
        "q6": lambda: act(T.pf[:, 14:15], qc, ["pf"], ["q6"], None, 6.75),
        "oxd": lambda: ts(T.ox[:, 3:4], T.pf[:, 14:15], 11.75, A.min, ["q6"], ["oxd"], 64.0, A.mult),
        "q8": lambda: ts(T.pf[:, 13:14], qc, 8.0, A.is_ge, ["pf"], ["q8"], qc, A.add),
        "om0": lambda: ts(T.om[:, 0:1], T.pf[:, 13:14], 2.0, A.mult, ["q8"], ["om0"], 1.0, A.add),
        "om1": lambda: ts(T.om[:, 1:2], T.pf[:, 13:14], 2.0, A.mult, ["q8"], ["om1"], 55.0, A.add),
        "ol0": lambda: cp(T.ol2[:, 0:1], T.pf[:, 13:14], ["q8"], ["ol0"]),
        "ol1": lambda: ts(T.ol2[:, 1:2], T.pf[:, 13:14], -1.0, A.mult, ["q8"], ["ol1"], 69.0, A.add),
        "od": lambda: ts(T.od[:, 0:1], qc, bc, A.subtract, ["pf"], ["od"], 0.5, A.mult),
        "o2": lambda: ts(T.o2[:], T.keep[:, 0:2], 15.0, A.add, ["keep", "pf"], ["o2"], qc, A.add),
        "fsp": lambda: level(T.fs[:, C:4 * FW:FW], 4, 0.0, ["fsp"]),
        "ptp": lambda: level(T.pt[:, 4 * CAP:], 64, 0.0, ["ptp"]),
        "htp": lambda: level(T.ht[:, 4 * CAP:], 64, 0.0, ["htp"]),
        "t1p": lambda: level(T.t1[:, 4 * C:], 48, 0.0, ["t1p"]),
        "ox1": lambda: ts(T.ox[:, 4:8], T.ox[:, 0:4], 1.0, A.add, ["oxa", "oxb", "oxc", "oxd"], ["ox1"]),
        "vq": lambda: quant(T.vq[:], T.vs[:], T.vt[:], ["vt"], ["vq"]),
    }
    for b in range(7):
        once["unit%d" % b] = lambda b=b: unit(b)
        once["half%d" % b] = lambda b=b: half(b)
        once["bits%d" % b] = lambda b=b: bits(b)
        once["base%d" % b] = lambda b=b: base(b)
        once["sign%d" % b] = lambda b=b: sign(b)
        once["jump%d" % b] = lambda b=b: jump(b)
    for name in LISTS[ROUNDS].split():
        once[name]()

    layer = [(T.w0c, T.w0s), (T.w1c, T.w1s)]
    part_of = {c: i for i, (c0, c1) in enumerate(PARTS) for c in range(c0, c1)}
    stores = []
    wd = CAP + 2

    def runs(name, c0, c1, width=16):
        return ["%s_%d" % (name, k) for k in range(c0 // width, c1 // width)]

    qk = ["q0", "q00"]
    kept = {"qb", "q0", "q00", "zk"}
    for t in range(ROUNDS):
        tn, qn, sn = [(T.t1, T.qa, T.sa), (T.t2, T.q2, T.s2)][t]
        wq, wsc = layer[t]
        hq, hs, pa, pb = [(T.hq0, T.hs0, T.pa0, T.pb0), (T.hq1, T.hs1, T.pa1, T.pb1)][t]
        last = t == ROUNDS - 1
        first = len(ops)
        names = LISTS[t].split()
        mm(T.psR[:, 0:LATE], T.uq[:], T.us[:], T.qb[:, 0:LATE], T.sb[:, 0:LATE], ["qb"], ["psR0"], "s%d" % t, False)
        mm(T.psR[:, 512:512 + LATE - PAD], T.uq[:], T.us[:], T.qb[:, PAD:LATE], T.sb[:, PAD:LATE], ["qb"], ["psR1"],
           "s%d" % t, False)
        for b in range(PAD):
            turn(T.st[:, 64 * b:64 * b + 64], T.psR[:, b:1024:16], ["psR0", "psR1"], ["st%d" % b], "tr%d" % t)
        if t == 0:
            dma("Y", T.vt[:], T.v[:], ["st0"], ["vt"])

        def hold(b, qk=qk):
            e, es = T.eq[:, 128 * b:128 * b + 128], T.es[:, 128 * b:128 * b + 128]
            mm(T.psF[:, 512 * b:512 * b + 512], e, es, T.qa[:, 0:C], T.sa[:, 0:C], ["eq%d" % b, "qs"] + qk, ["psF%d" % b],
               stop=False)
            mm(T.psF[:, 512 * b:512 * b + LATE], e, es, T.qb[:, 0:LATE], T.sb[:, 0:LATE], ["qb"], ["psF%d" % b],
               start=False)

        qk = runs("q%d" % (t + 1), 0 if last else LATE, C)

        def held(b):
            act(T.fs[:, FW * b:FW * b + C], T.psF[:, 512 * b:512 * b + 512], ["psF%d" % b], ["fs%d" % b])

        def leaves(h):
            tt(T.xy[:, 48 * h:48 * h + 17], T.xs[:, 27 * h + 1:27 * h + 18], T.m8[:, 27 * h + 2:27 * h + 19], A.is_le,
               ["xs", "m8", "xy"], ["x%d" % h])

        def enters(h):
            tt(T.xy[:, 96 + 48 * h:113 + 48 * h], T.xs[:, 27 * h + 10:27 * h + 27], T.m8[:, 27 * h + 1:27 * h + 18], A.is_lt,
               ["xs", "m8", "xy"], ["y%d" % h])

        def sums(h):
            scan(T.lb[:, 68:34:-1] if h else T.lb[:, 1:35], T.xy[:, 48 * h:48 * h + 34], T.xy[:, 96 + 48 * h:130 + 48 * h],
                 A.add, A.add, ["x%d" % h, "y%d" % h, "lbz"], ["lb%d" % h])

        def kf(c):
            i = part_of[c]
            k = 8 * i + c - PARTS[i][0]
            return T.kf[:, k:k + 1]

        def search(c, e):
            if e == "v":
                ts(T.f1[:, 72 * c:72 * c + 32], T.ub[:], T.slot1[:, c:c + 1], A.is_lt, ["ub", "ub0", "slot1"], ["f1%d" % c],
                   2.0, A.mult)
            else:
                act(T.sg[:, 64 * c:64 * c + 32], T.ub[:], ["ub", "ub0", "slot1", "kfz"], ["kf%d" % c, "sg%d" % c], F.Sign,
                    T.slot1[:, c:c + 1], -1.0, kf(c))

        def count(c):
            reduce(kf(c), T.f1[:, 72 * c:72 * c + 33], A.add, ["f1%d" % c, "kfz", "f1p"], ["kf%d" % c])

        def run_list(i):
            c0, c1 = PARTS[i]
            ts(T.kap[:, 16 * i:16 * i + 16], T.kf[:, 8 * i:8 * i + 8].indirect(T.od[:, 0:1]), 0.5, A.mult,
               ["od"] + ["kf%d" % c for c in range(c0, c1)], ["kap%d" % i], 15.0, A.add)

        def candidates(i):
            c0, c1 = PARTS[i]
            tt(T.dd[:, 32 * c0:32 * c1], T.vw[:].indirect(T.kap[:, 16 * i:16 * i + 2 * (c1 - c0)]),
               T.slot2[:, 32 * c0:32 * c1], A.subtract, ["vw", "kap%d" % i, "slot2"], ["dd%d" % i])

        def across(i):
            c0, c1 = PARTS[i]
            turn(T.dt2[:, 32 * c0:32 * c1], T.dd[:, 32 * c0:32 * c1], ["dd%d" % i], ["dt2%d" % i])

        def listed(i):
            c0, c1 = PARTS[i]
            k = sum(2 * ((b - a + 1) // 2) for a, b in PARTS[:i])
            return T.e16[:, k:k + c1 - c0]

        def least(c):
            reduce(T.em[:, c:c + 1], T.dt2[:, 32 * c:32 * c + 32], A.min, ["dt2%d" % part_of[c]], ["em%d" % c], True)

        def column(i):
            c0, c1 = PARTS[i]
            ts(listed(i), T.em[:, c0:c1], 1024.0, A.mult, ["em%d" % c for c in range(c0, c1)], ["e16%d" % i],
               float(C), A.min)

        def pack(i, b, e):
            c0, c1 = PARTS[i]
            (cp if e == "v" else act)(T.pt[:, 64 * c0 + b:64 * c1:4], T.fs[:, FW * b:FW * b + C + 1].indirect(listed(i)),
                                      ["fs%d" % b, "fsp", "e16%d" % i], ["pt%d%d" % (i, b)])

        def product(b):
            mm(T.psR[:, 512 * b:512 * b + 128], wq[:, 128 * b:128 * b + 128], wsc[:, 128 * b:128 * b + 128],
               T.pq[:], T.ps[:], ["w%d" % t, "pq"], ["psR%d" % b, "R%d" % b])

        def scaled(b, e):
            src = T.psR[:, 512 * b:512 * b + CAP]
            if e == "v":
                ts(T.ht[:, b:4 * CAP:4], src, 0.03125, A.mult, ["psR%d" % b, "R%d" % b], ["ht%d" % b])
            else:
                act(T.ht[:, b:4 * CAP:4], src, ["psR%d" % b, "R%d" % b], ["ht%d" % b], None, 0.0, 0.03125)

        def unpack(b):
            mm(T.psR[:, 512 * b:512 * b + 128], T.eq[:, 128 * b:128 * b + 128], T.es[:, 128 * b:128 * b + 128],
               hq[:], hs[:], ["eq%d" % b, "hq"], ["psR%d" % b, "D%d" % b])

        def unpacked(b, e):
            (act if e == "s" else cp)(T.dh[:, 128 * b:128 * b + wd], T.psR[:, 512 * b:512 * b + wd],
                                      ["psR%d" % b, "D%d" % b], ["dh%d" % b])

        def window(b, c0, c1):
            return T.dh[:, 128 * b:128 * b + wd].indirect(T.n16[:, c0 // 16:c1 // 16])

        def gather(b, c0, c1):
            act(T.tmp[:, C * b + c0:C * b + c1], window(b, c0, c1), ["dh%d" % b, "n16"], runs("tmp%d" % b, c0, c1))

        def add(b, c0, c1):
            tt(tn[:, 4 * c0 + b:4 * c1:4], T.tmp[:, C * b + c0:C * b + c1], T.psF[:, 512 * b + c0:512 * b + c1], A.add,
               runs("tmp%d" % b, c0, c1) + ["psF%d" % b], runs("t%d%d" % (t + 1, b), c0, c1))

        def both(b, c0, c1):
            tt(tn[:, 4 * c0 + b:4 * c1:4], window(b, c0, c1), T.fs[:, FW * b + c0:FW * b + c1], A.add,
               ["dh%d" % b, "n16", "fs%d" % b], runs("t%d%d" % (t + 1, b), c0, c1))

        def pick(h):
            cp(pa[:, 384 * h:384 * h + LATE].bitcast(dt.uint32),
               hq[:].bitcast(dt.uint32).indirect(T.n2[:, 32 * h:32 * h + LATE // 16]), ["hq", "n2%d" % h], ["pa%d" % h])

        def pick_scales(h, e):
            (move if e == "s" else cp)(pb[:, 384 * h:384 * h + LATE], hs[:].indirect(T.n2[:, 32 * h:32 * h + LATE // 16]),
                                       ["hq", "n2%d" % h], ["pb%d" % h])

        def opened(b):
            mm(T.psR[:, 512 * b:512 * b + LATE], T.eq[:, 128 * b:128 * b + 128], T.es[:, 128 * b:128 * b + 128],
               T.qb[:, 0:LATE], T.sb[:, 0:LATE], ["dh%d" % b, "qb"], ["psR%d" % b, "H%d" % b], stop=False)

        def joined(h, b):
            e, es, key = [(T.eq, T.es, "eq%d"), (T.eg, T.egs, "eg%d")][h]
            mm(T.psR[:, 512 * b:512 * b + LATE], e[:, 128 * b:128 * b + 128], es[:, 128 * b:128 * b + 128],
               pa[:, 384 * h:384 * h + LATE], pb[:, 384 * h:384 * h + LATE],
               [key % b, "pa%d" % h, "pb%d" % h, "H%d" % b], ["psR%d" % b, "J%d%d" % (h, b)], start=False,
               stop=names.index("J%d%d" % (1 - h, b)) < names.index("J%d%d" % (h, b)))

        def cast(b, c0, c1, e):
            (act if e == "s" else cp)(tn[:, 4 * c0 + b:4 * c1:4], T.psR[:, 512 * b + c0:512 * b + c1],
                                      ["psR%d" % b, "J0%d" % b, "J1%d" % b], runs("t%d%d" % (t + 1, b), c0, c1))

        def state(c0, c1):
            rd = [k for b in range(4) for k in runs("t%d%d" % (t + 1, b), c0, c1)]
            if c0 == 0 and not last:
                assert c1 == LATE
                quant(T.qb[:, 0:c1], T.sb[:, 0:c1], tn[:, 0:4 * c1], rd, ["qb"])
                return
            keys = runs("q%d" % (t + 1), c0, c1)
            end = c1
            if c1 == C and not last:
                end += PAD
                rd.append("t1p")
            quant(qn[:, c0:end], sn[:, c0:end], tn[:, 4 * c0:4 * end], rd, keys + ([] if last else ["q0", "q00"]))
            if last:
                k = c0 // 128
                mm(T.psR[:, 512 * k:512 * k + c1 - c0], T.vq[:], T.vs[:], qn[:, c0:c1], sn[:, c0:c1],
                   ["vq"] + keys + runs("t2%d" % k, 0, LATE), ["psR%d" % k, "Y%d" % k])

        def result(c0, c1, e):
            k = c0 // 128
            (cp if e == "v" else act)(T.ys[:, c0:c1], T.psR[:, 512 * k:512 * k + c1 - c0], ["psR%d" % k, "Y%d" % k],
                                      runs("ys", c0, c1))

        def codes_out(c0, c1, e):
            dma("S" if e == "s" else "Y", T.oc[:, 4 * c0:4 * c1], codes(qn, c0, c1), runs("q%d" % (t + 1), c0, c1),
                ["oc%d" % c0])
            stores.append("oc%d" % c0)

        def result_out(c0, c1, e):
            dma("S" if e == "s" else "Y", T.y[:, c0:c1], T.ys[:, c0:c1], runs("ys", c0, c1), ["y%d" % c0])
            stores.append("y%d" % c0)

        def scales():
            for r in range(4):
                dma("S" if r % 2 else "Y", T.osc[4 * r:4 * r + 4, :], sn[32 * r:32 * r + 4, :], qk, ["osc%d" % r], "osc")
                stores.append("osc%d" % r)

        def lists_out():
            tt(T.na[:], T.va[:], T.mf[:], A.subtract, ["va", "mf"], ["na"])
            for h in range(2):
                dma("Y", T.ol[h:8:2, 0:C], T.ma[:, 16 * h:16 * h + 16], ["ma"], ["olm%d" % h], "ol")
                dma("Y", T.ol[h:8:2, C:2 * C], T.na[:, 16 * h:16 * h + 16], ["na"], ["oln%d" % h], "ol")
            stores.extend(["olm0", "olm1", "oln0", "oln1"])

        oxk = ["oxa", "oxb", "oxc", "oxd"] if t == 0 else ["ox1"]
        step = {
            "xs": lambda: tt(T.xs[:], T.st[:].indirect(T.ox[:, 4 * t:4 * t + 4]), T.cap[:], A.max,
                             ["st%d" % b for b in range(PAD)] + ["cap1", "cap2"] + oxk, ["xs"]),
            "pm": lambda: scan(T.pm[:, 0:54], T.rz[:, 0:54], T.xs[:, 0:54], A.add, A.min, ["xs", "rz"], ["pm"]),
            "sm": lambda: scan(T.sm[:, 53::-1], T.rz[:, 54:0:-1], T.xs[:, 53::-1], A.add, A.min, ["xs", "rz"], ["sm"]),
            "m8": lambda: tt(T.m8[:, 0:46], T.sm[:, 0:46], T.pm[:, 8:54], A.min, ["sm", "pm"], ["m8"]),
            "ff": lambda: tt(T.ff[:, 1:54], T.xs[:, 1:54], T.pm[:, 0:53], A.is_lt, ["xs", "pm"], ["ff"]),
            "nf": lambda: tt(T.nf[:, 0:45], T.xs[:, 0:45], T.sm[:, 0:45], A.not_equal, ["xs", "sm"], ["nf"]),
            "c3": lambda: tt(T.z0[:, 1:88:2], T.pm[:, 9:53], T.sm[:, 1:45], A.is_lt, ["sm", "pm", "zk"], ["c3", "zk"]),
            "lf": lambda: scan(T.z1[:, 0:88:2], T.ff[:, 9:53], T.a0[:, 9:53], A.add, A.min, ["ff", "a0"], ["lf"]),
            "lr": lambda: scan(T.z1[:, 87::-2], T.nf[:, 44:0:-1], T.a0[:, 44:0:-1], A.mult, A.max, ["nf", "a0"], ["lr"]),
            "a3": lambda: scan(T.a3[:, 0:88], T.z0[:, 0:88], T.z1[:, 0:88], A.mult, A.max, ["c3", "lf", "lr"], ["a3"]),
            "lk": lambda: act(T.lk[:], T.lb[:, 0:70].indirect(T.ol2[:]), ["lb0", "lb1", "ol0", "ol1"], ["lk"]),
            "mfl": lambda: tt(T.mfl[:], T.a3[:, 0:88].indirect(T.om[:]), T.lk[:], A.add, ["a3", "om0", "om1", "lk"], ["mfl"]),
            "mt": lambda: turn(T.mt[:], T.mfl[:], ["mfl"], ["mt"]),
            "mf": lambda: act(T.mf[:], T.a3[:, 0:88].indirect(T.om[:]), ["a3", "om0", "om1"], ["mf"]),
            "ma": lambda: act(T.ma[:], T.mf[:], ["mf"], ["ma"], None, 0.0, 1024.0),
            "wt": lambda: turn(T.wt[:], T.lb[:, 19:51], ["lb0", "lb1"], ["wt"]),
            "ub": lambda: scan(T.ub[:, 1:32], T.wt[:, 0:31], T.keep[:, 0:31], A.add, A.mult, ["wt", "keep"], ["ub"]),
            "vw": lambda: tt(T.vw[:], T.ub[:], T.mt[:], A.add, ["ub", "ub0", "mt"], ["vw"]),
            "n16": lambda: ts(T.n16[:], T.vw[:], float(CAP), A.min, ["vw"], ["n16"]),
            "pq": lambda: quant(T.pq[:], T.ps[:], T.pt[:],
                                ["pt%d%d" % (i, b) for i in range(len(PARTS)) for b in range(4)] + ["ptp"], ["pq"]),
            "hq": lambda: quant(hq[:], hs[:], T.ht[:], ["ht0", "ht1", "ht2", "ht3", "htp"], ["hq"]),
            "va": lambda: turn(T.va[:], T.vw[:], ["vw"], ["va"]),
            "na": lists_out,
            "nn": lambda: cp(T.nn[:], T.va[:].indirect(T.o2[:]), ["va", "o2"], ["nn"]),
            "nns": lambda: act(T.nn[:], T.va[:].indirect(T.o2[:]), ["va", "o2"], ["nn"]),
            "nt": lambda: turn(T.nt[:], T.nn[:], ["nn"], ["nt"]),
            "n20": lambda: ts(T.n2[:, 0:32], T.vw[:], float(CAP), A.min, ["vw", "h7"], ["n20"], T.pf[:, 12:13], A.max),
            "n21": lambda: ts(T.n2[:, 32:64], T.nt[:], float(CAP), A.min, ["nt"], ["n21"]),
            "osc": scales,
            "early": lambda: early(qk + runs("t10", 0, LATE) + runs("t11", 0, LATE)),
        }
        by_letter = {"F": hold, "f": held, "x": leaves, "y": enters, "b": sums, "s": search, "r": count, "k": run_list,
                     "d": candidates, "t": across, "e": least, "l": column, "p": pack, "W": product, "h": scaled,
                     "D": unpack, "u": unpacked, "G": gather, "A": add, "B": both, "P": pick, "S": pick_scales,
                     "H": opened, "J": joined, "C": cast, "Q": state, "Y": result, "O": codes_out, "Z": result_out}
        for name in names:
            if name in once:
                k = len(ops)
                once[name]()
                kept.update(x for o in ops[k:] for x in o["w"])
            elif name in step:
                step[name]()
            else:
                engine = [name[-1]] if name[-1] in "sv" else []
                rest = name[1:len(name) - len(engine)]
                by_letter[name[0]](*([int(x) for x in (rest.split(".") if "." in rest else rest)] + engine))
        stale.update(k for o in ops[first:] for k in o["w"] if k not in kept and k not in qk)

    stale.clear()
    op(None, None, (), ["sent"], sem=("sent", sent[0]))
    op("G", None, ["sent"] + stores)
    emit(ops, queues, T)
